import numpy as np, ml_dtypes
CORES = [242,247,114,119]
N = 4
BF = ml_dtypes.bfloat16
S, U, CH, CP, MS, Q, D, T, SH = 256, 128, 2048, 2048, 4, 8, 3, 3, 5
MX = 16 * MS
def base(rng):
    top = rng.choice(np.array([4, 8, 16, 16]), (N, 8, 1, S)); v = (rng.random((N, 8, 16 + T, S)) * top).astype(np.int64)
    return {"hist": rng.integers(0, 16, (N, 8, 16, CH)), "score": 4 * rng.random((N, 8, 16, CP)) - 2, "weight": (0.0625 + 0.9375 * rng.random((N, 8, 16, 16 * MX))) * (2 * rng.integers(0, 2, (N, 8, 16, 16 * MX)) - 1),
            "past": np.array(v[:, :, :16]), "coming": np.array(v[:, :, 16:]), "kap": rng.integers(0, 65536, (N, 8, 16)), "lam": rng.integers(0, 65536, (N, 8, 16))}
def pack(d):
    out = {k: np.ascontiguousarray(d[k].reshape(N, 128, -1)).astype(np.float32).astype(BF) for k in ("hist", "score", "weight", "past")}
    out["coming"] = np.ascontiguousarray(d["coming"].reshape(N, 8, T * S)).astype(np.float32).astype(BF)
    for k in ("kap", "lam"): out[k] = np.ascontiguousarray(d[k].reshape(N, 128, 1)).astype(np.int32)
    return out
def setup_inputs(rng):
    return pack(base(rng))
def setup_inputs_spread(rng):
    d = base(rng)
    for k, n in (("score", CP), ("weight", 16 * MX)):
        d[k] = d[k] * np.exp2(-rng.integers(0, 3, (N, 8, 1, n)).astype(np.float64))
    for k in ("kap", "lam"): d[k] = np.minimum(np.exp2(4 + 12 * rng.random((N, 8, 16))).astype(np.int64), 65535)
    d["hist"] = np.minimum((np.exp2(4 * rng.random((N, 8, 1, CH))) * rng.random((N, 8, 16, CH))).astype(np.int64), 15)
    return pack(d)
def setup_inputs_ends(rng):
    d = base(rng)
    c = rng.integers(0, 3, (N, 8, 1, CH)); d["hist"] = 15 * np.where(c == 2, rng.integers(0, 2, (N, 8, 16, CH)), c)
    c = rng.integers(0, 6, (N, 8, 1, S)); v = 15 * np.where(c >= 2, rng.integers(0, 2, (N, 8, 16 + T, S)), c)
    d["past"] = np.array(v[:, :, :16]); d["coming"] = np.array(v[:, :, 16:])
    d["kap"] = 65535 * rng.integers(0, 2, (N, 8, 16)); d["lam"] = 65535 * rng.integers(0, 2, (N, 8, 16))
    d["score"] = 4.0 * rng.integers(0, 2, (N, 8, 16, CP)) - 2; d["weight"] = 2.0 * rng.integers(0, 2, (N, 8, 16, 16 * MX)) - 1
    z = N - 1; d["kap"][z, 7] = 65535; d["lam"][z, 7] = 65535
    for u in (0, 1, U - 1, U, U + 1, S - 2, S - 1): d["past"][:, 6:8, :, u] = 15; d["coming"][:, 6:8, :, u] = 15
    d["hist"][z, 7, :, CH - 17:] = 15; d["hist"][z, 7, :, 0] = 0
    cols = (37 * 3600 + 3681 * np.arange(16)) & (CP - 1)
    d["score"][z, 7][:8][:, cols] = 2.0; d["score"][z, 7][8:][:, cols] = -2.0; d["weight"][z, 7, :, 16 * MX - 16:] = 1.0
    return pack(d)
def setup_inputs_corners(rng):
    d = base(rng); h, p, n, ka, la = d["hist"], d["past"], d["coming"], d["kap"], d["lam"]
    ka[:, 0] = 0; la[:, 0] = 0; p[:, 0] = np.maximum(p[:, 0], 1); n[:, 0] = np.maximum(n[:, 0], 1)
    ka[:, 1] = 0; la[:, 1] = 64 * np.arange(16); p[:, 1] |= 1; n[:, 1] |= 1; h[:, 1] = 0; h[:, 1, 0, 1:] = 1
    h[:, 2] = 0; n[:, 2] = 15
    h[:, 3] = 15; p[:, 3] = 15; n[:, 3] = 15; ka[:, 3] = 65535; la[:, 3] = 65535
    ka[:, 4, 1:] = 0; la[:, 4] = 0
    ka[:, 5, :15] = 0; la[:, 5] = 0
    p[:, 6] = 0; n[:, 6] = 0
    few = np.array([0, 1, 15, 16, 65535]); ka[:, 7] = rng.choice(few, (N, 16)); la[:, 7] = rng.choice(few, (N, 16)); p[:, 7] = rng.choice(np.array([0, 1, 14, 15]), (N, 16, S))
    ka[1] = rng.integers(0, 65536, (8, 16)); la[1] = rng.integers(0, 65536, (8, 16))
    return pack(d)
def setup_inputs_crowd(rng):
    d = base(rng); kind = rng.integers(0, 4, S)
    for k in ("past", "coming"):
        a = d[k]; old = np.array(a)
        for g in range(6): a[:, g] = old[:1, g, :, :1]
        for q in range(N):
            for s in range(S // U):
                u = U * s + (0 if q % 2 == 0 else U - 1)
                a[q, 4:6, :, u] = (old[q, 4:6, :, u] + 1 + a[q, 4:6, :, u]) & 15
        a[:, 6] = old[:, 6][:, :, kind]
    d["coming"][:, 6] = np.maximum(d["coming"][:, 6], 1)
    pr = np.array([17, 19, 23, 29, 31, 37, 41, 43, 47, 53, 59, 61, 67, 71, 73, 79]); d["kap"][:, 7] = 0; d["lam"][:, 7] = pr << SH
    low = Q * rng.integers(0, 16 // Q, (N, 16, 16, 15)) + np.eye(16, dtype=np.int64)[None, :, :, None]
    d["hist"][:, 7][:, :, pr[:, None] * np.arange(1, 16)[None, :]] = low
    want = np.stack([np.concatenate([rng.permutation(max(U, MX))[:U] & (MX - 1) for s in range(S // U)]) for q in range(N)])
    m = (want // MS)[:, None, :]; v = (want % MS + MS * rng.integers(0, 16 // MS, (N, S)))[:, None, :]; o = np.arange(16)[None, :, None]
    d["past"][:, 7] = np.where(o > m, v + rng.integers(1, Q, (N, 16, S)), np.where((o == m) | (o == 0), v, rng.integers(0, 16, (N, 16, S)))) & 15
    return pack(d)
def setup_inputs_calm(rng):
    d = base(rng); val = ((np.arange(N)[:, None] + np.arange(8)[None, :]) & 3)[:, :, None, None]
    v = np.where(rng.random((N, 8, 16 + T, S)) < 0.6, val, rng.integers(0, 4, (N, 8, 16 + T, S)))
    v[:, :, 2:16] *= rng.integers(0, 2, (N, 8, 1, S))
    d["past"] = np.array(v[:, :, :16]); d["coming"] = np.array(v[:, :, 16:]); d["hist"] = rng.integers(0, 4, (N, 8, 16, CH))
    return pack(d)
def check_ranges(d):
    bad = []
    for k, lo, hi in (("hist", 0, 15), ("past", 0, 15), ("coming", 0, 15), ("kap", 0, 65535), ("lam", 0, 65535), ("score", -2, 2), ("weight", -1, 1)):
        v = np.asarray(d[k]).astype(np.float64)
        if not (np.min(v) >= lo and np.max(v) <= hi): bad.append("range of " + k)
        elif k == "weight" and np.min(np.abs(v)) < 0.015625: bad.append("least size of " + k)
        elif k not in ("score", "weight") and np.any(v != np.floor(v)): bad.append("whole numbers in " + k)
    return bad
def reference(hist, score, weight, past, coming, kap, lam):
    H = hist.astype(np.float32).astype(np.int64).reshape(N, 8, 16, CH); P = score.astype(np.float64).reshape(N, 8, 16, CP); W = weight.astype(np.float64).reshape(N, 8, 16, 16 * MX)
    X = past.astype(np.float32).astype(np.int64).reshape(N, 8, 16, S); C = coming.astype(np.float32).astype(np.int64).reshape(N, 8, T, S)
    K = kap.astype(np.int64).reshape(N, 8, 16, 1); L = lam.astype(np.int64).reshape(N, 8, 16, 1)
    B = np.zeros((N, 8, 16, S)); kk = np.arange(16).reshape(1, 1, 16, 1)
    for t in range(T):
        home = np.array([(q - D * t) % N for q in range(N)])
        x = X[home]; s = C[home, :, t]; b = B[home]
        sig = np.add.accumulate(K * x, axis=2) + L * np.roll(s, 1, axis=1)[:, :, None, :]
        c = (sig >> SH) & (CH - 1)
        hp = np.take_along_axis(H, c.reshape(N, 8, 1, 16 * S), 3).reshape(N, 8, 16, 16, S)
        z = np.add.reduce(hp * x[:, :, :, None, :], axis=2)
        a = (37 * z + 3681 * kk) & (CP - 1)
        m = np.max(np.where((z & (Q - 1)) == (z[:, :, :1] & (Q - 1)), kk, 0), axis=2)
        e = MS * m + (x[:, :, 0] & (MS - 1))
        p = np.take_along_axis(P, a.reshape(N, 8, 1, 16 * S), 3).reshape(N, 8, 16, 16, S)
        w = np.take_along_axis(W, (16 * e[:, :, None, :] + kk).reshape(N, 8, 1, 16 * S), 3).reshape(N, 8, 16, 16, S)
        logit = np.add.reduce(w * p, axis=3) + np.roll(b, 1, axis=1)
        y = np.reciprocal(1.0 + np.exp(-logit))
        err = (kk == s[:, :, None, :]) - y
        B[home] = 0.5 * b + err
        cm = np.take_along_axis(c, m[:, :, None, :], 2)[:, :, 0]; lo = U * (t % (S // U))
        for q in range(N):
            for g in range(8):
                u = lo + np.unique(e[q, g, lo:lo + U], return_index=True)[1]
                cols = (16 * e[q, g, u][None, :] + np.arange(16)[:, None]).reshape(-1)
                W[q, g][:, cols] += (0.03125 * err[q, g][:, None, u] * p[q, g][:, :, u]).reshape(16, -1)
                if t < T - 1:
                    u = lo + np.unique(cm[q, g, lo:lo + U], return_index=True)[1]
                    col = cm[q, g, u]; old = H[q, g][:, col]
                    H[q, g][:, col] = np.concatenate([s[q, g, u][None, :], old[:15]], axis=0)
        X = np.concatenate([C[:, :, t][:, :, None, :], X[:, :, :15]], axis=2)
    return {"yw": W.reshape(N, 128, 16 * MX).astype(np.float32), "yb": B.reshape(N, 128, S).astype(np.float32)}

def check_inputs(d):
    bad = list(check_ranges(d))
    if not bad:
        for name, y in reference(**d).items():
            for q in range(N):
                v = np.abs(np.asarray(y[q], np.float64)); s = np.sqrt(np.mean(v * v))
                if v.max() > 4 * s or s < 2.0 ** -3: bad.append('%s of rank %d is uneven or too small' % (name, q))
    return bad

@@ -1,0 +1,646 @@
+from concourse.bass import DstId, RemoteDMATransfer
+from concourse.mybir import dt, AluOpType, AxisListType, ActivationFunctionType
+
+AL = AluOpType
+AF = ActivationFunctionType
+F, B, I32, U16 = "float32", "bfloat16", "int32", "uint16"
+NR, STEPS, MOVE = 4, 3, 3
+MAGIC = 12582912.0
+
+SB = {
+    "H": (2176, B), "SC": (2048, B), "W0": (1024, B), "W1": (1024, F), "W2": (1024, F), "W3": (1024, F),
+    "X0": (256, B), "OUTX": (704, B), "IN1": (320, B), "IN2": (320, B), "S0R": (256, B),
+    "R0": (256, B), "R1": (256, B), "R2": (256, B), "CTI": (192, I32), "CTJ": (192, I32),
+    "XR0": (4096, B), "XR1": (4096, B), "XR2": (4096, B),
+    "KL": (2, I32), "KA": (2, I32), "KB": (2, I32), "KC": (2, I32), "KH": (2, F), "KO": (2, F),
+    "KHI": (128, B), "KLO": (128, B), "LM": (256, B), "DL": (256, B), "GT": (8, B),
+    "IO": (256, F), "IOG": (144, F), "IOL": (128, F), "PI": (4, I32), "PJ": (4, I32), "PF": (4, F), "COL": (16, F),
+    "Z": (144, B), "BO": (128, B), "BOF": (128, F), "IW": (240, F), "ID": (128, B), "NI": (128, B), "N2I": (128, B),
+    "BI": (128, B), "NH": (128, F), "TRI": (128, B), "WM": (128, B), "WN": (128, B), "NB": (128, B), "SH": (128, B), "DMF": (128, F),
+    "S0M": (128, F), "MOF": (128, B), "GW": (128, B), "EQQ": (4, F), "RC": (8, F), "OHT": (128, F), "OHS": (128, B), "Q16": (128, B),
+    "VQ": (512, B), "S0S": (128, B), "CR": (256, B), "CL": (1024, B), "DG": (16, F), "D0": (128, F),
+    "D0H": (16, F), "DUM": (128, F), "RM": (512, B), "KM": (1024, B),
+    "CI": (256, I32), "CJ": (256, I32), "CY": (256, F), "CQ": (256, B), "CF0": (256, F), "CF1": (256, F), "CF2": (256, F),
+    "CU0": (256, U16), "CU1": (256, U16), "CU2": (256, U16),
+    "HP": (4096, B), "PP": (3 * 4112, B), "PW": (4096, F), "YA": (256, B), "ZF": (256, F), "DY": (256, F), "DZ": (256, F),
+    "EQ": (256, B), "OH": (256, B), "AU": (256, U16), "WU": (768, U16), "OS0": (256, B), "OS1": (256, B), "OS2": (256, B), "Y": (256, F),
+    "ES": (136, F), "EG": (1024, F), "DW": (1024, F), "FS": (512, F), "SP": (64, B), "UP": (64, U16), "UE": (64, U16),
+    "PC": (128, F), "KS": (128, F), "NBC": (8, F), "AB": (576, F), "EM": (576, B), "OM": (128, F), "OT": (128, F), "HU": (8, U16), "HV": (8, U16),
+    "OLD": (128, B), "NEW": (128, B), "LS": (1024, F),
+    "BN0": (256, F), "BN1": (256, F), "BN2": (256, F), "BI1": (256, F), "BI2": (256, F), "BI3": (256, F),
+}
+BANKS = ["LG0", "LG1", "ZA0", "ZA1", "DM", "CC", "UU", "HD"]
+SCRATCH = {k: ("sbuf", [128, v[0]], v[1]) for k, v in SB.items()}
+for _b in BANKS:
+    SCRATCH[_b] = ("psum", [128, 512], F)
+SEMAPHORES = ["v", "s", "t", "g", "sent"] + ["d%d" % i for i in range(44)] + ["r%d" % i for i in range(12)]
+WIDTH = {k: v[1][1] for k, v in SCRATCH.items()}
+WIDTH.update({"hist": 2048, "score": 2048, "weight": 1024, "past": 256, "coming": 768, "kap": 1, "lam": 1, "yw": 1024, "yb": 256})
+
+CYC = 0.00104
+GATH = 1.56
+PEC = 0.00052
+XSPLIT = [8, 0]
+TAILSCAN = [1]
+EARLY = [1]
+FINE = [(0, 0), (2, 1)]
+ACC = [1]
+WBK = [(("UU", "CC"), ("UU", "CC"), ("HD", "UU"))]
+SEQ = ["p0 l0 n0 h0 f0 p1 L0 l1 w0 N0 n1 h1 f1 p2 L1 l2 w1 N1 n2 f2 L2 N2 w2"]
+PCH = [4]
+HCH = [2]
+
+
+def A(name, c0=0, c1=None, cs=1, p0=0, p1=128, ps=1):
+    return (name, p0, p1, ps, c0, WIDTH[name] if c1 is None else c1, cs)
+
+
+def _bits(a, b, s):
+    if s == 1:
+        return ((1 << (b - a)) - 1) << a
+    m = 0
+    for i in range(a, b, s):
+        m |= 1 << i
+    return m
+
+
+def ncol(a):
+    return (a[5] - a[4] + a[6] - 1) // a[6]
+
+
+def build(T, topo, core):
+    rank = T.rank_of(core)
+    ops = []
+
+    def ap(a):
+        if a[0] in ("kap", "lam"):
+            return T[a[0]][:]
+        if a[3] == 1 and a[6] == 1:
+            return T[a[0]][a[1]:a[2], a[4]:a[5]]
+        return T[a[0]][a[1]:a[2]:a[3], a[4]:a[5]:a[6]]
+
+    def sc(x):
+        return ap(x) if isinstance(x, tuple) else x
+
+    def aps(*xs):
+        return [x for x in xs if isinstance(x, tuple)]
+
+    def add(eng, fn, rd, wr, busy, lat=0.0, kind="c", **kw):
+        o = {"eng": eng, "fn": fn, "rd": rd, "wr": wr, "busy": busy, "lat": lat, "kind": kind, "name": wr[0][0]}
+        o.update(kw)
+        ops.append(o)
+        return o
+
+    def vcost(n, c=1.0):
+        return 0.06 + max(64, n * c) * CYC
+
+    def two(*xs):
+        return all(SCRATCH[x[0]][2] in (B, U16) for x in xs)
+
+    def ts(out, in0, s1, s2, op0, op1=None):
+        def fn(e):
+            if op1 is None:
+                return e.tensor_scalar(ap(out), ap(in0), sc(s1), None, op0)
+            return e.tensor_scalar(ap(out), ap(in0), sc(s1), sc(s2), op0, op1)
+        add("v", fn, aps(in0, s1, s2), [out], vcost(ncol(out), 0.5 if two(out, in0) else 1))
+
+    def tt(out, in0, in1, op):
+        both = in0[0] not in BANKS and in1[0] not in BANKS
+        add("v", lambda e: e.tensor_tensor(ap(out), ap(in0), ap(in1), op), [in0, in1], [out], vcost(ncol(out), 2 if both else 1))
+
+    def vcopy(out, in_):
+        add("v", lambda e: e.tensor_copy(ap(out), ap(in_)), [in_], [out], vcost(ncol(out), 0.5 if two(out, in_) else 1))
+
+    def vset(out, val):
+        add("v", lambda e: e.memset(ap(out), val), [], [out], vcost(ncol(out), 0.5 if two(out) else 1))
+
+    def scan(out, d0, d1, op0, op1):
+        add("v", lambda e: e.tensor_tensor_scan(ap(out), ap(d0), ap(d1), 0.0, op0, op1), [d0, d1], [out], vcost(ncol(out)))
+
+    def vgather(out, win, off, in1):
+        add("v", lambda e: e.tensor_tensor(ap(out), ap(win).indirect(ap(off)), ap(in1), AL.mult), [win, off, in1], [out],
+            vcost(ncol(out), GATH))
+
+    def vscatter(win, off, in_):
+        add("v", lambda e: e.tensor_copy(ap(win).indirect(ap(off)), ap(in_)), [off, in_], [win], vcost(ncol(in_), 3.8))
+
+    def act(out, in_, func=AF.Identity, bias=0.0, scale=1.0, extra=0.0):
+        add("s", lambda e: e.activation(ap(out), ap(in_), func, bias=sc(bias), scale=sc(scale)), aps(in_, bias, scale), [out],
+            vcost(ncol(out)) + extra)
+
+    def sgather(out, win, off):
+        add("s", lambda e: e.activation(ap(out), ap(win).indirect(ap(off)), AF.Copy), [win, off], [out], vcost(ncol(out), GATH))
+
+    def mm(items):
+        def fn(e):
+            r = None
+            for o, l, rh, st, sp in items:
+                r = e.matmul(ap(o), ap(l), ap(rh), st, sp)
+            return r
+        rd, wr, cost = [], [], 0.05
+        for o, l, rh, st, sp in items:
+            rd += [l, rh]
+            wr.append(o)
+            cost += max(64, ncol(rh)) * (4 if SCRATCH[rh[0]][2] == F else 1) * PEC
+        add("t", fn, rd, wr, cost)
+
+    def mms(items, n):
+        for i in range(0, len(items), n):
+            mm(items[i:i + n])
+
+    def group(out, pairs, start=True, stop=True):
+        n = len(pairs)
+        return [(out, l, r, start and i == 0, stop and i == n - 1) for i, (l, r) in enumerate(pairs)]
+
+    def iota(out, pat, base, cm):
+        if SCRATCH[out[0]][2] == I32:
+            add("g", lambda e: e.iota(ap(out), pat, base, cm), [], [out], 0.16 + 2 * ncol(out) * CYC)
+        else:
+            add("g", lambda e: e.iota(ap(out), pat, base, cm, allow_small_or_imprecise_dtypes=True), [], [out],
+                0.16 + 2 * ncol(out) * CYC)
+
+    def asel(out, in_, pat, cmp_, fill, base, cm):
+        add("g", lambda e: e.affine_select(ap(out), ap(in_), pat, cmp_, fill, base, cm), [in_], [out], 0.21 + 2 * ncol(out) * CYC)
+
+    def dma(q, out, in_, kb, accum=False):
+        if accum:
+            fn = lambda e: e.dma_start(ap(out), ap(in_), accum_op=AL.add)
+        else:
+            fn = lambda e: e.dma_start(ap(out), ap(in_))
+        add(q, fn, [in_] + ([out] if accum else []), [out], 1.0 if q == "g" else 0.1, 1.9 + kb / (130.0 if accum else 250.0), "dma")
+
+    nrem = [0]
+
+    def remote(out, in_, to_rank, kb):
+        dst = T.cores[to_rank]
+        rid, pid = topo.addr(dst, core)
+        mask = 0
+        for e_ in topo.engines(core, dst)[:8]:
+            mask |= 1 << e_
+        sem = "r%d" % nrem[0]
+        nrem[0] += 1
+        add("g", lambda e: e.remote_dma(ap(out), ap(in_), T.sem[sem], T.sem["sent"], pid, rid, mask), [in_], [out],
+            0.4, 2.0 + kb / 60.0, "rem", sem=sem, to=to_rank)
+
+    col = lambda i, p1=128: A("COL", i, i + 1, 1, 0, p1)
+    G15, KBI, KAD, M64, OFP, OHB, L0C, SCL, LSQ = range(9)
+    GCOL, LANE, R7, QT = (A("PF", i, i + 1) for i in range(4))
+    CT1, CT0, CT2 = 256, 320, 384
+    X2C = 448
+    ctc = (CT0, CT1, CT2)
+
+    dma("y", A("X0"), A("past"), 64)
+    dma("s", A("KL", 1, 2), A("lam"), 1)
+    dma("y", A("KL", 0, 1), A("kap"), 1)
+    dma("s", A("S0R", p1=8), A("coming", 0, 256, p1=8), 4)
+    dma("y", A("H", 0, 1024), A("hist", 1024, 2048), 400)
+    dma("s", A("H", 1024, 2048), A("hist", 0, 1024), 500)
+    dma("y", A("OUTX", 0, 256, p0=1), A("past", p1=127), 300)
+    dma("s", A("OUTX", X2C, 704, p0=2), A("past", p1=126), 300)
+    for t in range(STEPS):
+        c = ctc[t]
+        dma("y", A("OUTX", c, c + 64, p1=32), A("coming", 256 * t, 256 * t + 256, p1=8), 4)
+        src = A("past", ps=16) if t == 0 else A("coming", 256 * (t - 1), 256 * t, p1=8)
+        dma("s", A("OUTX", c, c + 64, p0=64, p1=96), src, 4)
+    dma("y", A("SC"), A("score"), 900)
+    dma("s", A("W0"), A("weight"), 1000)
+    dma("y", A("OUTX", 0, 256, ps=16), A("coming", 0, 256, p1=8), 4)
+    dma("y", A("OUTX", X2C, 704, ps=16), A("coming", 256, 512, p1=8), 4)
+    dma("y", A("OUTX", X2C, 704, p0=1, ps=16), A("coming", 0, 256, p1=8), 4)
+    last = {}
+    for i, o in enumerate(ops):
+        if o["eng"] in last:
+            o["ord"] = [last[o["eng"]]]
+        last[o["eng"]] = i
+
+    iota(A("PI", 0, 1), [[0, 1]], 0, 1)
+    iota(A("IOG", 0, 128), [[16, 8], [0, 16]], 0, 0)
+    vset(A("IOG", 128, 144), 0.0)
+    iota(A("IO"), [[0, 2], [1, 128]], 0, 0)
+    iota(A("IOL"), [[0, 8], [1, 16]], 0, 0)
+    P_ = A("PI", 0, 1)
+    ts(A("PJ", 0, 1), P_, 112, None, AL.bitwise_and)
+    ts(A("PJ", 1, 2), P_, 15, None, AL.bitwise_and)
+    ts(A("PJ", 2, 3), P_, 7, None, AL.bitwise_and)
+    ts(A("PJ", 3, 4), P_, 3, None, AL.logical_shift_right)
+    vcopy(A("PF"), A("PJ"))
+    iota(col(9), [[0, 1]], 0, 1)
+    ts(A("BO"), A("IOG", 0, 128), GCOL, None, AL.is_equal)
+    asel(A("TRI"), A("BO"), [[1, 128]], AL.is_ge, 0.0, 0, -1)
+    act(col(10), R7, scale=16.0)
+    ts(A("GW", p1=32), A("IOG", 0, 128, p1=32), col(10, 32), None, AL.is_equal)
+    ts(A("GT"), A("IOG", 16, 144, 16), GCOL, None, AL.is_equal)
+    ts(A("IW"), A("IO", 0, 240), col(9), None, AL.is_equal)
+    IF, PCY = A("IW", 0, 128), A("IW", 112, 240)
+    act(col(G15), GCOL, bias=15.0)
+    ts(A("Z"), A("IO", 0, 144), col(G15), 37.0, AL.is_equal, AL.mult)
+    ts(A("KA"), A("KL"), 32768.0, None, AL.add)
+    ts(A("KC"), A("KL"), 255, None, AL.bitwise_and)
+    ts(A("KB"), A("KA"), 65280, None, AL.bitwise_and)
+    vcopy(A("KO"), A("KC"))
+    ts(A("KH"), A("KB"), 32768.0, None, AL.subtract)
+    act(A("DL", 128, 256), IF, scale=A("KO", 1, 2))
+    act(A("DL", 0, 128), IF, scale=A("KH", 1, 2))
+    mm(group(A("UU", 0, 256, p1=8), [(A("GT"), A("DL"))]))
+    act(A("LM", p1=8), A("UU", 0, 256, p1=8))
+    ts(A("KHI"), A("TRI"), A("KH", 0, 1), None, AL.mult)
+    ts(A("KLO"), A("TRI"), A("KO", 0, 1), None, AL.mult)
+
+    def sig(t, x, srow):
+        return [(A("KHI"), x), (A("LM", 0, 128, p1=8), srow), (A("KLO"), x), (A("LM", 128, 256, p1=8), srow)]
+
+    for a, bk in ((0, "CC"), (128, "DM")):
+        mm(group(A(bk, 0, 128), sig(0, A("X0", a, a + 128), A("S0R", a, a + 128, p1=8))))
+        ts(A("CI", a, a + 128), A(bk, 0, 128), 8421376.0, None, AL.add)
+        ts(A("CJ", a, a + 128), A("CI", a, a + 128), 5, 2047, AL.logical_shift_right, AL.bitwise_and)
+        vcopy(A("CU0", a, a + 128), A("CJ", a, a + 128))
+    vcopy(A("CF0", 0, 128), A("CJ", 0, 128))
+    for h in range(2):
+        for k in range(16):
+            o, i = A("XR0", 2048 * h + k, 2048 * h + 2048, 16), A("X0", 128 * h, 128 * h + 128)
+            if k >= XSPLIT[h]:
+                act(o, i, AF.Copy)
+            else:
+                vcopy(o, i)
+    vset(A("H", 2048, 2176), 0.0)
+
+    act(A("OUTX", CT1, X2C, p0=32, p1=64), A("OUTX", CT1, X2C, p1=32), AF.Square)
+    vcopy(A("CTI", p0=64, p1=96), A("OUTX", CT1, X2C, p0=64, p1=96))
+    ts(A("CTJ", p0=64, p1=96), A("CTI", p0=64, p1=96), 3, None, AL.bitwise_and)
+    vcopy(A("OUTX", CT1, X2C, p0=64, p1=96), A("CTJ", p0=64, p1=96))
+    act(A("OUTX", CT1, X2C, p0=96, p1=128), A("OUTX", CT1, X2C, p0=64, p1=96), AF.Square)
+    remote(A("IN1"), A("OUTX", 0, 320), (rank + MOVE) % NR, 220)
+    remote(A("IN2"), A("OUTX", CT2, 704), (rank + 2 * MOVE) % NR, 220)
+    dma("y", A("R0", p1=32), A("OUTX", CT0, CT0 + 64), 16)
+    dma("y", A("R1", p1=32), A("IN1", 256, 320), 16)
+    dma("y", A("R2", p1=32), A("IN2", 0, 64), 16)
+    XT = (A("X0"), A("IN1", 0, 256), A("IN2", 64, 320))
+
+    act(col(KBI), LANE, scale=3681.0 / 2048, bias=129.0 - 1023.5 / 2048)
+    act(col(KAD), LANE, scale=3681.0, bias=2048.0 * 129)
+    act(A("N2I"), IF, scale=-2048.0)
+    act(col(L0C), LANE, AF.Relu, scale=-0.125, bias=0.125)
+    act(A("S0M"), A("BO"), scale=col(L0C))
+    act(A("NH"), IF, scale=0.125)
+    tt(A("DMF"), A("NH"), A("S0M"), AL.subtract)
+    act(A("NH"), IF, scale=-0.5)
+    act(A("NB"), A("BO"), scale=-1.0)
+    asel(A("WN"), A("NB"), [[-1, 128]], AL.is_gt, 0.0, 0, 1)
+    asel(A("WM"), A("WN"), [[-1, 128]], AL.not_equal, 1.0, 0, 1)
+    asel(A("SH"), A("BO"), [[1, 128]], AL.is_equal, 0.0, -1, -1)
+    act(col(M64), LANE, scale=64.0)
+    act(A("MOF"), A("BO"), scale=col(M64))
+    act(A("ID"), IF)
+    act(A("NI"), IF, scale=-1.0)
+    act(A("BI"), IF, scale=4096.0)
+    act(A("BOF"), A("BO"))
+    act(col(OFP), LANE, bias=2048.0)
+    act(col(LSQ), LANE, AF.Square)
+    act(col(OHB), col(LSQ), scale=-1.0, bias=1.0)
+    q32 = A("PF", 3, 4, p1=32)
+    ts(A("EQQ", p1=32), A("IO", 0, 4, p1=32), q32, None, AL.is_equal)
+    eqq = lambda i: A("EQQ", i, i + 1, p1=32)
+    rc = lambda i, j=None: A("RC", i, i + 1 if j is None else j, p1=32)
+    act(rc(0), eqq(0), scale=2.0)
+    act(rc(1), eqq(1), scale=-1.0)
+    act(rc(2), eqq(2), scale=16.0)
+    act(rc(3), eqq(3), scale=-256.0)
+    act(A("EQQ", 0, 1, p1=32), eqq(2), scale=512.0)
+    act(rc(4, 8), A("IO", 0, 4, p1=32), scale=eqq(0), bias=rc(3))
+    G32 = A("GW", 0, 128, p1=32)
+    act(A("OHT", p1=32), A("IOL", p1=32), scale=rc(0), bias=rc(1))
+    tt(A("OHS", p1=32), A("OHT", p1=32), G32, AL.mult)
+    act(A("Q16", p1=32), G32, scale=rc(2))
+    for q in range(4):
+        act(A("VQ", 128 * q, 128 * q + 128, p1=32), G32, scale=rc(4 + q))
+    asel(A("S0S", p1=8), A("GW", 0, 128, p1=8), [[1, 128]], AL.is_equal, 0.0, 0, -16)
+    asel(A("CR", p1=2), A("IO", p1=2), [[0, 256]], AL.not_equal, 1.0, 0, 1)
+    for q in range(4):
+        iota(A("CL", 128 * q, 128 * q + 128, p1=2), [[0, 128]], -128 * (31 + 2 * q * q), 128 * (31 + 2 * q * q) - 1)
+    vset(A("CL", 512, 640, p1=2), 1.0 / 256)
+    vset(A("CL", 512, 640, p1=1), 4096.0)
+    act(A("CL", 640, 768, p1=1), A("IO", 0, 128, p1=1), scale=0.0, bias=0.5)
+    iota(A("CL", 768, 896, p1=1), [[0, 128]], -16, 0)
+    ts(A("DG"), A("IOL", 0, 16), LANE, None, AL.is_equal)
+    ts(A("D0"), A("IOL"), LANE, 2.0, AL.is_gt, AL.mult)
+    act(A("D0H"), A("D0", 0, 16), scale=-0.25, bias=1.0)
+    add("v", lambda e: e.tensor_reduce(ap(col(SCL)), ap(A("D0H")), AxisListType.X, AL.mult), [A("D0H")], [col(SCL)], vcost(16))
+    act(A("DUM"), A("IO", 0, 128), bias=6144.0)
+    iota(A("KM"), [[0, 1024]], 1, 0)
+    iota(A("KM", 0, 1024, 16), [[0, 64]], 0, 0)
+    iota(A("RM"), [[0, 512]], 1, 0)
+    iota(A("RM", 0, 512, 128), [[0, 4]], 0, 0)
+    for t in range(STEPS):
+        iota(A("PP", 4112 * t + 4096, 4112 * t + 4112), [[0, 16]], 0, 0)
+    iota(A("ES", 128, 136), [[0, 8]], 0, 0)
+
+    if ACC[0]:
+        dma("g", A("W1"), A("weight"), 512)
+        ops[-1]["ord"] = [i for i, o in enumerate(ops) if o["kind"] == "rem"]
+
+    def pp(t, h, c0=0, c1=2064):
+        b = 4112 * t + (2048 if h == t % 2 else 0)
+        return A("PP", b + c0, b + c1)
+
+    def prep(t):
+        R = "R%d" % t
+        if t > 0:
+            x = XT[t]
+            for a, n in ((128, 128), (0, 128)) if t == 1 else ((0, 256),):
+                for k in range(16):
+                    asel(A("XR%d" % t, 16 * a + k, 16 * (a + n), 16), A(x[0], x[4] + a, x[4] + a + n), [[0, n]], AL.is_equal, 0.0, 0, 0)
+            cc = A("CC", 0, 256)
+            whole = sig(t, XT[t], A(R, p1=8)) + [(A("CL", 640, 768, p1=1), A("CR", p1=1))]
+            mm(group(cc, whole))
+            act(A("CY"), cc, scale=1.0 / 65536, bias=MAGIC)
+            act(A("CQ"), A("CY"), scale=-65536.0, bias=MAGIC * 65536)
+            mm(group(cc, whole + [(A("ID"), A("CQ")), (A("CL", 768, 896, p1=1), A("CR", p1=1))]))
+            act(A("CF%d" % t), cc, scale=1.0 / 32, bias=MAGIC)
+            ts(A("CU%d" % t), A("CF%d" % t), 1024.0 - MAGIC, None, AL.add)
+        mm(group(A("CC", 256, 512), [(A("OHS", p1=32), A(R, p1=32))]))
+        act(A("OS%d" % t), A("CC", 256, 512), AF.Relu, bias=col(OHB))
+
+    def ints(t, h):
+        u0 = 128 * h
+        m = 64 if (t, h) in FINE else 128
+        for b in range(u0, u0 + 128, m):
+            n = 128 // HCH[0]
+            for a in range(b, b + m, n):
+                vgather(A("HP", 16 * a, 16 * (a + n)), A("H"), A("CU%d" % t, a, a + n), A("XR%d" % t, 16 * a, 16 * (a + n)))
+            za = A("ZA%d" % (h if m == 128 or b > u0 else 1 - h), 0, m)
+            mms(group(za, [(A("Z", 15 - k, 143 - k), A("HP", 16 * b + k, 16 * (b + m), 16)) for k in range(16)]), 1024 // m)
+            act(A("YA", b, b + m), za, scale=1.0 / 2048, bias=col(KBI))
+            act(A("ZF", b, b + m), za)
+            mm(group(za, [(A("N2I"), A("YA", b, b + m)), (IF, A("ZF", b, b + m))]))
+            ts(A("AU", b, b + m), za, col(KAD), None, AL.add)
+            n = 128 // PCH[0]
+            for a in range(b - u0, b - u0 + m, n):
+                sgather(pp(t, h, 16 * a, 16 * (a + n)), A("SC"), A("AU", u0 + a, u0 + a + n))
+        d8, w_, wo = A("DM", 0, 128), A("DM", 128, 256), A("DM", 256, 384)
+        mm(group(d8, [(A("DMF"), A("ZF", u0, u0 + 128))]))
+        act(A("DY", u0, u0 + 128), d8, bias=MAGIC)
+        act(A("DZ", u0, u0 + 128), A("DY", u0, u0 + 128), bias=-MAGIC)
+        tt(A("EQ", u0, u0 + 128), A("DZ", u0, u0 + 128), d8, AL.is_equal)
+        mm(group(w_, [(A("WM"), A("EQ", u0, u0 + 128))]))
+        act(A("OH", u0, u0 + 128), w_, AF.Relu)
+        mm(group(wo, [(A("Q16", p1=32), A("R%d" % t, u0, u0 + 128, p1=32)), (A("MOF"), A("OH", u0, u0 + 128))]))
+        ts(A("WU", 256 * t + u0, 256 * t + u0 + 128), wo, LANE, None, AL.add)
+
+    def hist_update(t, h):
+        u0 = 128 * h
+        p1_, k1, o_, nw = (A("HD", 128 * i, 128 * i + 128) for i in range(4))
+        mm(group(p1_, [(IF, A("CF%d" % t, u0, u0 + 128)), (A("BI"), A("OH", u0, u0 + 128))]))
+        act(A("PC"), p1_, AF.Relu, bias=-4096.0 if t == 0 else 1024.0 - MAGIC - 4096.0)
+        mm(group(k1, [(A("CL", 512, 640, p1=2), A("CR", 0, 128, p1=2)), (A("BOF"), A("PC"))]))
+        scan(A("KS"), A("D0"), k1, AL.mult, AL.max)
+        act(A("NBC"), A("KS", 15, 128, 16), scale=col(SCL), bias=0.25)
+        if EARLY[0]:
+            ts(A("HV"), A("KS", 15, 128, 16), col(SCL), 4096.0, AL.mult, AL.subtract)
+        at, seg = 0, []
+        for b in range(8):
+            n = 128 - 16 * b
+            act(A("AB", at, at + n), A("HD", 128 + 16 * b, 256), AF.Abs, scale=-1.0, bias=A("NBC", b, b + 1))
+            seg.append((at, n))
+            at += n
+        act(A("EM"), A("AB"), AF.Relu, scale=-1048576.0, bias=262144.0)
+        items = [(o_, A("CL", 512, 640, p1=1), A("CR", 0, 128, p1=1), True, False), (o_, A("BOF"), A("PC"), False, False)]
+        for b in range(7, -1, -1):
+            items.append((A("HD", 256 + 16 * b, 384), A("BO"), A("EM", seg[b][0], seg[b][0] + seg[b][1]), False, b == 0))
+        mm(items)
+        tt(A("OM"), A("DUM"), o_, AL.min)
+        scan(A("OT"), A("D0"), A("OM"), AL.mult, AL.max)
+        ts(A("HU"), A("OT", 15, 128, 16), col(SCL), 4096.0, AL.mult, AL.subtract)
+        sgather(A("OLD"), A("H"), A("HV" if EARLY[0] else "HU"))
+        mm(group(nw, [(A("S0S", p1=8), A("R%d" % t, u0, u0 + 128, p1=8)), (A("SH"), A("OLD"))]))
+        act(A("NEW"), nw)
+        vscatter(A("H"), A("HU"), A("NEW"))
+
+    def firsts(t, h):
+        u0 = 128 * h
+        items = []
+        for q in range(4):
+            items += group(A("UU", 128 * q, 128 * q + 128),
+                           [(A("CL", 128 * q, 128 * q + 128, p1=2), A("CR", 0, 128, p1=2)),
+                            (A("VQ", 128 * q, 128 * q + 128, p1=32), A("R%d" % t, u0, u0 + 128, p1=32)),
+                            (A("BI"), A("OH", u0, u0 + 128))])
+        mms(items, 6)
+        scan(A("FS"), A("RM"), A("UU"), AL.mult, AL.max)
+        for q in range(4):
+            act(A("SP", q, 64, 4), A("DG"), scale=A("FS", 128 * q + 127, 128 * q + 128))
+        mm(group(A("UU", 0, 64), [(A("BO"), A("SP"))]))
+        ts(A("UE"), A("UU", 0, 64), -1.0, 128.0, AL.mult, AL.add)
+        ts(A("UP"), A("UU", 0, 64), -16.0, col(OFP), AL.mult, AL.add)
+
+    first_sig = [1.5]
+
+    def carry(t, lg, a, n, learner):
+        o = a % 128
+        y, oh = A("Y", a, a + n), A("OS%d" % t, a, a + n)
+        act(y, A(lg, o, o + n), AF.Sigmoid, extra=first_sig[0])
+        first_sig[0] = 0.0
+        pb = A(lg, 256 + o, 256 + o + n)
+        old = [(A("NH"), A("BI%d" % t, a, a + n))] if t > 0 else []
+        if learner:
+            pe = A(lg, 128 + o, 128 + o + n)
+            mm(group(pe, [(A("NI"), oh), (IF, y)]))
+            act(A("ES", o, o + n), pe, scale=-1.0 / 32)
+        mm(group(pb, old + [(A("NI"), oh), (IF, y)]))
+        act(A("BN%d" % t, a, a + n), pb, scale=-1.0)
+        to = (rank + MOVE) % NR if t < STEPS - 1 else (rank - MOVE * t) % NR
+        remote(A("BI%d" % (t + 1), a, a + n), A("BN%d" % t, a, a + n), to, n / 2)
+        if t == STEPS - 1:
+            dma("y", A("yb", a, a + n), A("BI3", a, a + n), n / 2)
+
+    def mix(t, h, learner):
+        u0 = 128 * h
+        lg = "LG%d" % h
+        tail = t == STEPS - 1 and not learner
+        for q in range(2):
+            a = u0 + 64 * q
+            vgather(A("PW", 16 * a, 16 * a + 1024), A("W%d" % t), A("WU", 256 * t + a, 256 * t + a + 64),
+                    pp(t, h, 1024 * q, 1024 * q + 1024))
+            if tail and q == 1 and TAILSCAN[0]:
+                scan(A("LS"), A("KM"), A("PW", 16 * a, 16 * a + 1024), AL.mult, AL.add)
+                pairs = [(IF, A("LS", 15, 1024, 16))]
+            else:
+                pairs = [(IF, A("PW", 16 * a + k, 16 * a + 1024, 16)) for k in range(16)]
+            if t > 0:
+                pairs.append((PCY, A("BI%d" % t, a, a + 64)))
+            mms(group(A("CC" if tail and q == 1 else lg, 64 * q, 64 * q + 64), pairs), 4)
+            if tail:
+                carry(t, "CC" if q == 1 else lg, a, 64, False)
+        if not tail:
+            carry(t, lg, u0, 128, learner)
+
+    def learn(t, h):
+        for j in range(2):
+            c0, c1 = 512 * j, 512 * j + 512
+            sgather(A("EG", c0, c1), A("ES"), A("UE", 32 * j, 32 * j + 32))
+            vgather(A("DW", c0, c1), pp(t, h), A("UP", 32 * j, 32 * j + 32), A("EG", c0, c1))
+            if t < STEPS - 1 and ACC[0]:
+                dma("g", A("W%d" % (t + 1), c0, c1), A("DW", c0, c1), 256, True)
+                if t == 0:
+                    dma("y", A("W2", c0, c1), A("W1", c0, c1), 256)
+                continue
+            bk = A(WBK[0][t][j])
+            act(bk, A("W%d" % t, c0, c1))
+            tt(A("W%d" % (t + 1), c0, c1), A("DW", c0, c1), bk, AL.add)
+            if t == STEPS - 1:
+                dma("s", A("yw", c0, c1), A("W3", c0, c1), 256)
+
+    for w in SEQ[0].split():
+        t = int(w[1])
+        hl = t % 2
+        {"p": lambda: prep(t), "l": lambda: ints(t, hl), "n": lambda: ints(t, 1 - hl), "h": lambda: hist_update(t, hl),
+         "f": lambda: firsts(t, hl), "L": lambda: mix(t, hl, True), "N": lambda: mix(t, 1 - hl, False), "w": lambda: learn(t, hl)}[w[0]]()
+    return ops
+
+
+HOP = 0.12
+ROUNDS = [7000]
+WIN = [6.0, 0.1, 0.15]
+PLAN = {}
+
+
+def order(ops):
+    acc, bank = {}, {}
+    for i, o in enumerate(ops):
+        deps, soft = set(), set()
+        for lst, w in ((o["rd"], False), (o["wr"], True)):
+            for a in lst:
+                if a[0] in BANKS:
+                    for e_, j in bank.setdefault(a[0], {}).items():
+                        if j != i:
+                            both_read = not w and all(x[0] != a[0] for x in ops[j]["wr"])
+                            (soft if e_ == o["eng"] and (e_ == "t" or both_read) else deps).add(j)
+                    continue
+                pm, cm = _bits(a[1], a[2], a[3]), _bits(a[4], a[5], a[6])
+                for j, w2, pm2, cm2 in acc.setdefault(a[0], []):
+                    if j != i and (w or w2) and pm & pm2 and cm & cm2:
+                        deps.add(j)
+        for lst, w in ((o["rd"], False), (o["wr"], True)):
+            for a in lst:
+                if a[0] in BANKS:
+                    bank[a[0]][o["eng"]] = i
+                else:
+                    acc[a[0]].append((i, w, _bits(a[1], a[2], a[3]), _bits(a[4], a[5], a[6])))
+        o["deps"], o["soft"] = deps, soft - deps
+    n = len(ops)
+    succ = [[] for _ in range(n)]
+    for i, o in enumerate(ops):
+        for j in o["deps"] | o["soft"]:
+            succ[j].append(i)
+    busy = [o["busy"] for o in ops]
+    lat = [o["lat"] for o in ops]
+    eng = [o["eng"] for o in ops]
+    pre = [[(j, lat[j] + (HOP if j in o["deps"] else 0.0)) for j in o["deps"] | o["soft"]] for o in ops]
+    post = [[(j, lat[i] + (HOP if i in ops[j]["deps"] else 0.0)) for j in succ[i]] for i in range(n)]
+    for i, o in enumerate(ops):
+        for j in o.get("ord", []):
+            pre[i].append((j, 0.0))
+            post[j].append((i, 0.0))
+
+    def place(lst, before, rel):
+        end = [0.0] * n
+        st = {e: [] for e in "vstgy"}
+        en = {e: [] for e in "vstgy"}
+        for i in lst:
+            t = rel[i]
+            for j, d in before[i]:
+                if end[j] + d > t:
+                    t = end[j] + d
+            s_, e_, b = st[eng[i]], en[eng[i]], busy[i]
+            k = len(s_)
+            while k > 0 and e_[k - 1] > t:
+                k -= 1
+            while k < len(s_) and s_[k] < t + b:
+                t = max(t, e_[k])
+                k += 1
+            s_.insert(k, t)
+            e_.insert(k, t + b)
+            end[i] = t + b
+        return end
+
+    zero = [0.0] * n
+    big = [i for i in range(n) if eng[i] == "v" and busy[i] > 0.8]
+
+    def span(end):
+        return max(end[i] + lat[i] for i in range(n)) + WIN[2] * sum(end[i] for i in big) / len(big)
+
+    def polish(lst):
+        end = place(lst, pre, zero)
+        best = (span(end), end)
+        for _ in range(3):
+            back = place(sorted(range(n), key=lambda i: (-end[i], -i)), post, lat)
+            end = place(sorted(range(n), key=lambda i: (-back[i], i)), pre, zero)
+            if span(end) > best[0] - 0.01:
+                break
+            best = (span(end), end)
+        return best
+
+    if "end" not in PLAN:
+        best = polish(list(range(n)))
+        seed = 12345
+        cur = best
+        for it in range(ROUNDS[0]):
+            key = [cur[1][i] - busy[i] for i in range(n)]
+            seed = (seed * 1103515245 + 12345) % 2147483648
+            mid, amp = (seed >> 8) % 1000 / 1000.0 * cur[0], (0.5, 1.0, 2.0, 4.0)[it % 4]
+            for i in range(n):
+                if abs(key[i] - mid) < WIN[0]:
+                    seed = (seed * 1103515245 + 12345) % 2147483648
+                    key[i] += ((seed >> 8) % 1000 / 1000.0) * amp
+                for j, d in pre[i]:
+                    if key[j] >= key[i]:
+                        key[i] = key[j] + 1e-6
+            cand = polish(sorted(range(n), key=lambda i: (key[i], i)))
+            if cand[0] <= cur[0] + WIN[1] * (1.0 - it / ROUNDS[0]):
+                cur = cand
+            if cand[0] <= best[0]:
+                best = cand
+        PLAN["end"] = best[1]
+    end = PLAN["end"]
+    for i, o in enumerate(ops):
+        o["t0"], o["t1"] = end[i] - busy[i], end[i] + lat[i]
+    return sorted(range(n), key=lambda i: (ops[i]["t0"], i))
+
+
+def rank_program(g, core, T, topo):
+    if T.rank_of(core) is None:
+        return
+    ops = build(T, topo, core)
+    seq = order(ops)
+    queue = {"v": g.vector, "s": g.scalar, "t": g.tensor, "g": g, "y": g.sync}
+    count = {e: 0 for e in "vstg"}
+    known = {e: {} for e in "vstgy"}
+    final, ndma = {}, 0
+    for i in seq:
+        o = ops[i]
+        e = o["eng"]
+        kn = known[e]
+        for j in sorted(o["deps"], key=lambda j: -ops[j]["t1"]):
+            s, v = ops[j]["sig"]
+            if kn.get(s, 0) < v:
+                queue[e].wait_ge(T.sem[s], v)
+                kn[s] = v
+                if ops[j]["kind"] != "rem":
+                    for s2, v2 in ops[j]["known"].items():
+                        if kn.get(s2, 0) < v2:
+                            kn[s2] = v2
+        o["known"] = dict(kn)
+        ins = o["fn"](queue[e])
+        if o["kind"] == "c":
+            count[e] += 1
+            ins.then_inc(T.sem[e], 1)
+            o["sig"] = (e, count[e])
+        elif o["kind"] == "dma":
+            o["sig"] = ("d%d" % ndma, 16)
+            ndma += 1
+            ins.then_inc(T.sem[o["sig"][0]], 16)
+        else:
+            o["sig"] = (o["sem"], 8)
+            final["sent"] = final.get("sent", 0) + 8
+        final[o["sig"][0]] = o["sig"][1]
+    for s, v in final.items():
+        if all(known[e].get(s, 0) < v for e in known):
+            g.sync.wait_ge(T.sem[s], v)

@@ -3,33 +3,34 @@ from concourse.mybir import dt, AluOpType, AxisListType, ActivationFunctionType
 
 AL = AluOpType
 AF = ActivationFunctionType
-F, B, I32, U16 = "float32", "bfloat16", "int32", "uint16"
+F, B, I32, U16, F16 = "float32", "bfloat16", "int32", "uint16", "float16"
 NR, STEPS, MOVE = 4, 3, 3
 MAGIC = 12582912.0
 
 SB = {
-    "H": (2176, B), "SC": (2048, B), "W0": (1024, B), "W1": (1024, F), "W2": (1024, F), "W3": (1024, F),
-    "X0": (256, B), "OUTX": (704, B), "IN1": (320, B), "IN2": (320, B), "S0R": (256, B),
+    "H0": (2048, B), "H1": (2176, B), "H2": (2176, B), "ZT": (1024, B), "SC": (2048, B),
+    "W0": (1024, B), "W1": (1024, F), "W2": (1024, F), "W3": (1024, F),
+    "X0": (256, B), "OUTX": (704, B), "IN1": (576, B), "IN2": (320, B), "S0R": (768, B),
     "R0": (256, B), "R1": (256, B), "R2": (256, B), "CTI": (192, I32), "CTJ": (192, I32),
-    "XR0": (4096, B), "XR1": (4096, B), "XR2": (4096, B),
-    "KL": (2, I32), "KA": (2, I32), "KB": (2, I32), "KC": (2, I32), "KH": (2, F), "KO": (2, F),
-    "KHI": (128, B), "KLO": (128, B), "LM": (256, B), "DL": (256, B), "GT": (8, B),
-    "IO": (256, F), "IOG": (144, F), "IOL": (128, F), "PI": (4, I32), "PJ": (4, I32), "PF": (4, F), "COL": (16, F),
-    "Z": (144, B), "BO": (128, B), "BOF": (128, F), "IW": (240, F), "ID": (128, B), "NI": (128, B), "N2I": (128, B),
-    "BI": (128, B), "NH": (128, F), "TRI": (128, B), "WM": (128, B), "WN": (128, B), "NB": (128, B), "SH": (128, B), "DMF": (128, F),
-    "S0M": (128, F), "MOF": (128, B), "GW": (128, B), "EQQ": (4, F), "RC": (8, F), "OHT": (128, F), "OHS": (128, B), "Q16": (128, B),
-    "VQ": (512, B), "S0S": (128, B), "CR": (256, B), "CL": (1024, B), "DG": (16, F), "D0": (128, F),
-    "D0H": (16, F), "DUM": (128, F), "RM": (512, B), "KM": (1024, B),
-    "CI": (256, I32), "CJ": (256, I32), "CY": (256, F), "CQ": (256, B), "CF0": (256, F), "CF1": (256, F), "CF2": (256, F),
-    "CU0": (256, U16), "CU1": (256, U16), "CU2": (256, U16),
-    "HP": (4096, B), "PP": (3 * 4112, B), "PW": (4096, F), "YA": (256, B), "ZF": (256, F), "DY": (256, F), "DZ": (256, F),
-    "EQ": (256, B), "OH": (256, B), "AU": (256, U16), "WU": (768, U16), "OS0": (256, B), "OS1": (256, B), "OS2": (256, B), "Y": (256, F),
-    "ES": (136, F), "EG": (1024, F), "DW": (1024, F), "FS": (512, F), "SP": (64, B), "UP": (64, U16), "UE": (64, U16),
-    "PC": (128, F), "KS": (128, F), "NBC": (8, F), "AB": (576, F), "EM": (576, B), "OM": (128, F), "OT": (128, F), "HU": (8, U16), "HV": (8, U16),
+    "XB": (3 * 2048, B), "XR": (3 * 4096, B),
+    "KL": (2, I32), "KA": (2, F), "KB": (2, F), "KH": (2, F), "KO": (2, F),
+    "KHI": (128, B), "KLO": (128, B), "LM": (256, B), "DL": (256, B), "GT": (32, B),
+    "IO": (256, B), "IOG": (128, B), "IOL": (128, B), "IOM": (512, B), "IOT": (32, F), "PJ": (12, I32), "PF": (12, F), "COL": (24, F),
+    "Z": (144, B), "BO": (128, B), "BOX": (128, B), "BO4": (128, B), "IW": (240, F), "IB": (240, B), "NI": (128, B), "BI": (128, B),
+    "BOC": (8, F), "I37": (128, B),
+    "HI": (128, F), "TRI": (128, B), "WM": (128, B), "WN": (128, B), "NB": (128, B), "SH": (128, B), "DM": (128, B), "S0M": (128, B),
+    "MOF": (128, B), "GW": (128, B), "RC": (16, F), "Q16": (128, B), "SBM": (128, B), "VQ": (512, B), "S0S": (128, B),
+    "DG": (64, B), "D0": (128, B), "MD": (128, B), "DUI": (128, F), "RM": (512, B), "KM": (1024, B), "SEL": (480, B),
+    "MASK": (512, B), "BR": (512, B), "NB16": (128, B), "JR": (64, B),
+    "CQ": (256, B), "CI": (256, I32), "CF": (256, F16), "CU": (768, U16),
+    "HP": (3 * 4096, B), "PP": (3 * 4112, B), "PW": (4096, F), "D16": (1024, F16), "YA": (256, B), "ZH": (256, F16), "RR": (256, F16),
+    "EQ": (256, B), "OH": (768, B), "AU": (768, U16), "WU": (768, U16), "OS": (768, B), "Y": (256, F),
+    "ES": (136, F), "E4": (256, F), "DW": (1024, F), "FS": (512, F), "SP": (256, B), "UP": (192, U16), "UE": (48, U16),
+    "PC": (128, F16), "KS": (128, F), "EM": (576, B), "OM": (128, F), "OT": (128, F), "HU": (8, U16), "HV": (8, U16),
     "OLD": (128, B), "NEW": (128, B), "LS": (1024, F),
-    "BN0": (256, F), "BN1": (256, F), "BN2": (256, F), "BI1": (256, F), "BI2": (256, F), "BI3": (256, F),
+    "BN0": (264, F), "BN1": (256, F), "BN2": (256, F), "BI1": (256, F), "BI2": (256, F), "BI3": (256, F),
 }
-BANKS = ["LG0", "LG1", "ZA0", "ZA1", "DM", "CC", "UU", "HD"]
+BANKS = ["LGL", "LGN", "ZL", "ZN", "DD", "CC", "UU", "HD"]
 SCRATCH = {k: ("sbuf", [128, v[0]], v[1]) for k, v in SB.items()}
 for _b in BANKS:
     SCRATCH[_b] = ("psum", [128, 512], F)
@@ -37,18 +38,13 @@ SEMAPHORES = ["v", "s", "t", "g", "sent"] + ["d%d" % i for i in range(44)] + ["r
 WIDTH = {k: v[1][1] for k, v in SCRATCH.items()}
 WIDTH.update({"hist": 2048, "score": 2048, "weight": 1024, "past": 256, "coming": 768, "kap": 1, "lam": 1, "yw": 1024, "yb": 256})
 
-CYC = 0.00104
-GATH = 1.56
-PEC = 0.00052
-XSPLIT = [8, 0]
-TAILSCAN = [1]
-EARLY = [1]
-FINE = [(0, 0), (2, 1)]
-ACC = [1]
-WBK = [(("UU", "CC"), ("UU", "CC"), ("HD", "UU"))]
-SEQ = ["p0 l0 n0 h0 f0 p1 L0 l1 w0 N0 n1 h1 f1 p2 L1 l2 w1 N1 n2 f2 L2 N2 w2"]
-PCH = [4]
-HCH = [2]
+CASES = [(1.0, 1.56, 3.8, 1.0, 1.0), (1.15, 1.1, 2.5, 1.0, 0.7), (1.35, 2.0, 5.0, 1.3, 0.7)]
+CYC, PEC = 0.00083, 0.000417
+HMODE = {(0, 0): "xeeee", (0, 1): "xeeee", (1, 1): "xeeee", (1, 0): "xeeee", (2, 0): "xeeee", (2, 1): "xeeee"}
+PMODE = {(0, 0): "eeee", (0, 1): "eeee", (1, 1): "eeee", (1, 0): "eeee", (2, 0): "eeee", (2, 1): "eeee"}
+TAIL = [(96, "t"), (32, "v")]
+OPT = {"bits": (), "g1": 16, "gl": 8, "pw": 64, "xbv": (0,), "dd1": "CC", "wadd": "ppp", "wbk": [("CC", None), ("CC", "HD"), ("CC", "HD")]}
+SEQ = ["p0 l0 h0 n0 p1 f0 p2 l1 L0 h1 w0 N0 n1 f1 l2 L1 n2 w1 N1 f2 L2 w2 N2"]
 
 
 def A(name, c0=0, c1=None, cs=1, p0=0, p1=128, ps=1):
@@ -85,17 +81,17 @@ def build(T, topo, core):
     def aps(*xs):
         return [x for x in xs if isinstance(x, tuple)]
 
-    def add(eng, fn, rd, wr, busy, lat=0.0, kind="c", **kw):
-        o = {"eng": eng, "fn": fn, "rd": rd, "wr": wr, "busy": busy, "lat": lat, "kind": kind, "name": wr[0][0]}
+    def add(eng, fn, rd, wr, cost, lat=0.0, kind="c", **kw):
+        o = {"eng": eng, "fn": fn, "rd": rd, "wr": wr, "cost": cost, "lat": lat, "kind": kind, "name": wr[0][0]}
         o.update(kw)
         ops.append(o)
         return o
 
     def vcost(n, c=1.0):
-        return 0.06 + max(64, n * c) * CYC
+        return (0.05 + max(64, n * c) * CYC, 0, 0)
 
     def two(*xs):
-        return all(SCRATCH[x[0]][2] in (B, U16) for x in xs)
+        return all(SCRATCH[x[0]][2] in (B, U16, F16) for x in xs)
 
     def ts(out, in0, s1, s2, op0, op1=None):
         def fn(e):
@@ -119,17 +115,34 @@ def build(T, topo, core):
 
     def vgather(out, win, off, in1):
         add("v", lambda e: e.tensor_tensor(ap(out), ap(win).indirect(ap(off)), ap(in1), AL.mult), [win, off, in1], [out],
-            vcost(ncol(out), GATH))
+            (0.05, ncol(out), 0))
 
     def vscatter(win, off, in_):
-        add("v", lambda e: e.tensor_copy(ap(win).indirect(ap(off)), ap(in_)), [off, in_], [win], vcost(ncol(in_), 3.8))
+        add("v", lambda e: e.tensor_copy(ap(win).indirect(ap(off)), ap(in_)), [off, in_], [win], (0.05, 0, ncol(in_)))
 
     def act(out, in_, func=AF.Identity, bias=0.0, scale=1.0, extra=0.0):
+        c = vcost(ncol(out))
         add("s", lambda e: e.activation(ap(out), ap(in_), func, bias=sc(bias), scale=sc(scale)), aps(in_, bias, scale), [out],
-            vcost(ncol(out)) + extra)
+            (c[0] + extra, 0, 0))
 
-    def sgather(out, win, off):
-        add("s", lambda e: e.activation(ap(out), ap(win).indirect(ap(off)), AF.Copy), [win, off], [out], vcost(ncol(out), GATH))
+    def either(q):
+        v, s = ops.pop(), ops.pop()
+        o = v if q == "v" else s
+        if q == "e":
+            o["alt"] = {"s": (s["fn"], s["cost"]), "v": (v["fn"], v["cost"])}
+        ops.append(o)
+
+    def lin(q, out, in_, scale=1.0, bias=0.0):
+        act(out, in_, AF.Identity, bias, scale)
+        ts(out, in_, scale, bias, AL.mult, AL.add)
+        either(q)
+
+    def gather(q, out, win, off, scale=1.0, bias=0.0):
+        add("s", lambda e: e.activation(ap(out), ap(win).indirect(ap(off)), AF.Identity, bias=bias, scale=scale), [win, off], [out],
+            (0.065, ncol(out), 0))
+        add("v", lambda e: e.tensor_scalar(ap(out), ap(win).indirect(ap(off)), scale, bias, AL.mult, AL.add), [win, off], [out],
+            (0.05, ncol(out), 0))
+        either(q)
 
     def mm(items):
         def fn(e):
@@ -137,12 +150,12 @@ def build(T, topo, core):
             for o, l, rh, st, sp in items:
                 r = e.matmul(ap(o), ap(l), ap(rh), st, sp)
             return r
-        rd, wr, cost = [], [], 0.05
+        rd, wr, cost = [], [], 0.04
         for o, l, rh, st, sp in items:
             rd += [l, rh]
             wr.append(o)
-            cost += max(64, ncol(rh)) * (4 if SCRATCH[rh[0]][2] == F else 1) * PEC
-        add("t", fn, rd, wr, cost)
+            cost += max(min(64, ncol(l)), ncol(rh)) * (4 if SCRATCH[rh[0]][2] == F else 1) * PEC
+        add("t", fn, rd, wr, (cost, 0, 0))
 
     def mms(items, n):
         for i in range(0, len(items), n):
@@ -153,21 +166,23 @@ def build(T, topo, core):
         return [(out, l, r, start and i == 0, stop and i == n - 1) for i, (l, r) in enumerate(pairs)]
 
     def iota(out, pat, base, cm):
+        c = (0.13 + 2 * ncol(out) * CYC, 0, 0)
         if SCRATCH[out[0]][2] == I32:
-            add("g", lambda e: e.iota(ap(out), pat, base, cm), [], [out], 0.16 + 2 * ncol(out) * CYC)
+            add("g", lambda e: e.iota(ap(out), pat, base, cm), [], [out], c)
         else:
-            add("g", lambda e: e.iota(ap(out), pat, base, cm, allow_small_or_imprecise_dtypes=True), [], [out],
-                0.16 + 2 * ncol(out) * CYC)
+            add("g", lambda e: e.iota(ap(out), pat, base, cm, allow_small_or_imprecise_dtypes=True), [], [out], c)
 
     def asel(out, in_, pat, cmp_, fill, base, cm):
-        add("g", lambda e: e.affine_select(ap(out), ap(in_), pat, cmp_, fill, base, cm), [in_], [out], 0.21 + 2 * ncol(out) * CYC)
+        add("g", lambda e: e.affine_select(ap(out), ap(in_), pat, cmp_, fill, base, cm), [in_], [out],
+            (0.17 + 2 * ncol(out) * CYC, 0, 0))
 
     def dma(q, out, in_, kb, accum=False):
         if accum:
             fn = lambda e: e.dma_start(ap(out), ap(in_), accum_op=AL.add)
         else:
             fn = lambda e: e.dma_start(ap(out), ap(in_))
-        add(q, fn, [in_] + ([out] if accum else []), [out], 1.0 if q == "g" else 0.1, 1.9 + kb / (130.0 if accum else 250.0), "dma")
+        add(q, fn, [in_] + ([out] if accum else []), [out], (0.9 if q == "g" else 0.09, 0, 0),
+            1.9 + kb / (130.0 if accum else 250.0), "dma")
 
     nrem = [0]
 
@@ -180,161 +195,160 @@ def build(T, topo, core):
         sem = "r%d" % nrem[0]
         nrem[0] += 1
         add("g", lambda e: e.remote_dma(ap(out), ap(in_), T.sem[sem], T.sem["sent"], pid, rid, mask), [in_], [out],
-            0.4, 2.0 + kb / 60.0, "rem", sem=sem, to=to_rank)
+            (0.4, 0, 0), 2.0 + kb / 60.0, "rem", sem=sem, to=to_rank)
 
     col = lambda i, p1=128: A("COL", i, i + 1, 1, 0, p1)
-    G15, KBI, KAD, M64, OFP, OHB, L0C, SCL, LSQ = range(9)
-    GCOL, LANE, R7, QT = (A("PF", i, i + 1) for i in range(4))
+    G15, KBI, KAD, KBZ, M64, OFP, L0C, G8, L112, LMB = range(10)
+    GCOL, LANE, R7, U4, L4, GBEF, LOW, HIGH, PCOL = (A("PF", i, i + 1) for i in range(9))
     CT1, CT0, CT2 = 256, 320, 384
     X2C = 448
     ctc = (CT0, CT1, CT2)
 
-    dma("y", A("X0"), A("past"), 64)
-    dma("s", A("KL", 1, 2), A("lam"), 1)
+    vset(A("S0R", 0, 512), 1.0)
+    first = len(ops)
     dma("y", A("KL", 0, 1), A("kap"), 1)
-    dma("s", A("S0R", p1=8), A("coming", 0, 256, p1=8), 4)
-    dma("y", A("H", 0, 1024), A("hist", 1024, 2048), 400)
-    dma("s", A("H", 1024, 2048), A("hist", 0, 1024), 500)
-    dma("y", A("OUTX", 0, 256, p0=1), A("past", p1=127), 300)
-    dma("s", A("OUTX", X2C, 704, p0=2), A("past", p1=126), 300)
+    dma("s", A("KL", 1, 2), A("lam"), 1)
+    dma("y", A("X0"), A("past"), 64)
+    dma("s", A("S0R", 0, 512, p1=8), A("coming", 0, 512, p1=8), 4)
+    dma("y", A("H0", 0, 1024), A("hist", 1024, 2048), 400)
+    dma("s", A("H0", 1024, 2048), A("hist", 0, 1024), 500)
     for t in range(STEPS):
         c = ctc[t]
         dma("y", A("OUTX", c, c + 64, p1=32), A("coming", 256 * t, 256 * t + 256, p1=8), 4)
         src = A("past", ps=16) if t == 0 else A("coming", 256 * (t - 1), 256 * t, p1=8)
-        dma("s", A("OUTX", c, c + 64, p0=64, p1=96), src, 4)
+        dma("y", A("OUTX", c, c + 64, p0=64, p1=96), src, 4)
     dma("y", A("SC"), A("score"), 900)
-    dma("s", A("W0"), A("weight"), 1000)
-    dma("y", A("OUTX", 0, 256, ps=16), A("coming", 0, 256, p1=8), 4)
-    dma("y", A("OUTX", X2C, 704, ps=16), A("coming", 256, 512, p1=8), 4)
-    dma("y", A("OUTX", X2C, 704, p0=1, ps=16), A("coming", 0, 256, p1=8), 4)
+    dma("y", A("W0"), A("weight"), 1000)
+    dma("y", A("H1", 0, 1024), A("hist", 1024, 2048), 900)
+    dma("y", A("H1", 1024, 2048), A("hist", 0, 1024), 900)
     last = {}
-    for i, o in enumerate(ops):
+    for i in range(first, len(ops)):
+        o = ops[i]
         if o["eng"] in last:
             o["ord"] = [last[o["eng"]]]
         last[o["eng"]] = i
 
-    iota(A("PI", 0, 1), [[0, 1]], 0, 1)
-    iota(A("IOG", 0, 128), [[16, 8], [0, 16]], 0, 0)
-    vset(A("IOG", 128, 144), 0.0)
+    iota(A("PJ", 8, 12), [[64, 2], [112, 2]], 0, 1)
+    iota(A("IOG"), [[16, 8], [0, 16]], 0, 0)
     iota(A("IO"), [[0, 2], [1, 128]], 0, 0)
+    iota(A("IOT"), [[16, 32]], 0, 0)
     iota(A("IOL"), [[0, 8], [1, 16]], 0, 0)
-    P_ = A("PI", 0, 1)
+    P_ = A("PJ", 8, 9)
     ts(A("PJ", 0, 1), P_, 112, None, AL.bitwise_and)
     ts(A("PJ", 1, 2), P_, 15, None, AL.bitwise_and)
     ts(A("PJ", 2, 3), P_, 7, None, AL.bitwise_and)
-    ts(A("PJ", 3, 4), P_, 3, None, AL.logical_shift_right)
-    vcopy(A("PF"), A("PJ"))
-    iota(col(9), [[0, 1]], 0, 1)
-    ts(A("BO"), A("IOG", 0, 128), GCOL, None, AL.is_equal)
+    ts(A("PJ", 3, 4), P_, 4, 3, AL.logical_shift_right, AL.bitwise_and)
+    ts(A("PJ", 4, 5), P_, 3, None, AL.bitwise_and)
+    ts(A("PJ", 5, 6), A("PJ", 9, 10), 112, None, AL.bitwise_and)
+    ts(A("PJ", 6, 8), A("PJ", 8, 12, 2), 79, None, AL.bitwise_and)
+    vcopy(A("PF", 0, 9), A("PJ", 0, 9))
+    ts(A("BO"), A("IOG"), GCOL, None, AL.is_equal)
+    ts(A("BOC"), A("IOT", 0, 8), GCOL, None, AL.is_equal)
     asel(A("TRI"), A("BO"), [[1, 128]], AL.is_ge, 0.0, 0, -1)
-    act(col(10), R7, scale=16.0)
-    ts(A("GW", p1=32), A("IOG", 0, 128, p1=32), col(10, 32), None, AL.is_equal)
-    ts(A("GT"), A("IOG", 16, 144, 16), GCOL, None, AL.is_equal)
-    ts(A("IW"), A("IO", 0, 240), col(9), None, AL.is_equal)
-    IF, PCY = A("IW", 0, 128), A("IW", 112, 240)
-    act(col(G15), GCOL, bias=15.0)
-    ts(A("Z"), A("IO", 0, 144), col(G15), 37.0, AL.is_equal, AL.mult)
-    ts(A("KA"), A("KL"), 32768.0, None, AL.add)
-    ts(A("KC"), A("KL"), 255, None, AL.bitwise_and)
-    ts(A("KB"), A("KA"), 65280, None, AL.bitwise_and)
-    vcopy(A("KO"), A("KC"))
-    ts(A("KH"), A("KB"), 32768.0, None, AL.subtract)
-    act(A("DL", 128, 256), IF, scale=A("KO", 1, 2))
-    act(A("DL", 0, 128), IF, scale=A("KH", 1, 2))
-    mm(group(A("UU", 0, 256, p1=8), [(A("GT"), A("DL"))]))
-    act(A("LM", p1=8), A("UU", 0, 256, p1=8))
-    ts(A("KHI"), A("TRI"), A("KH", 0, 1), None, AL.mult)
-    ts(A("KLO"), A("TRI"), A("KO", 0, 1), None, AL.mult)
+    ts(A("IB"), A("IO", 0, 240), PCOL, None, AL.is_equal)
+    lin("e", A("IW"), A("IB"))
+    IF, PCY, ID = A("IW", 0, 128), A("IW", 112, 240), A("IB", 0, 128)
+    lin("e", A("NI"), ID, -1.0)
+    ts(A("GT"), A("IOT"), GBEF, None, AL.is_equal)
+    ts(col(LMB, 32), A("PF", 8, 9, p1=32), 9.0, 0.25, AL.is_equal, AL.mult)
+    ts(A("KA"), A("KL"), 1.5 * 2.0 ** 39, 1.5 * 2.0 ** 39, AL.add, AL.subtract)
+    ts(A("KB"), A("KL"), 1.5 * 2.0 ** 31, 1.5 * 2.0 ** 31, AL.add, AL.subtract)
+    tt(A("KH"), A("KB"), A("KA"), AL.subtract)
+    tt(A("KO"), A("KL"), A("KB"), AL.subtract)
+    lin("e", A("DL", 0, 128), ID, A("KH", 1, 2))
+    lin("e", A("DL", 128, 256), ID, A("KO", 1, 2))
+    mm(group(A("UU", 0, 256, p1=32), [(A("GT"), A("DL"))]))
+    lin("e", A("LM", p1=32), A("UU", 0, 256, p1=32), 1.0, col(LMB, 32))
+    lin("e", A("KHI"), A("TRI"), A("KH", 0, 1))
+    lin("e", A("KLO"), A("TRI"), A("KO", 0, 1))
+    iota(A("H1", 2048, 2176), [[0, 128]], 0, 0)
+    vset(A("ZT"), 0.0)
+    for t, h in ((0, 1), (1, 1), (1, 0), (2, 0), (2, 1)):
+        if HMODE[t, h][0] == "x" and (t > 0 or h not in OPT["xbv"]):
+            dma("y", A("XB", 2048 * t + 1024 * h, 2048 * t + 1024 * h + 1024), A("ZT"), 256)
 
-    def sig(t, x, srow):
-        return [(A("KHI"), x), (A("LM", 0, 128, p1=8), srow), (A("KLO"), x), (A("LM", 128, 256, p1=8), srow)]
-
-    for a, bk in ((0, "CC"), (128, "DM")):
-        mm(group(A(bk, 0, 128), sig(0, A("X0", a, a + 128), A("S0R", a, a + 128, p1=8))))
-        ts(A("CI", a, a + 128), A(bk, 0, 128), 8421376.0, None, AL.add)
-        ts(A("CJ", a, a + 128), A("CI", a, a + 128), 5, 2047, AL.logical_shift_right, AL.bitwise_and)
-        vcopy(A("CU0", a, a + 128), A("CJ", a, a + 128))
-    vcopy(A("CF0", 0, 128), A("CJ", 0, 128))
-    for h in range(2):
-        for k in range(16):
-            o, i = A("XR0", 2048 * h + k, 2048 * h + 2048, 16), A("X0", 128 * h, 128 * h + 128)
-            if k >= XSPLIT[h]:
-                act(o, i, AF.Copy)
-            else:
-                vcopy(o, i)
-    vset(A("H", 2048, 2176), 0.0)
-
-    act(A("OUTX", CT1, X2C, p0=32, p1=64), A("OUTX", CT1, X2C, p1=32), AF.Square)
+    iota(A("OUTX", CT1, X2C, p0=32, p1=64), [[0, 3], [1, 64]], 0, 64)
+    asel(A("OUTX", CT1, X2C, p0=32, p1=64), A("OUTX", CT1, X2C, p0=32, p1=64), [[0, 192]], AL.is_gt, 1.0, 4, -1)
     vcopy(A("CTI", p0=64, p1=96), A("OUTX", CT1, X2C, p0=64, p1=96))
     ts(A("CTJ", p0=64, p1=96), A("CTI", p0=64, p1=96), 3, None, AL.bitwise_and)
     vcopy(A("OUTX", CT1, X2C, p0=64, p1=96), A("CTJ", p0=64, p1=96))
     act(A("OUTX", CT1, X2C, p0=96, p1=128), A("OUTX", CT1, X2C, p0=64, p1=96), AF.Square)
-    remote(A("IN1"), A("OUTX", 0, 320), (rank + MOVE) % NR, 220)
-    remote(A("IN2"), A("OUTX", CT2, 704), (rank + 2 * MOVE) % NR, 220)
+    asel(A("SH"), A("BO"), [[1, 128]], AL.is_equal, 0.0, -1, -1)
+    lin("e", col(G8, 32), A("PF", 2, 3, p1=32), 16.0)
+    ts(A("S0S", p1=8), A("IO", 0, 128, p1=8), col(G8, 8), None, AL.is_equal)
+    mm(group(A("LGL", 0, 256), [(A("SH"), A("X0")), (A("S0S", p1=8), A("S0R", 0, 256, p1=8))]))
+    lin("e", A("S0R", 512, 768), A("LGL", 0, 256))
+    mm(group(A("LGN", 0, 256), [(A("SH"), A("S0R", 512, 768)), (A("S0S", p1=8), A("S0R", 256, 512, p1=8))]))
+    lin("e", A("OUTX", X2C, 704), A("LGN", 0, 256))
+    remote(A("IN1", 0, 512), A("S0R", 256, 768), (rank + MOVE) % NR, 220)
+    remote(A("IN1", 512, 576), A("OUTX", CT1, CT1 + 64), (rank + MOVE) % NR, 40)
+    remote(A("IN2"), A("OUTX", CT2, 704), (rank + 2 * MOVE) % NR, 120)
     dma("y", A("R0", p1=32), A("OUTX", CT0, CT0 + 64), 16)
-    dma("y", A("R1", p1=32), A("IN1", 256, 320), 16)
+    dma("y", A("R1", p1=32), A("IN1", 512, 576), 16)
     dma("y", A("R2", p1=32), A("IN2", 0, 64), 16)
-    XT = (A("X0"), A("IN1", 0, 256), A("IN2", 64, 320))
+    XT = (A("X0"), A("IN1", 256, 512), A("IN2", 64, 320))
 
-    act(col(KBI), LANE, scale=3681.0 / 2048, bias=129.0 - 1023.5 / 2048)
-    act(col(KAD), LANE, scale=3681.0, bias=2048.0 * 129)
-    act(A("N2I"), IF, scale=-2048.0)
-    act(col(L0C), LANE, AF.Relu, scale=-0.125, bias=0.125)
-    act(A("S0M"), A("BO"), scale=col(L0C))
-    act(A("NH"), IF, scale=0.125)
-    tt(A("DMF"), A("NH"), A("S0M"), AL.subtract)
-    act(A("NH"), IF, scale=-0.5)
-    act(A("NB"), A("BO"), scale=-1.0)
+    def xs(t, a, b):
+        return A(XT[t][0], XT[t][4] + a, XT[t][4] + b)
+
+    if any(v[0] == "f" for v in HMODE.values()):
+        lin("s", col(G15), GCOL, 1.0, 15.0)
+        ts(A("Z"), A("IO", 0, 144), col(G15), None, AL.is_equal)
+    for j, c in enumerate((LOW, HIGH)):
+        ts(A("SEL", 240 * j, 240 * j + 240), A("IO", 0, 240), c, 112.0, AL.subtract, AL.is_equal)
+    iota(A("IOM"), [[0, 16], [1, 4], [0, 8]], 0, 0)
+    ts(A("MASK"), A("IOM"), U4, None, AL.is_equal)
+    lin("e", A("BOX"), A("BO"), 8.0)
+    lin("e", A("BO4"), A("BO"), 4096.0)
+    lin("e", A("I37"), ID, 37.0)
+    lin("e", col(KBI), LANE, 3681.0, 2048.0 * 129 - 1023.5)
+    lin("e", col(KAD), LANE, 3681.0, 2048.0 * 129 + 37 * 1800.0)
+    act(col(L0C), LANE, AF.Relu, scale=-1.0, bias=1.0)
+    lin("e", A("S0M"), A("BO"), col(L0C))
+    tt(A("DM"), ID, A("S0M"), AL.subtract)
+    lin("e", A("HI"), IF, 0.5)
+    lin("e", col(KBZ), LANE, 3681.0, 2048.0 * 129 - 1023.5 + 37 * 1800.0)
+    lin("e", A("NB"), A("BO"), -1.0)
     asel(A("WN"), A("NB"), [[-1, 128]], AL.is_gt, 0.0, 0, 1)
     asel(A("WM"), A("WN"), [[-1, 128]], AL.not_equal, 1.0, 0, 1)
-    asel(A("SH"), A("BO"), [[1, 128]], AL.is_equal, 0.0, -1, -1)
-    act(col(M64), LANE, scale=64.0)
-    act(A("MOF"), A("BO"), scale=col(M64))
-    act(A("ID"), IF)
-    act(A("NI"), IF, scale=-1.0)
-    act(A("BI"), IF, scale=4096.0)
-    act(A("BOF"), A("BO"))
-    act(col(OFP), LANE, bias=2048.0)
-    act(col(LSQ), LANE, AF.Square)
-    act(col(OHB), col(LSQ), scale=-1.0, bias=1.0)
-    q32 = A("PF", 3, 4, p1=32)
-    ts(A("EQQ", p1=32), A("IO", 0, 4, p1=32), q32, None, AL.is_equal)
-    eqq = lambda i: A("EQQ", i, i + 1, p1=32)
+    lin("e", col(M64), LANE, 1.0 / 64)
+    lin("e", A("MOF"), A("BO"), col(M64))
+    lin("e", A("BI"), ID, 33.0 / 32)
+    lin("e", col(OFP), L4, 4.0, 2048.0)
+    for r in range(4):
+        asel(A("BR", 128 * r, 128 * r + 128), A("BO"), [[0, 8], [1, 4], [0, 4]], AL.is_equal, 0.0, -r, 0)
+    iota(A("JR"), [[1, 4], [0, 16]], 0, 0)
+    ts(A("GW", p1=32), A("IOG", 0, 128, p1=32), col(G8, 32), None, AL.is_equal)
     rc = lambda i, j=None: A("RC", i, i + 1 if j is None else j, p1=32)
-    act(rc(0), eqq(0), scale=2.0)
-    act(rc(1), eqq(1), scale=-1.0)
-    act(rc(2), eqq(2), scale=16.0)
-    act(rc(3), eqq(3), scale=-256.0)
-    act(A("EQQ", 0, 1, p1=32), eqq(2), scale=512.0)
-    act(rc(4, 8), A("IO", 0, 4, p1=32), scale=eqq(0), bias=rc(3))
+    iota(rc(0, 2), [[15, 2]], 1, 0)
+    asel(rc(0), rc(0), [[0, 1]], AL.is_gt, 0.0, 8, -1)
+    asel(rc(1), rc(1), [[0, 1]], AL.is_gt, 0.0, 24, -1)
+    iota(rc(2, 8), [[512, 6]], -1024, 0)
+    asel(rc(4, 8), rc(4, 8), [[0, 4]], AL.is_gt, -256.0, 24, -1)
+    asel(rc(1, 8), rc(1, 8), [[0, 7]], AL.is_ge, 0.0, -16, 1)
+    for q in range(4):
+        iota(rc(8 + q), [[0, 1]], -128 * (31 + 2 * q * q), 0)
+    asel(rc(8, 12), rc(8, 12), [[0, 4]], AL.is_equal, 0.0, -9, 1)
+    asel(rc(8, 12), rc(8, 12), [[0, 4]], AL.not_equal, -1.0, -8, 1)
     G32 = A("GW", 0, 128, p1=32)
-    act(A("OHT", p1=32), A("IOL", p1=32), scale=rc(0), bias=rc(1))
-    tt(A("OHS", p1=32), A("OHT", p1=32), G32, AL.mult)
-    act(A("Q16", p1=32), G32, scale=rc(2))
+    lin("e", A("SBM", p1=32), G32, rc(0))
+    lin("e", A("Q16", p1=32), G32, rc(1))
     for q in range(4):
-        act(A("VQ", 128 * q, 128 * q + 128, p1=32), G32, scale=rc(4 + q))
-    asel(A("S0S", p1=8), A("GW", 0, 128, p1=8), [[1, 128]], AL.is_equal, 0.0, 0, -16)
-    asel(A("CR", p1=2), A("IO", p1=2), [[0, 256]], AL.not_equal, 1.0, 0, 1)
-    for q in range(4):
-        iota(A("CL", 128 * q, 128 * q + 128, p1=2), [[0, 128]], -128 * (31 + 2 * q * q), 128 * (31 + 2 * q * q) - 1)
-    vset(A("CL", 512, 640, p1=2), 1.0 / 256)
-    vset(A("CL", 512, 640, p1=1), 4096.0)
-    act(A("CL", 640, 768, p1=1), A("IO", 0, 128, p1=1), scale=0.0, bias=0.5)
-    iota(A("CL", 768, 896, p1=1), [[0, 128]], -16, 0)
-    ts(A("DG"), A("IOL", 0, 16), LANE, None, AL.is_equal)
-    ts(A("D0"), A("IOL"), LANE, 2.0, AL.is_gt, AL.mult)
-    act(A("D0H"), A("D0", 0, 16), scale=-0.25, bias=1.0)
-    add("v", lambda e: e.tensor_reduce(ap(col(SCL)), ap(A("D0H")), AxisListType.X, AL.mult), [A("D0H")], [col(SCL)], vcost(16))
-    act(A("DUM"), A("IO", 0, 128), bias=6144.0)
-    iota(A("KM"), [[0, 1024]], 1, 0)
-    iota(A("KM", 0, 1024, 16), [[0, 64]], 0, 0)
+        lin("e", A("VQ", 128 * q, 128 * q + 128, p1=32), G32, rc(4 + q), rc(8 + q))
+    ts(A("DG"), A("IOL", 0, 64), LANE, -16.0, AL.is_equal, AL.mult)
+    ts(A("D0"), A("IOL"), LANE, None, AL.is_gt)
+    ts(A("MD"), A("IOL"), LANE, -2.0 ** 20, AL.not_equal, AL.mult)
+    iota(A("DUI"), [[1, 128]], 6145, 0)
+    nk = max([16 * n for n, q in TAIL if q == "v"] + [16])
+    iota(A("KM", 0, nk), [[0, nk]], 1, 0)
+    iota(A("KM", 0, nk, 16), [[0, nk // 16]], 0, 0)
     iota(A("RM"), [[0, 512]], 1, 0)
     iota(A("RM", 0, 512, 128), [[0, 4]], 0, 0)
     for t in range(STEPS):
         iota(A("PP", 4112 * t + 4096, 4112 * t + 4112), [[0, 16]], 0, 0)
     iota(A("ES", 128, 136), [[0, 8]], 0, 0)
-
-    if ACC[0]:
+    iota(A("BN0", 128, 136), [[0, 8]], 0, 0)
+    if OPT["wadd"][0] == "d":
         dma("g", A("W1"), A("weight"), 512)
         ops[-1]["ord"] = [i for i, o in enumerate(ops) if o["kind"] == "rem"]
 
@@ -342,151 +356,234 @@ def build(T, topo, core):
         b = 4112 * t + (2048 if h == t % 2 else 0)
         return A("PP", b + c0, b + c1)
 
+    def role(t, h):
+        return "L" if h == t % 2 else "N"
+
+    def st(nm, t, a, b, m=1):
+        return A(nm, m * (256 * t + a), m * (256 * t + b))
+
     def prep(t):
-        R = "R%d" % t
-        if t > 0:
-            x = XT[t]
-            for a, n in ((128, 128), (0, 128)) if t == 1 else ((0, 256),):
-                for k in range(16):
-                    asel(A("XR%d" % t, 16 * a + k, 16 * (a + n), 16), A(x[0], x[4] + a, x[4] + a + n), [[0, n]], AL.is_equal, 0.0, 0, 0)
-            cc = A("CC", 0, 256)
-            whole = sig(t, XT[t], A(R, p1=8)) + [(A("CL", 640, 768, p1=1), A("CR", p1=1))]
+        R = ("S0R", "IN1", "R2")[t]
+        for a, n in ((0, 128), (128, 128)) if t == 0 else ((0, 256),):
+            cc = A("CC" if a == 0 else "HD", 0, n)
+            x, srow = xs(t, a, a + n), A(R, a, a + n, p1=32)
+            whole = [(A("KHI"), x), (A("KLO"), x), (A("LM", 0, 128, p1=32), srow), (A("LM", 128, 256, p1=32), srow)]
             mm(group(cc, whole))
-            act(A("CY"), cc, scale=1.0 / 65536, bias=MAGIC)
-            act(A("CQ"), A("CY"), scale=-65536.0, bias=MAGIC * 65536)
-            mm(group(cc, whole + [(A("ID"), A("CQ")), (A("CL", 768, 896, p1=1), A("CR", p1=1))]))
-            act(A("CF%d" % t), cc, scale=1.0 / 32, bias=MAGIC)
-            ts(A("CU%d" % t), A("CF%d" % t), 1024.0 - MAGIC, None, AL.add)
-        mm(group(A("CC", 256, 512), [(A("OHS", p1=32), A(R, p1=32))]))
-        act(A("OS%d" % t), A("CC", 256, 512), AF.Relu, bias=col(OHB))
+            if t in OPT["bits"]:
+                ts(A("CI", a, a + n), cc, 8421375.5, None, AL.add)
+                ts(A("CI", a, a + n), A("CI", a, a + n), 5, 2047, AL.logical_shift_right, AL.bitwise_and)
+                vcopy(st("CU", t, a, a + n), A("CI", a, a + n))
+                continue
+            ts(A("CQ", a, a + n), cc, 1.5 * 2.0 ** 39, 1.5 * 2.0 ** 39, AL.add, AL.subtract)
+            mm(group(cc, whole + [(A("NI"), A("CQ", a, a + n))]))
+            ts(st("CU", t, a, a + n), cc, 1.0 / 32, 1023.5, AL.mult, AL.add)
+        for h in (t % 2, 1 - t % 2):
+            x = xs(t, 128 * h, 128 * h + 128)
+            c0 = 256 * t + 128 * h
+            if HMODE[t, h][0] == "f":
+                for k in range(16):
+                    asel(A("XR", 16 * c0 + k, 16 * c0 + 2048, 16), x, [[0, 128]], AL.is_equal, 0.0, 0, 0)
+            elif t == 0 and h in OPT["xbv"]:
+                for gq in range(8):
+                    lin("e", A("XB", 8 * c0 + gq, 8 * c0 + 1024, 8), x, A("BOC", gq, gq + 1))
+            else:
+                for gq in range(8):
+                    p0 = 32 * (gq // 2)
+                    o = A("XB", 8 * c0 + gq, 8 * c0 + 1024, 8, p0, p0 + 32)
+                    i = A(x[0], x[4], x[5], 1, p0, p0 + 32)
+                    if gq % 2 == 0:
+                        asel(o, i, [[0, 128]], AL.is_gt, 0.0, 16, -1)
+                    else:
+                        asel(o, i, [[0, 128]], AL.is_ge, 0.0, -16, 1)
+        mm(group(A("CC", 256, 512), [(A("SBM", p1=32), A(R, 0, 256, p1=32))]))
+        ts(st("OS", t, 0, 256), A("CC", 256, 512), LANE, None, AL.is_equal)
 
     def ints(t, h):
         u0 = 128 * h
-        m = 64 if (t, h) in FINE else 128
-        for b in range(u0, u0 + 128, m):
-            n = 128 // HCH[0]
-            for a in range(b, b + m, n):
-                vgather(A("HP", 16 * a, 16 * (a + n)), A("H"), A("CU%d" % t, a, a + n), A("XR%d" % t, 16 * a, 16 * (a + n)))
-            za = A("ZA%d" % (h if m == 128 or b > u0 else 1 - h), 0, m)
-            mms(group(za, [(A("Z", 15 - k, 143 - k), A("HP", 16 * b + k, 16 * (b + m), 16)) for k in range(16)]), 1024 // m)
-            act(A("YA", b, b + m), za, scale=1.0 / 2048, bias=col(KBI))
-            act(A("ZF", b, b + m), za)
-            mm(group(za, [(A("N2I"), A("YA", b, b + m)), (IF, A("ZF", b, b + m))]))
-            ts(A("AU", b, b + m), za, col(KAD), None, AL.add)
-            n = 128 // PCH[0]
-            for a in range(b - u0, b - u0 + m, n):
-                sgather(pp(t, h, 16 * a, 16 * (a + n)), A("SC"), A("AU", u0 + a, u0 + a + n))
-        d8, w_, wo = A("DM", 0, 128), A("DM", 128, 256), A("DM", 256, 384)
-        mm(group(d8, [(A("DMF"), A("ZF", u0, u0 + 128))]))
-        act(A("DY", u0, u0 + 128), d8, bias=MAGIC)
-        act(A("DZ", u0, u0 + 128), A("DY", u0, u0 + 128), bias=-MAGIC)
-        tt(A("EQ", u0, u0 + 128), A("DZ", u0, u0 + 128), d8, AL.is_equal)
-        mm(group(w_, [(A("WM"), A("EQ", u0, u0 + 128))]))
-        act(A("OH", u0, u0 + 128), w_, AF.Relu)
-        mm(group(wo, [(A("Q16", p1=32), A("R%d" % t, u0, u0 + 128, p1=32)), (A("MOF"), A("OH", u0, u0 + 128))]))
-        ts(A("WU", 256 * t + u0, 256 * t + u0 + 128), wo, LANE, None, AL.add)
+        zb = "Z" + role(t, h)
+        za, aa, dd, d2, w_, wo = (A(zb, 128 * (i % 4), 128 * (i % 4) + 128) for i in range(6))
+        mode, qs = HMODE[t, h][0], HMODE[t, h][1:]
+        n = 128 // len(qs)
+        table = A("H%d" % t, 0, 2048)
+        for i, q in enumerate(qs):
+            a = u0 + n * i
+            if mode == "f":
+                vgather(st("HP", t, a, a + n, 16), table, st("CU", t, a, a + n), st("XR", t, a, a + n, 16))
+            else:
+                gather(q, st("HP", t, a, a + n, 16), table, st("CU", t, a, a + n), 1.0, -8.0)
+        if mode == "f":
+            c0 = 16 * (256 * t + u0)
+            mms(group(za, [(A("Z", 15 - k, 143 - k), A("HP", c0 + k, c0 + 2048, 16)) for k in range(16)]), 8)
+        else:
+            db = OPT["dd1"] if (t, h) == (0, 1) else "DD"
+            items = []
+            for j in range(2):
+                for b in range(16):
+                    s0 = u0 + 64 * j + 4 * b
+                    items.append((A(db, 32 * b, 32 * b + 32, 1, 64 * j, 64 * j + 64), st("HP", t, s0, s0 + 4, 16),
+                                  st("XB", t, s0, s0 + 4, 8), True, True))
+            mms(items, 32 // len(qs))
+            tt(A("D16", 512 * h, 512 * h + 512), A(db), A("MASK"), AL.mult)
+            items = [(za, A("BOX"), xs(t, u0, u0 + 128), True, False)]
+            for j in range(2):
+                for gq in range(8):
+                    items.append((A(zb, 64 * j, 64 * j + 64), A("SEL", 240 * j + 112 - 16 * gq, 240 * j + 240 - 16 * gq),
+                                  A("D16", 512 * h + gq, 512 * h + 512, 8), False, j == 1 and gq == 7))
+            mm(items)
+        hs = lambda nm: A(nm, u0, u0 + 128)
+        oh = st("OH", t, u0, u0 + 128)
+        ts(hs("ZH"), za, 1800.0, None, AL.subtract)
+        if h == t % 2 and t < STEPS - 1:
+            aa = A("UU", 0, 128)
+            mm(group(dd, [(A("DM"), hs("ZH"))]))
+            ts(hs("YA"), hs("ZH"), 37.0, col(KBZ), AL.mult, AL.add)
+            mm(group(aa, [(A("I37"), hs("ZH")), (A("NI"), hs("YA"))]))
+        else:
+            lin("e", hs("YA"), za, 37.0, col(KBI))
+            mm(group(aa, [(A("I37"), hs("ZH")), (A("NI"), hs("YA"))]) + group(dd, [(A("DM"), hs("ZH"))]))
+        ts(st("AU", t, u0, u0 + 128), aa, col(KAD), None, AL.add)
+        ts(hs("RR"), dd, 12284.5, None, AL.add)
+        qs = PMODE[t, h]
+        n = 128 // len(qs)
+        for i, q in enumerate(qs):
+            gather(q, pp(t, h, 16 * n * i, 16 * n * (i + 1)), A("SC"), st("AU", t, u0 + n * i, u0 + n * (i + 1)))
+        mm(group(d2, [(A("DM"), hs("ZH")), (A("NI"), hs("RR"))]))
+        act(hs("EQ"), d2, AF.Relu, scale=-4096.0, bias=-4096.0 * 12287)
+        ts(hs("EQ"), d2, -12288.0, 4096.0, AL.is_equal, AL.mult)
+        either("e")
+        mm(group(w_, [(A("WM"), hs("EQ"))]))
+        act(oh, w_, AF.Relu)
+        ts(oh, w_, 0.0, None, AL.max)
+        either("e")
+        mm(group(wo, [(A("Q16", p1=32), A("R%d" % t, u0, u0 + 128, p1=32)), (A("MOF"), oh)]))
+        ts(st("WU", t, u0, u0 + 128), wo, LANE, None, AL.add)
 
     def hist_update(t, h):
         u0 = 128 * h
-        p1_, k1, o_, nw = (A("HD", 128 * i, 128 * i + 128) for i in range(4))
-        mm(group(p1_, [(IF, A("CF%d" % t, u0, u0 + 128)), (A("BI"), A("OH", u0, u0 + 128))]))
-        act(A("PC"), p1_, AF.Relu, bias=-4096.0 if t == 0 else 1024.0 - MAGIC - 4096.0)
-        mm(group(k1, [(A("CL", 512, 640, p1=2), A("CR", 0, 128, p1=2)), (A("BOF"), A("PC"))]))
-        scan(A("KS"), A("D0"), k1, AL.mult, AL.max)
-        act(A("NBC"), A("KS", 15, 128, 16), scale=col(SCL), bias=0.25)
-        if EARLY[0]:
-            ts(A("HV"), A("KS", 15, 128, 16), col(SCL), 4096.0, AL.mult, AL.subtract)
-        at, seg = 0, []
-        for b in range(8):
-            n = 128 - 16 * b
-            act(A("AB", at, at + n), A("HD", 128 + 16 * b, 256), AF.Abs, scale=-1.0, bias=A("NBC", b, b + 1))
-            seg.append((at, n))
+        k1, k2, p_, nw = (A("HD", 128 * i, 128 * i + 128) for i in range(4))
+        o_ = A("UU", 128, 256)
+        cf = A("CF", u0, u0 + 128)
+        ts(cf, st("CU", t, u0, u0 + 128), 1.0, None, AL.add)
+        mm(group(p_, [(ID, cf), (A("WM"), A("EQ", u0, u0 + 128))]))
+        ts(A("PC"), p_, 4096.0, 0.0, AL.subtract, AL.max)
+        mm(group(k2, [(ID, A("MD")), (A("BO"), A("PC"))]) + group(k1, [(A("BO"), A("PC"))]))
+        mm([(o_, ID, A("MD"), True, False), (o_, A("BO"), A("PC"), False, False)])
+        scan(A("KS"), A("D0"), k2, AL.mult, AL.max)
+        ts(A("HV"), A("KS", 15, 128, 16), 1.0, None, AL.subtract)
+        gather("e", A("OLD"), A("H%d" % t, 0, 2048), A("HV"))
+        tt(A("EM", 0, 128), A("KS"), k1, AL.is_equal)
+        items = [(o_, A("BO4"), A("EM", 0, 128), False, False)]
+        at = 128
+        for b in range(7):
+            n = 112 - 16 * b
+            ts(A("EM", at, at + n), A("HD", 128 - n, 128), A("KS", 16 * b + 15, 16 * b + 16), None, AL.is_equal)
+            items.append((A("UU", 256 - n, 256), A("BO4"), A("EM", at, at + n), False, b == 6))
             at += n
-        act(A("EM"), A("AB"), AF.Relu, scale=-1048576.0, bias=262144.0)
-        items = [(o_, A("CL", 512, 640, p1=1), A("CR", 0, 128, p1=1), True, False), (o_, A("BOF"), A("PC"), False, False)]
-        for b in range(7, -1, -1):
-            items.append((A("HD", 256 + 16 * b, 384), A("BO"), A("EM", seg[b][0], seg[b][0] + seg[b][1]), False, b == 0))
-        mm(items)
-        tt(A("OM"), A("DUM"), o_, AL.min)
-        scan(A("OT"), A("D0"), A("OM"), AL.mult, AL.max)
-        ts(A("HU"), A("OT", 15, 128, 16), col(SCL), 4096.0, AL.mult, AL.subtract)
-        sgather(A("OLD"), A("H"), A("HV" if EARLY[0] else "HU"))
+        mm(items[:5])
+        mm(items[5:])
         mm(group(nw, [(A("S0S", p1=8), A("R%d" % t, u0, u0 + 128, p1=8)), (A("SH"), A("OLD"))]))
-        act(A("NEW"), nw)
-        vscatter(A("H"), A("HU"), A("NEW"))
+        lin("e", A("NEW"), nw)
+        tt(A("OM"), A("DUI"), o_, AL.min)
+        scan(A("OT"), A("D0"), A("OM"), AL.mult, AL.max)
+        ts(A("HU"), A("OT", 15, 128, 16), 4097.0, None, AL.subtract)
+        vscatter(A("H%d" % (t + 1)), A("HU"), A("NEW"))
+        if t == 0:
+            dma("y", A("H2"), A("H1"), 544)
 
     def firsts(t, h):
         u0 = 128 * h
         items = []
         for q in range(4):
             items += group(A("UU", 128 * q, 128 * q + 128),
-                           [(A("CL", 128 * q, 128 * q + 128, p1=2), A("CR", 0, 128, p1=2)),
-                            (A("VQ", 128 * q, 128 * q + 128, p1=32), A("R%d" % t, u0, u0 + 128, p1=32)),
-                            (A("BI"), A("OH", u0, u0 + 128))])
-        mms(items, 6)
+                           [(A("VQ", 128 * q, 128 * q + 128, p1=32), A("R%d" % t, u0, u0 + 128, p1=32)),
+                            (A("BI") if h else ID, st("OH", t, u0, u0 + 128))])
+        mm(items)
         scan(A("FS"), A("RM"), A("UU"), AL.mult, AL.max)
         for q in range(4):
-            act(A("SP", q, 64, 4), A("DG"), scale=A("FS", 128 * q + 127, 128 * q + 128))
-        mm(group(A("UU", 0, 64), [(A("BO"), A("SP"))]))
-        ts(A("UE"), A("UU", 0, 64), -1.0, 128.0, AL.mult, AL.add)
-        ts(A("UP"), A("UU", 0, 64), -16.0, col(OFP), AL.mult, AL.add)
+            lin("e", A("SP", 64 * q, 64 * q + 64), A("DG"), A("FS", 128 * q + 127, 128 * q + 128))
+        mm(group(A("UU", 0, 64), [(ID, A("JR"))] + [(A("BR", 128 * q, 128 * q + 128), A("SP", 64 * q, 64 * q + 64)) for q in range(4)]))
+        ts(A("UE", 16 * t, 16 * t + 16), A("UU", 0, 16), 1.0 / 16, 128.0, AL.mult, AL.add)
+        ts(A("UP", 64 * t, 64 * t + 64), A("UU", 0, 64), col(OFP), None, AL.add)
 
-    first_sig = [1.5]
+    first_sig = [1.3]
 
     def carry(t, lg, a, n, learner):
         o = a % 128
-        y, oh = A("Y", a, a + n), A("OS%d" % t, a, a + n)
-        act(y, A(lg, o, o + n), AF.Sigmoid, extra=first_sig[0])
+        oh = st("OS", t, a, a + n)
+        c = a + (8 if t == 0 and a >= 128 else 0)
+        bn = A("BN%d" % t, c, c + n)
+        tail = t == STEPS - 1 and not learner
+        bh = A("ZN", 128 + o, 128 + o + n) if tail else A(lg, 384, 384 + n)
+        if t == 0 or learner:
+            y = A(lg, 256, 256 + n)
+            act(y, A(lg, 0, n), AF.Sigmoid, extra=first_sig[0])
+            if t == 0:
+                tt(bn, oh, y, AL.subtract)
+            else:
+                tt(A("ES", o, o + n), oh, y, AL.subtract)
+                mm(group(bh, [(A("HI"), A("BI%d" % t, a, a + n))]))
+                tt(bn, A("ES", o, o + n), bh, AL.add)
+        else:
+            y = A("Y", a, a + n)
+            mm(group(bh, [(ID, oh), (A("HI"), A("BI%d" % t, a, a + n))]))
+            act(y, A(lg, 0, n), AF.Sigmoid)
+            tt(bn, bh, y, AL.subtract)
         first_sig[0] = 0.0
-        pb = A(lg, 256 + o, 256 + o + n)
-        old = [(A("NH"), A("BI%d" % t, a, a + n))] if t > 0 else []
-        if learner:
-            pe = A(lg, 128 + o, 128 + o + n)
-            mm(group(pe, [(A("NI"), oh), (IF, y)]))
-            act(A("ES", o, o + n), pe, scale=-1.0 / 32)
-        mm(group(pb, old + [(A("NI"), oh), (IF, y)]))
-        act(A("BN%d" % t, a, a + n), pb, scale=-1.0)
         to = (rank + MOVE) % NR if t < STEPS - 1 else (rank - MOVE * t) % NR
-        remote(A("BI%d" % (t + 1), a, a + n), A("BN%d" % t, a, a + n), to, n / 2)
+        remote(A("BI%d" % (t + 1), a, a + n), bn, to, n / 2)
         if t == STEPS - 1:
             dma("y", A("yb", a, a + n), A("BI3", a, a + n), n / 2)
 
     def mix(t, h, learner):
         u0 = 128 * h
-        lg = "LG%d" % h
         tail = t == STEPS - 1 and not learner
-        for q in range(2):
-            a = u0 + 64 * q
-            vgather(A("PW", 16 * a, 16 * a + 1024), A("W%d" % t), A("WU", 256 * t + a, 256 * t + a + 64),
-                    pp(t, h, 1024 * q, 1024 * q + 1024))
-            if tail and q == 1 and TAILSCAN[0]:
-                scan(A("LS"), A("KM"), A("PW", 16 * a, 16 * a + 1024), AL.mult, AL.add)
-                pairs = [(IF, A("LS", 15, 1024, 16))]
+        a = u0
+        for i, (n, q) in enumerate(TAIL if tail else [(64, "t"), (64, "t")]):
+            lg = ("LGN", "DD", "UU", "ZL")[i] if tail else "LG" + role(t, h)
+            lo = 0 if tail else a - u0
+            c0 = 16 * (a - u0)
+            m = min(n, OPT["pw"])
+            for b in range(0, n, m):
+                vgather(A("PW", 16 * (a + b), 16 * (a + b + m)), A("W%d" % t), st("WU", t, a + b, a + b + m),
+                        pp(t, h, c0 + 16 * b, c0 + 16 * (b + m)))
+            roll = [(PCY, A("BI%d" % t, a, a + n))] if tail else []
+            whole = t > 0 and not tail
+            if whole and i == 0:
+                mm([(A(lg, 0, 128), ID, A("ZT", 0, 128), True, False)])
+            if q == "v":
+                scan(A("LS", 0, 16 * n), A("KM", 0, 16 * n), A("PW", 16 * a, 16 * (a + n)), AL.mult, AL.add)
+                mms(group(A(lg, lo, lo + n), roll + [(IF, A("LS", 15, 16 * n, 16))], not whole, not whole), 1)
             else:
-                pairs = [(IF, A("PW", 16 * a + k, 16 * a + 1024, 16)) for k in range(16)]
-            if t > 0:
-                pairs.append((PCY, A("BI%d" % t, a, a + 64)))
-            mms(group(A("CC" if tail and q == 1 else lg, 64 * q, 64 * q + 64), pairs), 4)
+                items = group(A(lg, lo, lo + n), roll + [(IF, A("PW", 16 * a + k, 16 * (a + n), 16)) for k in range(16)],
+                              not whole, not whole)
+                mms(items[:len(roll)], 1)
+                mms(items[len(roll):], OPT["gl"])
             if tail:
-                carry(t, "CC" if q == 1 else lg, a, 64, False)
+                carry(t, lg, a, n, False)
+            a += n
         if not tail:
+            if t > 0:
+                mm([(A(lg, 0, 128), PCY, A("BI%d" % t, u0, u0 + 128), False, True)])
             carry(t, lg, u0, 128, learner)
 
     def learn(t, h):
-        for j in range(2):
-            c0, c1 = 512 * j, 512 * j + 512
-            sgather(A("EG", c0, c1), A("ES"), A("UE", 32 * j, 32 * j + 32))
-            vgather(A("DW", c0, c1), pp(t, h), A("UP", 32 * j, 32 * j + 32), A("EG", c0, c1))
-            if t < STEPS - 1 and ACC[0]:
-                dma("g", A("W%d" % (t + 1), c0, c1), A("DW", c0, c1), 256, True)
-                if t == 0:
-                    dma("y", A("W2", c0, c1), A("W1", c0, c1), 256)
-                continue
-            bk = A(WBK[0][t][j])
-            act(bk, A("W%d" % t, c0, c1))
-            tt(A("W%d" % (t + 1), c0, c1), A("DW", c0, c1), bk, AL.add)
-            if t == STEPS - 1:
-                dma("s", A("yw", c0, c1), A("W3", c0, c1), 256)
+        gather("e", A("E4"), A("BN0" if t == 0 else "ES", 0, 136), A("UE", 16 * t, 16 * t + 16), 1.0 / 32)
+        for j in range(4):
+            vgather(A("DW", j, 1024, 4), pp(t, h), A("UP", 64 * t + 16 * j, 64 * t + 16 * j + 16), A("E4"))
+        how = OPT["wadd"][t]
+        nxt = "W%d" % (t + 1) if t < STEPS - 1 else "yw"
+        if how == "d":
+            dma("g", A(nxt), A("DW"), 512, True)
+        else:
+            for j, bk in enumerate(OPT["wbk"][t]):
+                c0, c1 = 512 * j, 512 * j + 512
+                if bk:
+                    lin("s", A(bk), A("W%d" % t, c0, c1))
+                tt(A("W%d" % (t + 1), c0, c1), A("DW", c0, c1), A(bk) if bk else A("W%d" % t, c0, c1), AL.add)
+                if t == STEPS - 1:
+                    dma("s", A("yw", c0, c1), A("W3", c0, c1), 256)
+        if t < STEPS - 1 and OPT["wadd"][t + 1] == "d":
+            dma("y", A("W2" if t == 0 else "yw"), A(nxt), 512)
 
     for w in SEQ[0].split():
         t = int(w[1])
@@ -496,9 +593,10 @@ def build(T, topo, core):
     return ops
 
 
-HOP = 0.12
-ROUNDS = [7000]
-WIN = [6.0, 0.1, 0.15]
+HOP = 0.11
+ROUNDS = [300, 80000]
+WIN = [4.0, 0.15, 0.5, 0.3, 0.2, 0.0]
+SEED = [12345]
 PLAN = {}
 
 
@@ -506,13 +604,14 @@ def order(ops):
     acc, bank = {}, {}
     for i, o in enumerate(ops):
         deps, soft = set(), set()
+        me = "e%d" % i if "alt" in o else o["eng"]
         for lst, w in ((o["rd"], False), (o["wr"], True)):
             for a in lst:
                 if a[0] in BANKS:
-                    for e_, j in bank.setdefault(a[0], {}).items():
-                        if j != i:
-                            both_read = not w and all(x[0] != a[0] for x in ops[j]["wr"])
-                            (soft if e_ == o["eng"] and (e_ == "t" or both_read) else deps).add(j)
+                    if a[0] in bank and bank[a[0]][1] != i:
+                        e_, j = bank[a[0]]
+                        both_read = all(x[0] != a[0] for x in ops[j]["wr"] + o["wr"])
+                        (soft if e_ == me and (e_ == "t" or both_read) else deps).add(j)
                     continue
                 pm, cm = _bits(a[1], a[2], a[3]), _bits(a[4], a[5], a[6])
                 for j, w2, pm2, cm2 in acc.setdefault(a[0], []):
@@ -521,88 +620,207 @@ def order(ops):
         for lst, w in ((o["rd"], False), (o["wr"], True)):
             for a in lst:
                 if a[0] in BANKS:
-                    bank[a[0]][o["eng"]] = i
+                    bank[a[0]] = (me, i)
                 else:
                     acc[a[0]].append((i, w, _bits(a[1], a[2], a[3]), _bits(a[4], a[5], a[6])))
         o["deps"], o["soft"] = deps, soft - deps
     n = len(ops)
-    succ = [[] for _ in range(n)]
+    above = []
     for i, o in enumerate(ops):
-        for j in o["deps"] | o["soft"]:
-            succ[j].append(i)
-    busy = [o["busy"] for o in ops]
-    lat = [o["lat"] for o in ops]
-    eng = [o["eng"] for o in ops]
-    pre = [[(j, lat[j] + (HOP if j in o["deps"] else 0.0)) for j in o["deps"] | o["soft"]] for o in ops]
-    post = [[(j, lat[i] + (HOP if i in ops[j]["deps"] else 0.0)) for j in succ[i]] for i in range(n)]
+        m = 0
+        for j in o["deps"]:
+            m |= above[j]
+        o["deps"] = set(j for j in o["deps"] if not m >> j & 1)
+        for j in o["deps"]:
+            m |= 1 << j
+        above.append(m)
+    if "t0" not in PLAN:
+        PLAN.update(search(ops))
     for i, o in enumerate(ops):
-        for j in o.get("ord", []):
-            pre[i].append((j, 0.0))
-            post[j].append((i, 0.0))
+        o["eng"], o["t0"], o["t1"], o["busy"] = PLAN["eng"][i], PLAN["t0"][i], PLAN["t1"][i], PLAN["busy"][i]
+        if "alt" in o:
+            o["fn"] = o["alt"][o["eng"]][0]
+    return PLAN["lst"]
 
-    def place(lst, before, rel):
+
+def search(ops):
+    n = len(ops)
+    cases = []
+    for f, ga, sa, dl, wt in CASES:
+        cost = lambda c: f * (c[0] + (c[1] * ga + c[2] * sa) * CYC)
+        busy = [{e: cost(v[1]) for e, v in o["alt"].items()} if "alt" in o else {o["eng"]: cost(o["cost"])} for o in ops]
+        lat = [o["lat"] * dl for o in ops]
+        pre = [[(j, lat[j] + (HOP if j in o["deps"] else 0.0)) for j in o["deps"] | o["soft"]] + [(j, 0.0) for j in o.get("ord", [])]
+               for o in ops]
+        cases.append((busy, lat, pre, wt))
+    busy, lat, pre, _ = cases[0]
+    post = [[] for _ in range(n)]
+    for i in range(n):
+        for j, d in pre[i]:
+            post[j].append((i, d))
+    flex = [i for i in range(n) if "alt" in ops[i]]
+
+    def place(lst, before, rel, eng):
         end = [0.0] * n
         st = {e: [] for e in "vstgy"}
         en = {e: [] for e in "vstgy"}
         for i in lst:
-            t = rel[i]
+            t0 = rel[i]
             for j, d in before[i]:
-                if end[j] + d > t:
-                    t = end[j] + d
-            s_, e_, b = st[eng[i]], en[eng[i]], busy[i]
-            k = len(s_)
-            while k > 0 and e_[k - 1] > t:
-                k -= 1
-            while k < len(s_) and s_[k] < t + b:
-                t = max(t, e_[k])
-                k += 1
-            s_.insert(k, t)
-            e_.insert(k, t + b)
-            end[i] = t + b
+                if end[j] + d > t0:
+                    t0 = end[j] + d
+            pick = None
+            for q in eng[i] or "sv":
+                s_, e_, b, t = st[q], en[q], busy[i][q], t0
+                k = len(s_)
+                while k > 0 and e_[k - 1] > t:
+                    k -= 1
+                while k < len(s_) and s_[k] < t + b:
+                    if e_[k] > t:
+                        t = e_[k]
+                    k += 1
+                if pick is None or t + b < pick[0]:
+                    pick = (t + b, q, k, t)
+            end[i], q, k, t = pick
+            eng[i] = q
+            st[q].insert(k, t)
+            en[q].insert(k, end[i])
         return end
 
-    zero = [0.0] * n
-    big = [i for i in range(n) if eng[i] == "v" and busy[i] > 0.8]
+    def replay(lst, eng, case):
+        b_, l_, p_, _w = case
+        end, free, top = [0.0] * n, {e: 0.0 for e in "vstgy"}, 0.0
+        for i in lst:
+            q = eng[i]
+            t = free[q]
+            for j, d in p_[i]:
+                if end[j] + d > t:
+                    t = end[j] + d
+            end[i] = free[q] = t = t + b_[i][q]
+            if t + l_[i] > top:
+                top = t + l_[i]
+        return top + WIN[5] * sum(end) / n
 
-    def span(end):
-        return max(end[i] + lat[i] for i in range(n)) + WIN[2] * sum(end[i] for i in big) / len(big)
+    zero, wsum = [0.0] * n, sum(c[3] for c in cases)
 
-    def polish(lst):
-        end = place(lst, pre, zero)
-        best = (span(end), end)
-        for _ in range(3):
-            back = place(sorted(range(n), key=lambda i: (-end[i], -i)), post, lat)
-            end = place(sorted(range(n), key=lambda i: (-back[i], i)), pre, zero)
-            if span(end) > best[0] - 0.01:
-                break
-            best = (span(end), end)
-        return best
+    def polish(lst, eng):
+        end = place(lst, pre, zero, eng)
+        back = place(sorted(range(n), key=lambda i: (-end[i], -i)), post, lat, eng)
+        end = place(sorted(range(n), key=lambda i: (-back[i], i)), pre, zero, eng)
+        t0 = [end[i] - busy[i][eng[i]] for i in range(n)]
+        lst = sorted(range(n), key=lambda i: (t0[i], i))
+        times = [max(end[i] + lat[i] for i in range(n))] + [replay(lst, eng, c) for c in cases[1:]]
+        load = sum(busy[i]["v"] for i in flex if eng[i] == "v")
+        return (sum(x * c[3] for x, c in zip(times, cases)) / wsum + WIN[3] * load, t0, times, eng)
 
-    if "end" not in PLAN:
-        best = polish(list(range(n)))
-        seed = 12345
-        cur = best
-        for it in range(ROUNDS[0]):
-            key = [cur[1][i] - busy[i] for i in range(n)]
-            seed = (seed * 1103515245 + 12345) % 2147483648
-            mid, amp = (seed >> 8) % 1000 / 1000.0 * cur[0], (0.5, 1.0, 2.0, 4.0)[it % 4]
+    seed = [SEED[0]]
+
+    def rnd():
+        seed[0] = (seed[0] * 1103515245 + 12345) % 2147483648
+        return (seed[0] >> 8) % 4096 / 4096.0
+
+    best = cur = polish(list(range(n)), [o["eng"] for o in ops])
+    for it in range(ROUNDS[0]):
+        key, eng = list(cur[1]), list(cur[3])
+        mid, amp, move = rnd() * cur[2][0], (0.5, 1.0, 2.0, 4.0)[it % 4], rnd()
+        if move < WIN[2]:
+            for _ in range(1 + it % 2):
+                i = flex[int(rnd() * len(flex))]
+                eng[i] = "s" if eng[i] == "v" else "v"
+        if move > 0.5 * WIN[2]:
             for i in range(n):
                 if abs(key[i] - mid) < WIN[0]:
-                    seed = (seed * 1103515245 + 12345) % 2147483648
-                    key[i] += ((seed >> 8) % 1000 / 1000.0) * amp
+                    key[i] += rnd() * amp
                 for j, d in pre[i]:
                     if key[j] >= key[i]:
                         key[i] = key[j] + 1e-6
-            cand = polish(sorted(range(n), key=lambda i: (key[i], i)))
-            if cand[0] <= cur[0] + WIN[1] * (1.0 - it / ROUNDS[0]):
-                cur = cand
-            if cand[0] <= best[0]:
-                best = cand
-        PLAN["end"] = best[1]
-    end = PLAN["end"]
-    for i, o in enumerate(ops):
-        o["t0"], o["t1"] = end[i] - busy[i], end[i] + lat[i]
-    return sorted(range(n), key=lambda i: (ops[i]["t0"], i))
+        cand = polish(sorted(range(n), key=lambda i: (key[i], i)), eng)
+        if cand[0] <= cur[0] + WIN[1] * (1.0 - it / ROUNDS[0]):
+            cur = cand
+        if cand[0] <= best[0]:
+            best = cand
+    anc = []
+    for i in range(n):
+        m = 0
+        for j, d in pre[i]:
+            m |= anc[j] | 1 << j
+        anc.append(m)
+
+    def path(lst, eng, case):
+        b_, l_, p_, _w = case
+        end, why, free, prev, top, last = [0.0] * n, [None] * n, {e: 0.0 for e in "vstgy"}, {}, 0.0, 0
+        for i in lst:
+            q = eng[i]
+            t, w = free[q], (prev.get(q), True)
+            for j, d in p_[i]:
+                if end[j] + d > t:
+                    t, w = end[j] + d, (j, False)
+            end[i] = free[q] = t = t + b_[i][q]
+            prev[q], why[i] = i, w
+            if t + l_[i] > top:
+                top, last = t + l_[i], i
+        out = []
+        while last is not None:
+            out.append((last, why[last][0], why[last][1]))
+            last = why[last][0]
+        return out, end
+
+    def value(lst, eng, ref=None):
+        times = []
+        for c in cases:
+            times.append(replay(lst, eng, c))
+            if ref and times[-1] > ref[len(times) - 1] + 1.0:
+                return 1e9, times
+        load = sum(busy[i]["v"] for i in flex if eng[i] == "v")
+        return sum(x * c[3] for x, c in zip(times, cases)) / wsum + WIN[3] * load, times
+
+    lst, eng = sorted(range(n), key=lambda i: (best[1][i], i)), list(best[3])
+    now = value(lst, eng)
+    top, crit = (now, lst, eng), None
+    for it in range(ROUNDS[1]):
+        if crit is None or it % 64 == 0:
+            case = cases[int(rnd() * len(cases))]
+            crit, end = path(lst, eng, case)
+            lst = sorted(lst, key=lambda i: end[i] - case[0][i][eng[i]])
+        v, u, queued = crit[int(rnd() * len(crit))]
+        e2, r = eng, rnd()
+        if r < 0.15:
+            v = v if rnd() < 0.5 or u is None else u
+            if "alt" not in ops[v]:
+                continue
+            e2 = list(eng)
+            e2[v] = "s" if eng[v] == "v" else "v"
+            l2 = lst
+        elif not queued or u is None:
+            continue
+        elif r < 0.6:
+            pv = lst.index(v)
+            pu, hops = lst.index(u), int(rnd() * rnd() * 6)
+            while hops and pu > 0:
+                pu -= 1
+                hops -= eng[lst[pu]] == eng[v]
+            if anc[v] >> lst[pu] & 1 and eng[lst[pu]] == eng[v]:
+                continue
+            mid = lst[pu:pv]
+            l2 = lst[:pu] + [i for i in mid if anc[v] >> i & 1] + [v] + [i for i in mid if not anc[v] >> i & 1] + lst[pv + 1:]
+        else:
+            pu = lst.index(u)
+            pv, hops = lst.index(v), int(rnd() * rnd() * 6)
+            while hops and pv < n - 1:
+                pv += 1
+                hops -= eng[lst[pv]] == eng[u]
+            mid = lst[pu + 1:pv + 1]
+            l2 = lst[:pu] + [i for i in mid if not anc[i] >> u & 1] + [u] + [i for i in mid if anc[i] >> u & 1] + lst[pv + 1:]
+        cand = value(l2, e2, now[1])
+        if cand[0] <= now[0] + WIN[4] * (1.0 - it / ROUNDS[1]) * rnd():
+            now, lst, eng, crit = cand, l2, e2, None
+            if now[0] < top[0][0]:
+                top = (now, lst, eng)
+    now, lst, eng = top
+    end = path(lst, eng, cases[0])[1]
+    b = [busy[i][eng[i]] for i in range(n)]
+    return {"t0": [end[i] - b[i] for i in range(n)], "t1": [end[i] + lat[i] for i in range(n)], "eng": eng, "busy": b, "times": now[1],
+            "lst": lst}
 
 
 def rank_program(g, core, T, topo):
@@ -613,7 +831,7 @@ def rank_program(g, core, T, topo):
     queue = {"v": g.vector, "s": g.scalar, "t": g.tensor, "g": g, "y": g.sync}
     count = {e: 0 for e in "vstg"}
     known = {e: {} for e in "vstgy"}
-    final, ndma = {}, 0
+    final, ndma, pool = {}, 0, []
     for i in seq:
         o = ops[i]
         e = o["eng"]
@@ -627,6 +845,13 @@ def rank_program(g, core, T, topo):
                     for s2, v2 in ops[j]["known"].items():
                         if kn.get(s2, 0) < v2:
                             kn[s2] = v2
+        if e == "g" and o["kind"] == "c":
+            p0, p1 = o["wr"][0][1], o["wr"][0][2]
+            need = max([c for c, q0, q1 in pool if q0 != p0 and q0 < p1 and p0 < q1] + [0])
+            if kn.get("g", 0) < need:
+                g.wait_ge(T.sem["g"], need)
+                kn["g"] = need
+            pool.append((count["g"] + 1, p0, p1))
         o["known"] = dict(kn)
         ins = o["fn"](queue[e])
         if o["kind"] == "c":

@@ -10,11 +10,11 @@ MAGIC = 12582912.0
 SB = {
     "H0": (2048, B), "H1": (2176, B), "H2": (2176, B), "ZT": (1024, B), "SC": (2048, B),
     "W0": (1024, B), "W1": (1024, F), "W2": (1024, F), "W3": (1024, F),
-    "X0": (256, B), "OUTX": (704, B), "IN1": (576, B), "IN2": (320, B), "S0R": (768, B),
+    "X0": (256, B), "OUTX": (960, B), "OUT1": (512, B), "IN1": (576, B), "IN2": (576, B), "S0R": (768, B), "SB0": (256, B),
     "R0": (256, B), "R1": (256, B), "R2": (256, B), "CTI": (192, I32), "CTJ": (192, I32),
     "XB": (3 * 2048, B), "XR": (3 * 4096, B),
     "KL": (2, I32), "KA": (2, F), "KB": (2, F), "KH": (2, F), "KO": (2, F),
-    "KHI": (128, B), "KLO": (128, B), "LM": (256, B), "DL": (256, B), "GT": (32, B),
+    "KHI": (128, B), "KLO": (128, B), "DL": (256, B),
     "IO": (256, B), "IOG": (128, B), "IOL": (128, B), "IOM": (512, B), "IOT": (32, F), "PJ": (12, I32), "PF": (12, F), "COL": (24, F),
     "Z": (144, B), "BO": (128, B), "BOX": (128, B), "BO4": (128, B), "IW": (240, F), "IB": (240, B), "NI": (128, B), "BI": (128, B),
     "BOC": (8, F), "I37": (128, B),
@@ -22,7 +22,7 @@ SB = {
     "MOF": (128, B), "GW": (128, B), "RC": (16, F), "Q16": (128, B), "SBM": (128, B), "VQ": (512, B), "S0S": (128, B),
     "DG": (64, B), "D0": (128, B), "MD": (128, B), "DUI": (128, F), "RM": (512, B), "KM": (1024, B), "SEL": (480, B),
     "MASK": (512, B), "BR": (512, B), "NB16": (128, B), "JR": (64, B),
-    "CQ": (256, B), "CI": (256, I32), "CF": (256, F16), "CU": (768, U16),
+    "CI": (256, I32), "CJ": (256, I32), "AB": (448, F), "CF": (256, F16), "CU": (768, U16),
     "HP": (3 * 4096, B), "PP": (3 * 4112, B), "PW": (4096, F), "D16": (1024, F16), "YA": (256, B), "ZH": (256, F16), "RR": (256, F16),
     "EQ": (256, B), "OH": (768, B), "AU": (768, U16), "WU": (768, U16), "OS": (768, B), "Y": (256, F),
     "ES": (136, F), "E4": (256, F), "DW": (1024, F), "FS": (512, F), "SP": (256, B), "UP": (192, U16), "UE": (48, U16),
@@ -38,12 +38,12 @@ SEMAPHORES = ["v", "s", "t", "g", "sent"] + ["d%d" % i for i in range(44)] + ["r
 WIDTH = {k: v[1][1] for k, v in SCRATCH.items()}
 WIDTH.update({"hist": 2048, "score": 2048, "weight": 1024, "past": 256, "coming": 768, "kap": 1, "lam": 1, "yw": 1024, "yb": 256})
 
-CASES = [(1.0, 1.56, 3.8, 1.0, 1.0), (1.15, 1.1, 2.5, 1.0, 0.7), (1.35, 2.0, 5.0, 1.3, 0.7)]
+CASES = [(1.0, 1.56, 3.8, 1.0, 58.0), (1.15, 1.1, 2.5, 1.0, 63.0), (1.35, 2.0, 5.0, 1.3, 88.0)]
 CYC, PEC = 0.00083, 0.000417
-HMODE = {(0, 0): "xeeee", (0, 1): "xeeee", (1, 1): "xeeee", (1, 0): "xeeee", (2, 0): "xeeee", (2, 1): "xeeee"}
-PMODE = {(0, 0): "eeee", (0, 1): "eeee", (1, 1): "eeee", (1, 0): "eeee", (2, 0): "eeee", (2, 1): "eeee"}
-TAIL = [(96, "t"), (32, "v")]
-OPT = {"bits": (), "g1": 16, "gl": 8, "pw": 64, "xbv": (0,), "dd1": "CC", "wadd": "ppp", "wbk": [("CC", None), ("CC", "HD"), ("CC", "HD")]}
+HMODE = {(0, 0): "xeeee", (0, 1): "xee", (1, 1): "xeeee", (1, 0): "xee", (2, 0): "xeeee", (2, 1): "xeeee"}
+PMODE = {(0, 0): "eeee", (0, 1): "ee", (1, 1): "eeee", (1, 0): "ee", (2, 0): "eeee", (2, 1): "eeee"}
+TAIL = [(64, "t"), (48, "v"), (16, "v")]
+OPT = {"acc": 200.0, "d0": "s", "bhs": 1, "ems": (0, 0), "gl": 8, "pw": 64, "xbv": (0,), "dd1": "CC", "wadd": "dpp", "wbk": [("CC", "HD"), ("CC", "HD"), ("CC", "HD")]}
 SEQ = ["p0 l0 h0 n0 p1 f0 p2 l1 L0 h1 w0 N0 n1 f1 l2 L1 n2 w1 N1 f2 L2 w2 N2"]
 
 
@@ -70,7 +70,7 @@ def build(T, topo, core):
 
     def ap(a):
         if a[0] in ("kap", "lam"):
-            return T[a[0]][:]
+            return T[a[0]][a[1]:a[2]]
         if a[3] == 1 and a[6] == 1:
             return T[a[0]][a[1]:a[2], a[4]:a[5]]
         return T[a[0]][a[1]:a[2]:a[3], a[4]:a[5]:a[6]]
@@ -182,7 +182,7 @@ def build(T, topo, core):
         else:
             fn = lambda e: e.dma_start(ap(out), ap(in_))
         add(q, fn, [in_] + ([out] if accum else []), [out], (0.9 if q == "g" else 0.09, 0, 0),
-            1.9 + kb / (130.0 if accum else 250.0), "dma")
+            1.9 + kb / (OPT["acc"] if accum else 250.0), "dma")
 
     nrem = [0]
 
@@ -199,19 +199,19 @@ def build(T, topo, core):
 
     col = lambda i, p1=128: A("COL", i, i + 1, 1, 0, p1)
     G15, KBI, KAD, KBZ, M64, OFP, L0C, G8, L112, LMB = range(10)
-    GCOL, LANE, R7, U4, L4, GBEF, LOW, HIGH, PCOL = (A("PF", i, i + 1) for i in range(9))
+    GCOL, LANE, R7, U4, L4, LOW, HIGH, PCOL = (A("PF", i, i + 1) for i in range(8))
     CT1, CT0, CT2 = 256, 320, 384
     X2C = 448
     ctc = (CT0, CT1, CT2)
 
-    vset(A("S0R", 0, 512), 1.0)
     first = len(ops)
     dma("y", A("KL", 0, 1), A("kap"), 1)
-    dma("s", A("KL", 1, 2), A("lam"), 1)
+    dma("s", A("S0R", p1=8), A("coming", p1=8), 4)
+    dma("y", A("KL", 1, 2, p1=112), A("lam", p0=16), 1)
+    dma("s", A("KL", 1, 2, p0=112), A("lam", p1=16), 1)
     dma("y", A("X0"), A("past"), 64)
-    dma("s", A("S0R", 0, 512, p1=8), A("coming", 0, 512, p1=8), 4)
-    dma("y", A("H0", 0, 1024), A("hist", 1024, 2048), 400)
-    dma("s", A("H0", 1024, 2048), A("hist", 0, 1024), 500)
+    dma("y", A("H0", 0, 1024), A("hist", 0, 1024), 400)
+    dma("s", A("H0", 1024, 2048), A("hist", 1024, 2048), 500)
     for t in range(STEPS):
         c = ctc[t]
         dma("y", A("OUTX", c, c + 64, p1=32), A("coming", 256 * t, 256 * t + 256, p1=8), 4)
@@ -219,8 +219,7 @@ def build(T, topo, core):
         dma("y", A("OUTX", c, c + 64, p0=64, p1=96), src, 4)
     dma("y", A("SC"), A("score"), 900)
     dma("y", A("W0"), A("weight"), 1000)
-    dma("y", A("H1", 0, 1024), A("hist", 1024, 2048), 900)
-    dma("y", A("H1", 1024, 2048), A("hist", 0, 1024), 900)
+    dma("y", A("H1", 0, 2048), A("hist"), 1000)
     last = {}
     for i in range(first, len(ops)):
         o = ops[i]
@@ -228,37 +227,29 @@ def build(T, topo, core):
             o["ord"] = [last[o["eng"]]]
         last[o["eng"]] = i
 
-    iota(A("PJ", 8, 12), [[64, 2], [112, 2]], 0, 1)
+    iota(A("PJ", 7, 9), [[64, 2]], 0, 1)
     iota(A("IOG"), [[16, 8], [0, 16]], 0, 0)
     iota(A("IO"), [[0, 2], [1, 128]], 0, 0)
-    iota(A("IOT"), [[16, 32]], 0, 0)
     iota(A("IOL"), [[0, 8], [1, 16]], 0, 0)
-    P_ = A("PJ", 8, 9)
+    P_ = A("PJ", 7, 8)
     ts(A("PJ", 0, 1), P_, 112, None, AL.bitwise_and)
     ts(A("PJ", 1, 2), P_, 15, None, AL.bitwise_and)
     ts(A("PJ", 2, 3), P_, 7, None, AL.bitwise_and)
     ts(A("PJ", 3, 4), P_, 4, 3, AL.logical_shift_right, AL.bitwise_and)
     ts(A("PJ", 4, 5), P_, 3, None, AL.bitwise_and)
-    ts(A("PJ", 5, 6), A("PJ", 9, 10), 112, None, AL.bitwise_and)
-    ts(A("PJ", 6, 8), A("PJ", 8, 12, 2), 79, None, AL.bitwise_and)
-    vcopy(A("PF", 0, 9), A("PJ", 0, 9))
+    ts(A("PJ", 5, 7), A("PJ", 7, 9), 79, None, AL.bitwise_and)
+    vcopy(A("PF", 0, 8), A("PJ", 0, 8))
     ts(A("BO"), A("IOG"), GCOL, None, AL.is_equal)
-    ts(A("BOC"), A("IOT", 0, 8), GCOL, None, AL.is_equal)
+    ts(A("BOC"), A("IOG", 0, 128, 16), GCOL, None, AL.is_equal)
     asel(A("TRI"), A("BO"), [[1, 128]], AL.is_ge, 0.0, 0, -1)
     ts(A("IB"), A("IO", 0, 240), PCOL, None, AL.is_equal)
     lin("e", A("IW"), A("IB"))
     IF, PCY, ID = A("IW", 0, 128), A("IW", 112, 240), A("IB", 0, 128)
     lin("e", A("NI"), ID, -1.0)
-    ts(A("GT"), A("IOT"), GBEF, None, AL.is_equal)
-    ts(col(LMB, 32), A("PF", 8, 9, p1=32), 9.0, 0.25, AL.is_equal, AL.mult)
-    ts(A("KA"), A("KL"), 1.5 * 2.0 ** 39, 1.5 * 2.0 ** 39, AL.add, AL.subtract)
-    ts(A("KB"), A("KL"), 1.5 * 2.0 ** 31, 1.5 * 2.0 ** 31, AL.add, AL.subtract)
-    tt(A("KH"), A("KB"), A("KA"), AL.subtract)
-    tt(A("KO"), A("KL"), A("KB"), AL.subtract)
-    lin("e", A("DL", 0, 128), ID, A("KH", 1, 2))
-    lin("e", A("DL", 128, 256), ID, A("KO", 1, 2))
-    mm(group(A("UU", 0, 256, p1=32), [(A("GT"), A("DL"))]))
-    lin("e", A("LM", p1=32), A("UU", 0, 256, p1=32), 1.0, col(LMB, 32))
+    ts(A("KH"), A("KL"), 1.5 * 2.0 ** 31, 1.5 * 2.0 ** 31, AL.add, AL.subtract)
+    tt(A("KO"), A("KL"), A("KH"), AL.subtract)
+    lin("e", A("DL", 0, 128), A("IB", 112, 240), A("KH", 1, 2))
+    lin("e", A("DL", 128, 256), A("IB", 112, 240), A("KO", 1, 2))
     lin("e", A("KHI"), A("TRI"), A("KH", 0, 1))
     lin("e", A("KLO"), A("TRI"), A("KO", 0, 1))
     iota(A("H1", 2048, 2176), [[0, 128]], 0, 0)
@@ -276,17 +267,25 @@ def build(T, topo, core):
     asel(A("SH"), A("BO"), [[1, 128]], AL.is_equal, 0.0, -1, -1)
     lin("e", col(G8, 32), A("PF", 2, 3, p1=32), 16.0)
     ts(A("S0S", p1=8), A("IO", 0, 128, p1=8), col(G8, 8), None, AL.is_equal)
-    mm(group(A("LGL", 0, 256), [(A("SH"), A("X0")), (A("S0S", p1=8), A("S0R", 0, 256, p1=8))]))
-    lin("e", A("S0R", 512, 768), A("LGL", 0, 256))
-    mm(group(A("LGN", 0, 256), [(A("SH"), A("S0R", 512, 768)), (A("S0S", p1=8), A("S0R", 256, 512, p1=8))]))
-    lin("e", A("OUTX", X2C, 704), A("LGN", 0, 256))
-    remote(A("IN1", 0, 512), A("S0R", 256, 768), (rank + MOVE) % NR, 220)
+    ts(A("GW", p1=32), A("IOG", 0, 128, p1=32), col(G8, 32), None, AL.is_equal)
+    G8R = A("GW", p1=8)
+    mm(group(A("ZN", 0, 256), [(G8R, A("S0R", 0, 256, p1=8))]))
+    lin("e", A("SB0", 0, 128), A("ZN", 0, 128))
+    lin("e", A("SB0", 128, 256), A("ZN", 128, 256))
+    mm(group(A("LGL", 0, 256), [(A("SH"), A("X0")), (A("S0S", p1=8), A("S0R", 0, 256, p1=8))])
+       + group(A("LGL", 256, 512), [(G8R, A("S0R", 256, 512, p1=8))]))
+    lin("e", A("OUT1"), A("LGL"))
+    mm(group(A("LGN", 0, 256), [(A("SH"), A("OUT1", 0, 256)), (A("S0S", p1=8), A("S0R", 256, 512, p1=8))])
+       + group(A("LGN", 256, 512), [(G8R, A("S0R", 512, 768, p1=8))]))
+    lin("e", A("OUTX", X2C, X2C + 512), A("LGN"))
+    remote(A("IN1", 0, 512), A("OUT1"), (rank + MOVE) % NR, 220)
     remote(A("IN1", 512, 576), A("OUTX", CT1, CT1 + 64), (rank + MOVE) % NR, 40)
-    remote(A("IN2"), A("OUTX", CT2, 704), (rank + 2 * MOVE) % NR, 120)
+    remote(A("IN2"), A("OUTX", CT2, X2C + 512), (rank + 2 * MOVE) % NR, 160)
     dma("y", A("R0", p1=32), A("OUTX", CT0, CT0 + 64), 16)
     dma("y", A("R1", p1=32), A("IN1", 512, 576), 16)
     dma("y", A("R2", p1=32), A("IN2", 0, 64), 16)
-    XT = (A("X0"), A("IN1", 256, 512), A("IN2", 64, 320))
+    XT = (A("X0"), A("IN1", 0, 256), A("IN2", 64, 320))
+    ST = (A("SB0"), A("IN1", 256, 512), A("IN2", 320, 576))
 
     def xs(t, a, b):
         return A(XT[t][0], XT[t][4] + a, XT[t][4] + b)
@@ -318,10 +317,8 @@ def build(T, topo, core):
     for r in range(4):
         asel(A("BR", 128 * r, 128 * r + 128), A("BO"), [[0, 8], [1, 4], [0, 4]], AL.is_equal, 0.0, -r, 0)
     iota(A("JR"), [[1, 4], [0, 16]], 0, 0)
-    ts(A("GW", p1=32), A("IOG", 0, 128, p1=32), col(G8, 32), None, AL.is_equal)
     rc = lambda i, j=None: A("RC", i, i + 1 if j is None else j, p1=32)
-    iota(rc(0, 2), [[15, 2]], 1, 0)
-    asel(rc(0), rc(0), [[0, 1]], AL.is_gt, 0.0, 8, -1)
+    iota(rc(1), [[0, 1]], 16, 0)
     asel(rc(1), rc(1), [[0, 1]], AL.is_gt, 0.0, 24, -1)
     iota(rc(2, 8), [[512, 6]], -1024, 0)
     asel(rc(4, 8), rc(4, 8), [[0, 4]], AL.is_gt, -256.0, 24, -1)
@@ -331,12 +328,15 @@ def build(T, topo, core):
     asel(rc(8, 12), rc(8, 12), [[0, 4]], AL.is_equal, 0.0, -9, 1)
     asel(rc(8, 12), rc(8, 12), [[0, 4]], AL.not_equal, -1.0, -8, 1)
     G32 = A("GW", 0, 128, p1=32)
-    lin("e", A("SBM", p1=32), G32, rc(0))
     lin("e", A("Q16", p1=32), G32, rc(1))
     for q in range(4):
         lin("e", A("VQ", 128 * q, 128 * q + 128, p1=32), G32, rc(4 + q), rc(8 + q))
     ts(A("DG"), A("IOL", 0, 64), LANE, -16.0, AL.is_equal, AL.mult)
-    ts(A("D0"), A("IOL"), LANE, None, AL.is_gt)
+    if OPT["d0"] == "s":
+        lin("e", col(LMB), LANE, -256.0, -128.0)
+        act(A("D0"), A("IOL"), AF.Sigmoid, bias=col(LMB), scale=256.0, extra=1.3)
+    else:
+        ts(A("D0"), A("IOL"), LANE, None, AL.is_gt)
     ts(A("MD"), A("IOL"), LANE, -2.0 ** 20, AL.not_equal, AL.mult)
     iota(A("DUI"), [[1, 128]], 6145, 0)
     nk = max([16 * n for n, q in TAIL if q == "v"] + [16])
@@ -363,20 +363,13 @@ def build(T, topo, core):
         return A(nm, m * (256 * t + a), m * (256 * t + b))
 
     def prep(t):
-        R = ("S0R", "IN1", "R2")[t]
         for a, n in ((0, 128), (128, 128)) if t == 0 else ((0, 256),):
             cc = A("CC" if a == 0 else "HD", 0, n)
-            x, srow = xs(t, a, a + n), A(R, a, a + n, p1=32)
-            whole = [(A("KHI"), x), (A("KLO"), x), (A("LM", 0, 128, p1=32), srow), (A("LM", 128, 256, p1=32), srow)]
-            mm(group(cc, whole))
-            if t in OPT["bits"]:
-                ts(A("CI", a, a + n), cc, 8421375.5, None, AL.add)
-                ts(A("CI", a, a + n), A("CI", a, a + n), 5, 2047, AL.logical_shift_right, AL.bitwise_and)
-                vcopy(st("CU", t, a, a + n), A("CI", a, a + n))
-                continue
-            ts(A("CQ", a, a + n), cc, 1.5 * 2.0 ** 39, 1.5 * 2.0 ** 39, AL.add, AL.subtract)
-            mm(group(cc, whole + [(A("NI"), A("CQ", a, a + n))]))
-            ts(st("CU", t, a, a + n), cc, 1.0 / 32, 1023.5, AL.mult, AL.add)
+            x, s = xs(t, a, a + n), A(ST[t][0], ST[t][4] + a, ST[t][4] + a + n)
+            mm(group(cc, [(A("KHI"), x), (A("KLO"), x), (A("DL", 0, 128), s), (A("DL", 128, 256), s)]))
+            vcopy(A("CI", a, a + n), cc)
+            ts(A("CJ", a, a + n), A("CI", a, a + n), 5, 2047, AL.logical_shift_right, AL.bitwise_and)
+            vcopy(st("CU", t, a, a + n), A("CJ", a, a + n))
         for h in (t % 2, 1 - t % 2):
             x = xs(t, 128 * h, 128 * h + 128)
             c0 = 256 * t + 128 * h
@@ -395,8 +388,7 @@ def build(T, topo, core):
                         asel(o, i, [[0, 128]], AL.is_gt, 0.0, 16, -1)
                     else:
                         asel(o, i, [[0, 128]], AL.is_ge, 0.0, -16, 1)
-        mm(group(A("CC", 256, 512), [(A("SBM", p1=32), A(R, 0, 256, p1=32))]))
-        ts(st("OS", t, 0, 256), A("CC", 256, 512), LANE, None, AL.is_equal)
+        ts(st("OS", t, 0, 256), ST[t], LANE, None, AL.is_equal)
 
     def ints(t, h):
         u0 = 128 * h
@@ -435,22 +427,25 @@ def build(T, topo, core):
         ts(hs("ZH"), za, 1800.0, None, AL.subtract)
         if h == t % 2 and t < STEPS - 1:
             aa = A("UU", 0, 128)
-            mm(group(dd, [(A("DM"), hs("ZH"))]))
+            ts(hs("RR"), hs("ZH"), -1.0, -14084.5, AL.mult, AL.add)
+            mm(group(d2, [(A("DM"), hs("ZH")), (A("DM"), hs("RR"))]))
+            ts(hs("EQ"), d2, 0.0, 4096.0, AL.is_equal, AL.mult)
             ts(hs("YA"), hs("ZH"), 37.0, col(KBZ), AL.mult, AL.add)
             mm(group(aa, [(A("I37"), hs("ZH")), (A("NI"), hs("YA"))]))
+            ts(st("AU", t, u0, u0 + 128), aa, col(KAD), None, AL.add)
         else:
             lin("e", hs("YA"), za, 37.0, col(KBI))
             mm(group(aa, [(A("I37"), hs("ZH")), (A("NI"), hs("YA"))]) + group(dd, [(A("DM"), hs("ZH"))]))
-        ts(st("AU", t, u0, u0 + 128), aa, col(KAD), None, AL.add)
-        ts(hs("RR"), dd, 12284.5, None, AL.add)
+            ts(st("AU", t, u0, u0 + 128), aa, col(KAD), None, AL.add)
+            ts(hs("RR"), dd, 12284.5, None, AL.add)
+            mm(group(d2, [(A("DM"), hs("ZH")), (A("NI"), hs("RR"))]))
+            act(hs("EQ"), d2, AF.Relu, scale=-4096.0, bias=-4096.0 * 12287)
+            ts(hs("EQ"), d2, -12288.0, 4096.0, AL.is_equal, AL.mult)
+            either("e")
         qs = PMODE[t, h]
         n = 128 // len(qs)
         for i, q in enumerate(qs):
             gather(q, pp(t, h, 16 * n * i, 16 * n * (i + 1)), A("SC"), st("AU", t, u0 + n * i, u0 + n * (i + 1)))
-        mm(group(d2, [(A("DM"), hs("ZH")), (A("NI"), hs("RR"))]))
-        act(hs("EQ"), d2, AF.Relu, scale=-4096.0, bias=-4096.0 * 12287)
-        ts(hs("EQ"), d2, -12288.0, 4096.0, AL.is_equal, AL.mult)
-        either("e")
         mm(group(w_, [(A("WM"), hs("EQ"))]))
         act(oh, w_, AF.Relu)
         ts(oh, w_, 0.0, None, AL.max)
@@ -476,7 +471,13 @@ def build(T, topo, core):
         at = 128
         for b in range(7):
             n = 112 - 16 * b
-            ts(A("EM", at, at + n), A("HD", 128 - n, 128), A("KS", 16 * b + 15, 16 * b + 16), None, AL.is_equal)
+            key = A("KS", 16 * b + 15, 16 * b + 16)
+            if b < OPT["ems"][t]:
+                act(A("AB", at - 128, at - 128 + n), A("HD", 128 - n, 128), AF.Abs, scale=-1.0, bias=key)
+                if b == OPT["ems"][t] - 1:
+                    act(A("EM", 128, at + n), A("AB", 0, at - 128 + n), AF.Relu, scale=-1.0, bias=1.0)
+            else:
+                ts(A("EM", at, at + n), A("HD", 128 - n, 128), key, None, AL.is_equal)
             items.append((A("UU", 256 - n, 256), A("BO4"), A("EM", at, at + n), False, b == 6))
             at += n
         mm(items[:5])
@@ -505,7 +506,7 @@ def build(T, topo, core):
         ts(A("UE", 16 * t, 16 * t + 16), A("UU", 0, 16), 1.0 / 16, 128.0, AL.mult, AL.add)
         ts(A("UP", 64 * t, 64 * t + 64), A("UU", 0, 64), col(OFP), None, AL.add)
 
-    first_sig = [1.3]
+    first_sig = [0.0 if OPT["d0"] == "s" else 1.3]
 
     def carry(t, lg, a, n, learner):
         o = a % 128
@@ -521,11 +522,15 @@ def build(T, topo, core):
                 tt(bn, oh, y, AL.subtract)
             else:
                 tt(A("ES", o, o + n), oh, y, AL.subtract)
-                mm(group(bh, [(A("HI"), A("BI%d" % t, a, a + n))]))
+                if OPT["bhs"]:
+                    lin("s", bh, A("BI%d" % t, a, a + n), 0.5)
+                else:
+                    mm(group(bh, [(A("HI"), A("BI%d" % t, a, a + n))]))
                 tt(bn, A("ES", o, o + n), bh, AL.add)
         else:
             y = A("Y", a, a + n)
-            mm(group(bh, [(ID, oh), (A("HI"), A("BI%d" % t, a, a + n))]))
+            if o == 0:
+                mm(group(A(bh[0], bh[4], bh[4] + 128), [(ID, st("OS", t, a, a + 128)), (A("HI"), A("BI%d" % t, a, a + 128))]))
             act(y, A(lg, 0, n), AF.Sigmoid)
             tt(bn, bh, y, AL.subtract)
         first_sig[0] = 0.0
@@ -594,8 +599,8 @@ def build(T, topo, core):
 
 
 HOP = 0.11
-ROUNDS = [300, 80000]
-WIN = [4.0, 0.15, 0.5, 0.3, 0.2, 0.0]
+ROUNDS = [1500, 180000]
+WIN = [4.0, 0.15, 0.5, 0.3, 0.2, 0.3]
 SEED = [12345]
 PLAN = {}
 
@@ -633,7 +638,7 @@ def order(ops):
         o["deps"] = set(j for j in o["deps"] if not m >> j & 1)
         for j in o["deps"]:
             m |= 1 << j
-        above.append(m)
+        above.append(0 if o["kind"] == "rem" else m)
     if "t0" not in PLAN:
         PLAN.update(search(ops))
     for i, o in enumerate(ops):
@@ -652,7 +657,7 @@ def search(ops):
         lat = [o["lat"] * dl for o in ops]
         pre = [[(j, lat[j] + (HOP if j in o["deps"] else 0.0)) for j in o["deps"] | o["soft"]] + [(j, 0.0) for j in o.get("ord", [])]
                for o in ops]
-        cases.append((busy, lat, pre, wt))
+        cases.append((busy, lat, pre, 1.0 / wt))
     busy, lat, pre, _ = cases[0]
     post = [[] for _ in range(n)]
     for i in range(n):
@@ -699,7 +704,7 @@ def search(ops):
             end[i] = free[q] = t = t + b_[i][q]
             if t + l_[i] > top:
                 top = t + l_[i]
-        return top + WIN[5] * sum(end) / n
+        return top
 
     zero, wsum = [0.0] * n, sum(c[3] for c in cases)
 
@@ -765,14 +770,33 @@ def search(ops):
             last = why[last][0]
         return out, end
 
-    def value(lst, eng, ref=None):
-        times = []
-        for c in cases:
-            times.append(replay(lst, eng, c))
-            if ref and times[-1] > ref[len(times) - 1] + 1.0:
-                return 1e9, times
-        load = sum(busy[i]["v"] for i in flex if eng[i] == "v")
-        return sum(x * c[3] for x, c in zip(times, cases)) / wsum + WIN[3] * load, times
+    sinks = [i for i in range(n) if not post[i]]
+
+    def value(lst, eng, at=0, now=None):
+        times, ends = [], []
+        seen = {}
+        for i in lst[at - 1::-1] if at else []:
+            if eng[i] not in seen:
+                seen[eng[i]] = i
+                if len(seen) == 5:
+                    break
+        rest = lst[at:]
+        for k, (b_, l_, p_, w_) in enumerate(cases):
+            end = list(now[2][k]) if now else [0.0] * n
+            free = {e: end[seen[e]] if e in seen else 0.0 for e in "vstgy"}
+            for i in rest:
+                q = eng[i]
+                t = free[q]
+                for j, d in p_[i]:
+                    if end[j] + d > t:
+                        t = end[j] + d
+                end[i] = free[q] = t + b_[i][q]
+            times.append(max(end[i] + l_[i] for i in sinks))
+            if now and times[k] > now[1][k] + 1.0:
+                return 1e9, times, ends
+            ends.append(end)
+        rel = [x / c[4] * CASES[0][4] for x, c in zip(times, CASES)]
+        return (1 - WIN[5]) * sum(rel) / len(rel) + WIN[5] * max(rel), times, ends
 
     lst, eng = sorted(range(n), key=lambda i: (best[1][i], i)), list(best[3])
     now = value(lst, eng)
@@ -790,7 +814,7 @@ def search(ops):
                 continue
             e2 = list(eng)
             e2[v] = "s" if eng[v] == "v" else "v"
-            l2 = lst
+            l2, pu = lst, lst.index(v)
         elif not queued or u is None:
             continue
         elif r < 0.6:
@@ -811,7 +835,7 @@ def search(ops):
                 hops -= eng[lst[pv]] == eng[u]
             mid = lst[pu + 1:pv + 1]
             l2 = lst[:pu] + [i for i in mid if not anc[i] >> u & 1] + [u] + [i for i in mid if anc[i] >> u & 1] + lst[pv + 1:]
-        cand = value(l2, e2, now[1])
+        cand = value(l2, e2, pu, now)
         if cand[0] <= now[0] + WIN[4] * (1.0 - it / ROUNDS[1]) * rnd():
             now, lst, eng, crit = cand, l2, e2, None
             if now[0] < top[0][0]:

from concourse.bass import DstId, RemoteDMATransfer
from concourse.mybir import dt, AluOpType, AxisListType, ActivationFunctionType

AL = AluOpType
AF = ActivationFunctionType
F, B, I32, U16, F16 = "float32", "bfloat16", "int32", "uint16", "float16"
NR, STEPS, MOVE = 4, 3, 3
MAGIC = 12582912.0

SB = {
    "H0": (2048, B), "H1": (2176, B), "H2": (2176, B), "ZT": (1024, B), "SC": (2048, B),
    "W0": (1024, B), "W1": (1024, F), "W2": (1024, F), "W3": (1024, F),
    "X0": (256, B), "OUTX": (960, B), "OUT1": (512, B), "IN1": (576, B), "IN2": (576, B), "S0R": (768, B), "SB0": (256, B),
    "R0": (256, B), "R1": (256, B), "R2": (256, B), "CTI": (192, I32), "CTJ": (192, I32),
    "XB": (3 * 2048, B), "XR": (3 * 4096, B),
    "KL": (2, I32), "KA": (2, F), "KB": (2, F), "KH": (2, F), "KO": (2, F),
    "KHI": (128, B), "KLO": (128, B), "DL": (256, B),
    "IO": (256, B), "IOG": (128, B), "IOL": (128, B), "IOM": (512, B), "IOT": (32, F), "PJ": (12, I32), "PF": (12, F), "COL": (24, F),
    "Z": (144, B), "BO": (128, B), "BOX": (128, B), "BO4": (128, B), "IW": (240, F), "IB": (240, B), "NI": (128, B), "BI": (128, B),
    "BOC": (8, F), "I37": (128, B),
    "HI": (128, F), "TRI": (128, B), "WM": (128, B), "WN": (128, B), "NB": (128, B), "SH": (128, B), "DM": (128, B), "S0M": (128, B),
    "MOF": (128, B), "GW": (128, B), "RC": (16, F), "Q16": (128, B), "SBM": (128, B), "VQ": (512, B), "S0S": (128, B),
    "DG": (64, B), "D0": (128, B), "MD": (128, B), "DUI": (128, F), "RM": (512, B), "KM": (1024, B), "SEL": (480, B),
    "MASK": (512, B), "BR": (512, B), "NB16": (128, B), "JR": (64, B),
    "CI": (256, I32), "CJ": (256, I32), "AB": (448, F), "CF": (256, F16), "CU": (768, U16),
    "HP": (3 * 4096, B), "PP": (3 * 4112, B), "PW": (4096, F), "D16": (1024, F16), "YA": (256, B), "ZH": (256, F16), "RR": (256, F16),
    "EQ": (256, B), "OH": (768, B), "AU": (768, U16), "WU": (768, U16), "OS": (768, B), "Y": (256, F),
    "ES": (136, F), "E4": (256, F), "DW": (1024, F), "FS": (512, F), "SP": (256, B), "UP": (192, U16), "UE": (48, U16),
    "PC": (128, F16), "KS": (128, F), "EM": (576, B), "OM": (128, F), "OT": (128, F), "HU": (8, U16), "HV": (8, U16),
    "OLD": (128, B), "NEW": (128, B), "LS": (1024, F),
    "BN0": (264, F), "BN1": (256, F), "BN2": (256, F), "BI1": (256, F), "BI2": (256, F), "BI3": (256, F),
}
BANKS = ["LGL", "LGN", "ZL", "ZN", "DD", "CC", "UU", "HD"]
SCRATCH = {k: ("sbuf", [128, v[0]], v[1]) for k, v in SB.items()}
for _b in BANKS:
    SCRATCH[_b] = ("psum", [128, 512], F)
SEMAPHORES = ["v", "s", "t", "g", "sent"] + ["d%d" % i for i in range(44)] + ["r%d" % i for i in range(12)]
WIDTH = {k: v[1][1] for k, v in SCRATCH.items()}
WIDTH.update({"hist": 2048, "score": 2048, "weight": 1024, "past": 256, "coming": 768, "kap": 1, "lam": 1, "yw": 1024, "yb": 256})

CASES = [(1.0, 1.56, 3.8, 1.0, 58.0), (1.15, 1.1, 2.5, 1.0, 63.0), (1.35, 2.0, 5.0, 1.3, 88.0)]
CYC, PEC = 0.00083, 0.000417
HMODE = {(0, 0): "xeeee", (0, 1): "xee", (1, 1): "xeeee", (1, 0): "xee", (2, 0): "xeeee", (2, 1): "xeeee"}
PMODE = {(0, 0): "eeee", (0, 1): "ee", (1, 1): "eeee", (1, 0): "ee", (2, 0): "eeee", (2, 1): "eeee"}
TAIL = [(64, "t"), (48, "v"), (16, "v")]
OPT = {"acc": 200.0, "d0": "s", "bhs": 1, "ems": (0, 0), "gl": 8, "pw": 64, "xbv": (0,), "dd1": "CC", "wadd": "dpp", "wbk": [("CC", "HD"), ("CC", "HD"), ("CC", "HD")]}
SEQ = ["p0 l0 h0 n0 p1 f0 p2 l1 L0 h1 w0 N0 n1 f1 l2 L1 n2 w1 N1 f2 L2 w2 N2"]


def A(name, c0=0, c1=None, cs=1, p0=0, p1=128, ps=1):
    return (name, p0, p1, ps, c0, WIDTH[name] if c1 is None else c1, cs)


def _bits(a, b, s):
    if s == 1:
        return ((1 << (b - a)) - 1) << a
    m = 0
    for i in range(a, b, s):
        m |= 1 << i
    return m


def ncol(a):
    return (a[5] - a[4] + a[6] - 1) // a[6]


def build(T, topo, core):
    rank = T.rank_of(core)
    ops = []

    def ap(a):
        if a[0] in ("kap", "lam"):
            return T[a[0]][a[1]:a[2]]
        if a[3] == 1 and a[6] == 1:
            return T[a[0]][a[1]:a[2], a[4]:a[5]]
        return T[a[0]][a[1]:a[2]:a[3], a[4]:a[5]:a[6]]

    def sc(x):
        return ap(x) if isinstance(x, tuple) else x

    def aps(*xs):
        return [x for x in xs if isinstance(x, tuple)]

    def add(eng, fn, rd, wr, cost, lat=0.0, kind="c", **kw):
        o = {"eng": eng, "fn": fn, "rd": rd, "wr": wr, "cost": cost, "lat": lat, "kind": kind, "name": wr[0][0]}
        o.update(kw)
        ops.append(o)
        return o

    def vcost(n, c=1.0):
        return (0.05 + max(64, n * c) * CYC, 0, 0)

    def two(*xs):
        return all(SCRATCH[x[0]][2] in (B, U16, F16) for x in xs)

    def ts(out, in0, s1, s2, op0, op1=None):
        def fn(e):
            if op1 is None:
                return e.tensor_scalar(ap(out), ap(in0), sc(s1), None, op0)
            return e.tensor_scalar(ap(out), ap(in0), sc(s1), sc(s2), op0, op1)
        add("v", fn, aps(in0, s1, s2), [out], vcost(ncol(out), 0.5 if two(out, in0) else 1))

    def tt(out, in0, in1, op):
        both = in0[0] not in BANKS and in1[0] not in BANKS
        add("v", lambda e: e.tensor_tensor(ap(out), ap(in0), ap(in1), op), [in0, in1], [out], vcost(ncol(out), 2 if both else 1))

    def vcopy(out, in_):
        add("v", lambda e: e.tensor_copy(ap(out), ap(in_)), [in_], [out], vcost(ncol(out), 0.5 if two(out, in_) else 1))

    def vset(out, val):
        add("v", lambda e: e.memset(ap(out), val), [], [out], vcost(ncol(out), 0.5 if two(out) else 1))

    def scan(out, d0, d1, op0, op1):
        add("v", lambda e: e.tensor_tensor_scan(ap(out), ap(d0), ap(d1), 0.0, op0, op1), [d0, d1], [out], vcost(ncol(out)))

    def vgather(out, win, off, in1):
        add("v", lambda e: e.tensor_tensor(ap(out), ap(win).indirect(ap(off)), ap(in1), AL.mult), [win, off, in1], [out],
            (0.05, ncol(out), 0))

    def vscatter(win, off, in_):
        add("v", lambda e: e.tensor_copy(ap(win).indirect(ap(off)), ap(in_)), [off, in_], [win], (0.05, 0, ncol(in_)))

    def act(out, in_, func=AF.Identity, bias=0.0, scale=1.0, extra=0.0):
        c = vcost(ncol(out))
        add("s", lambda e: e.activation(ap(out), ap(in_), func, bias=sc(bias), scale=sc(scale)), aps(in_, bias, scale), [out],
            (c[0] + extra, 0, 0))

    def either(q):
        v, s = ops.pop(), ops.pop()
        o = v if q == "v" else s
        if q == "e":
            o["alt"] = {"s": (s["fn"], s["cost"]), "v": (v["fn"], v["cost"])}
        ops.append(o)

    def lin(q, out, in_, scale=1.0, bias=0.0):
        act(out, in_, AF.Identity, bias, scale)
        ts(out, in_, scale, bias, AL.mult, AL.add)
        either(q)

    def gather(q, out, win, off, scale=1.0, bias=0.0):
        add("s", lambda e: e.activation(ap(out), ap(win).indirect(ap(off)), AF.Identity, bias=bias, scale=scale), [win, off], [out],
            (0.065, ncol(out), 0))
        add("v", lambda e: e.tensor_scalar(ap(out), ap(win).indirect(ap(off)), scale, bias, AL.mult, AL.add), [win, off], [out],
            (0.05, ncol(out), 0))
        either(q)

    def mm(items):
        def fn(e):
            r = None
            for o, l, rh, st, sp in items:
                r = e.matmul(ap(o), ap(l), ap(rh), st, sp)
            return r
        rd, wr, cost = [], [], 0.04
        for o, l, rh, st, sp in items:
            rd += [l, rh]
            wr.append(o)
            cost += max(min(64, ncol(l)), ncol(rh)) * (4 if SCRATCH[rh[0]][2] == F else 1) * PEC
        add("t", fn, rd, wr, (cost, 0, 0))

    def mms(items, n):
        for i in range(0, len(items), n):
            mm(items[i:i + n])

    def group(out, pairs, start=True, stop=True):
        n = len(pairs)
        return [(out, l, r, start and i == 0, stop and i == n - 1) for i, (l, r) in enumerate(pairs)]

    def iota(out, pat, base, cm):
        c = (0.13 + 2 * ncol(out) * CYC, 0, 0)
        if SCRATCH[out[0]][2] == I32:
            add("g", lambda e: e.iota(ap(out), pat, base, cm), [], [out], c)
        else:
            add("g", lambda e: e.iota(ap(out), pat, base, cm, allow_small_or_imprecise_dtypes=True), [], [out], c)

    def asel(out, in_, pat, cmp_, fill, base, cm):
        add("g", lambda e: e.affine_select(ap(out), ap(in_), pat, cmp_, fill, base, cm), [in_], [out],
            (0.17 + 2 * ncol(out) * CYC, 0, 0))

    def dma(q, out, in_, kb, accum=False):
        if accum:
            fn = lambda e: e.dma_start(ap(out), ap(in_), accum_op=AL.add)
        else:
            fn = lambda e: e.dma_start(ap(out), ap(in_))
        add(q, fn, [in_] + ([out] if accum else []), [out], (0.9 if q == "g" else 0.09, 0, 0),
            1.9 + kb / (OPT["acc"] if accum else 250.0), "dma")

    nrem = [0]

    def remote(out, in_, to_rank, kb):
        dst = T.cores[to_rank]
        rid, pid = topo.addr(dst, core)
        mask = 0
        for e_ in topo.engines(core, dst)[:8]:
            mask |= 1 << e_
        sem = "r%d" % nrem[0]
        nrem[0] += 1
        add("g", lambda e: e.remote_dma(ap(out), ap(in_), T.sem[sem], T.sem["sent"], pid, rid, mask), [in_], [out],
            (0.4, 0, 0), 2.0 + kb / 60.0, "rem", sem=sem, to=to_rank)

    col = lambda i, p1=128: A("COL", i, i + 1, 1, 0, p1)
    G15, KBI, KAD, KBZ, M64, OFP, L0C, G8, L112, LMB = range(10)
    GCOL, LANE, R7, U4, L4, LOW, HIGH, PCOL = (A("PF", i, i + 1) for i in range(8))
    CT1, CT0, CT2 = 256, 320, 384
    X2C = 448
    ctc = (CT0, CT1, CT2)

    first = len(ops)
    dma("y", A("KL", 0, 1), A("kap"), 1)
    dma("s", A("S0R", p1=8), A("coming", p1=8), 4)
    dma("y", A("KL", 1, 2, p1=112), A("lam", p0=16), 1)
    dma("s", A("KL", 1, 2, p0=112), A("lam", p1=16), 1)
    dma("y", A("X0"), A("past"), 64)
    dma("y", A("H0", 0, 1024), A("hist", 0, 1024), 400)
    dma("s", A("H0", 1024, 2048), A("hist", 1024, 2048), 500)
    for t in range(STEPS):
        c = ctc[t]
        dma("y", A("OUTX", c, c + 64, p1=32), A("coming", 256 * t, 256 * t + 256, p1=8), 4)
        src = A("past", ps=16) if t == 0 else A("coming", 256 * (t - 1), 256 * t, p1=8)
        dma("y", A("OUTX", c, c + 64, p0=64, p1=96), src, 4)
    dma("y", A("SC"), A("score"), 900)
    dma("y", A("W0"), A("weight"), 1000)
    dma("y", A("H1", 0, 2048), A("hist"), 1000)
    last = {}
    for i in range(first, len(ops)):
        o = ops[i]
        if o["eng"] in last:
            o["ord"] = [last[o["eng"]]]
        last[o["eng"]] = i

    iota(A("PJ", 7, 9), [[64, 2]], 0, 1)
    iota(A("IOG"), [[16, 8], [0, 16]], 0, 0)
    iota(A("IO"), [[0, 2], [1, 128]], 0, 0)
    iota(A("IOL"), [[0, 8], [1, 16]], 0, 0)
    P_ = A("PJ", 7, 8)
    ts(A("PJ", 0, 1), P_, 112, None, AL.bitwise_and)
    ts(A("PJ", 1, 2), P_, 15, None, AL.bitwise_and)
    ts(A("PJ", 2, 3), P_, 7, None, AL.bitwise_and)
    ts(A("PJ", 3, 4), P_, 4, 3, AL.logical_shift_right, AL.bitwise_and)
    ts(A("PJ", 4, 5), P_, 3, None, AL.bitwise_and)
    ts(A("PJ", 5, 7), A("PJ", 7, 9), 79, None, AL.bitwise_and)
    vcopy(A("PF", 0, 8), A("PJ", 0, 8))
    ts(A("BO"), A("IOG"), GCOL, None, AL.is_equal)
    ts(A("BOC"), A("IOG", 0, 128, 16), GCOL, None, AL.is_equal)
    asel(A("TRI"), A("BO"), [[1, 128]], AL.is_ge, 0.0, 0, -1)
    ts(A("IB"), A("IO", 0, 240), PCOL, None, AL.is_equal)
    lin("e", A("IW"), A("IB"))
    IF, PCY, ID = A("IW", 0, 128), A("IW", 112, 240), A("IB", 0, 128)
    lin("e", A("NI"), ID, -1.0)
    ts(A("KH"), A("KL"), 1.5 * 2.0 ** 31, 1.5 * 2.0 ** 31, AL.add, AL.subtract)
    tt(A("KO"), A("KL"), A("KH"), AL.subtract)
    lin("e", A("DL", 0, 128), A("IB", 112, 240), A("KH", 1, 2))
    lin("e", A("DL", 128, 256), A("IB", 112, 240), A("KO", 1, 2))
    lin("e", A("KHI"), A("TRI"), A("KH", 0, 1))
    lin("e", A("KLO"), A("TRI"), A("KO", 0, 1))
    iota(A("H1", 2048, 2176), [[0, 128]], 0, 0)
    vset(A("ZT"), 0.0)
    for t, h in ((0, 1), (1, 1), (1, 0), (2, 0), (2, 1)):
        if HMODE[t, h][0] == "x" and (t > 0 or h not in OPT["xbv"]):
            dma("y", A("XB", 2048 * t + 1024 * h, 2048 * t + 1024 * h + 1024), A("ZT"), 256)

    iota(A("OUTX", CT1, X2C, p0=32, p1=64), [[0, 3], [1, 64]], 0, 64)
    asel(A("OUTX", CT1, X2C, p0=32, p1=64), A("OUTX", CT1, X2C, p0=32, p1=64), [[0, 192]], AL.is_gt, 1.0, 4, -1)
    vcopy(A("CTI", p0=64, p1=96), A("OUTX", CT1, X2C, p0=64, p1=96))
    ts(A("CTJ", p0=64, p1=96), A("CTI", p0=64, p1=96), 3, None, AL.bitwise_and)
    vcopy(A("OUTX", CT1, X2C, p0=64, p1=96), A("CTJ", p0=64, p1=96))
    act(A("OUTX", CT1, X2C, p0=96, p1=128), A("OUTX", CT1, X2C, p0=64, p1=96), AF.Square)
    asel(A("SH"), A("BO"), [[1, 128]], AL.is_equal, 0.0, -1, -1)
    lin("e", col(G8, 32), A("PF", 2, 3, p1=32), 16.0)
    ts(A("S0S", p1=8), A("IO", 0, 128, p1=8), col(G8, 8), None, AL.is_equal)
    ts(A("GW", p1=32), A("IOG", 0, 128, p1=32), col(G8, 32), None, AL.is_equal)
    G8R = A("GW", p1=8)
    mm(group(A("ZN", 0, 256), [(G8R, A("S0R", 0, 256, p1=8))]))
    lin("e", A("SB0", 0, 128), A("ZN", 0, 128))
    lin("e", A("SB0", 128, 256), A("ZN", 128, 256))
    mm(group(A("LGL", 0, 256), [(A("SH"), A("X0")), (A("S0S", p1=8), A("S0R", 0, 256, p1=8))])
       + group(A("LGL", 256, 512), [(G8R, A("S0R", 256, 512, p1=8))]))
    lin("e", A("OUT1"), A("LGL"))
    mm(group(A("LGN", 0, 256), [(A("SH"), A("OUT1", 0, 256)), (A("S0S", p1=8), A("S0R", 256, 512, p1=8))])
       + group(A("LGN", 256, 512), [(G8R, A("S0R", 512, 768, p1=8))]))
    lin("e", A("OUTX", X2C, X2C + 512), A("LGN"))
    remote(A("IN1", 0, 512), A("OUT1"), (rank + MOVE) % NR, 220)
    remote(A("IN1", 512, 576), A("OUTX", CT1, CT1 + 64), (rank + MOVE) % NR, 40)
    remote(A("IN2"), A("OUTX", CT2, X2C + 512), (rank + 2 * MOVE) % NR, 160)
    dma("y", A("R0", p1=32), A("OUTX", CT0, CT0 + 64), 16)
    dma("y", A("R1", p1=32), A("IN1", 512, 576), 16)
    dma("y", A("R2", p1=32), A("IN2", 0, 64), 16)
    XT = (A("X0"), A("IN1", 0, 256), A("IN2", 64, 320))
    ST = (A("SB0"), A("IN1", 256, 512), A("IN2", 320, 576))

    def xs(t, a, b):
        return A(XT[t][0], XT[t][4] + a, XT[t][4] + b)

    if any(v[0] == "f" for v in HMODE.values()):
        lin("s", col(G15), GCOL, 1.0, 15.0)
        ts(A("Z"), A("IO", 0, 144), col(G15), None, AL.is_equal)
    for j, c in enumerate((LOW, HIGH)):
        ts(A("SEL", 240 * j, 240 * j + 240), A("IO", 0, 240), c, 112.0, AL.subtract, AL.is_equal)
    iota(A("IOM"), [[0, 16], [1, 4], [0, 8]], 0, 0)
    ts(A("MASK"), A("IOM"), U4, None, AL.is_equal)
    lin("e", A("BOX"), A("BO"), 8.0)
    lin("e", A("BO4"), A("BO"), 4096.0)
    lin("e", A("I37"), ID, 37.0)
    lin("e", col(KBI), LANE, 3681.0, 2048.0 * 129 - 1023.5)
    lin("e", col(KAD), LANE, 3681.0, 2048.0 * 129 + 37 * 1800.0)
    act(col(L0C), LANE, AF.Relu, scale=-1.0, bias=1.0)
    lin("e", A("S0M"), A("BO"), col(L0C))
    tt(A("DM"), ID, A("S0M"), AL.subtract)
    lin("e", A("HI"), IF, 0.5)
    lin("e", col(KBZ), LANE, 3681.0, 2048.0 * 129 - 1023.5 + 37 * 1800.0)
    lin("e", A("NB"), A("BO"), -1.0)
    asel(A("WN"), A("NB"), [[-1, 128]], AL.is_gt, 0.0, 0, 1)
    asel(A("WM"), A("WN"), [[-1, 128]], AL.not_equal, 1.0, 0, 1)
    lin("e", col(M64), LANE, 1.0 / 64)
    lin("e", A("MOF"), A("BO"), col(M64))
    lin("e", A("BI"), ID, 33.0 / 32)
    lin("e", col(OFP), L4, 4.0, 2048.0)
    for r in range(4):
        asel(A("BR", 128 * r, 128 * r + 128), A("BO"), [[0, 8], [1, 4], [0, 4]], AL.is_equal, 0.0, -r, 0)
    iota(A("JR"), [[1, 4], [0, 16]], 0, 0)
    rc = lambda i, j=None: A("RC", i, i + 1 if j is None else j, p1=32)
    iota(rc(1), [[0, 1]], 16, 0)
    asel(rc(1), rc(1), [[0, 1]], AL.is_gt, 0.0, 24, -1)
    iota(rc(2, 8), [[512, 6]], -1024, 0)
    asel(rc(4, 8), rc(4, 8), [[0, 4]], AL.is_gt, -256.0, 24, -1)
    asel(rc(1, 8), rc(1, 8), [[0, 7]], AL.is_ge, 0.0, -16, 1)
    for q in range(4):
        iota(rc(8 + q), [[0, 1]], -128 * (31 + 2 * q * q), 0)
    asel(rc(8, 12), rc(8, 12), [[0, 4]], AL.is_equal, 0.0, -9, 1)
    asel(rc(8, 12), rc(8, 12), [[0, 4]], AL.not_equal, -1.0, -8, 1)
    G32 = A("GW", 0, 128, p1=32)
    lin("e", A("Q16", p1=32), G32, rc(1))
    for q in range(4):
        lin("e", A("VQ", 128 * q, 128 * q + 128, p1=32), G32, rc(4 + q), rc(8 + q))
    ts(A("DG"), A("IOL", 0, 64), LANE, -16.0, AL.is_equal, AL.mult)
    if OPT["d0"] == "s":
        lin("e", col(LMB), LANE, -256.0, -128.0)
        act(A("D0"), A("IOL"), AF.Sigmoid, bias=col(LMB), scale=256.0, extra=1.3)
    else:
        ts(A("D0"), A("IOL"), LANE, None, AL.is_gt)
    ts(A("MD"), A("IOL"), LANE, -2.0 ** 20, AL.not_equal, AL.mult)
    iota(A("DUI"), [[1, 128]], 6145, 0)
    nk = max([16 * n for n, q in TAIL if q == "v"] + [16])
    iota(A("KM", 0, nk), [[0, nk]], 1, 0)
    iota(A("KM", 0, nk, 16), [[0, nk // 16]], 0, 0)
    iota(A("RM"), [[0, 512]], 1, 0)
    iota(A("RM", 0, 512, 128), [[0, 4]], 0, 0)
    for t in range(STEPS):
        iota(A("PP", 4112 * t + 4096, 4112 * t + 4112), [[0, 16]], 0, 0)
    iota(A("ES", 128, 136), [[0, 8]], 0, 0)
    iota(A("BN0", 128, 136), [[0, 8]], 0, 0)
    if OPT["wadd"][0] == "d":
        dma("g", A("W1"), A("weight"), 512)
        ops[-1]["ord"] = [i for i, o in enumerate(ops) if o["kind"] == "rem"]

    def pp(t, h, c0=0, c1=2064):
        b = 4112 * t + (2048 if h == t % 2 else 0)
        return A("PP", b + c0, b + c1)

    def role(t, h):
        return "L" if h == t % 2 else "N"

    def st(nm, t, a, b, m=1):
        return A(nm, m * (256 * t + a), m * (256 * t + b))

    def prep(t):
        for a, n in ((0, 128), (128, 128)) if t == 0 else ((0, 256),):
            cc = A("CC" if a == 0 else "HD", 0, n)
            x, s = xs(t, a, a + n), A(ST[t][0], ST[t][4] + a, ST[t][4] + a + n)
            mm(group(cc, [(A("KHI"), x), (A("KLO"), x), (A("DL", 0, 128), s), (A("DL", 128, 256), s)]))
            vcopy(A("CI", a, a + n), cc)
            ts(A("CJ", a, a + n), A("CI", a, a + n), 5, 2047, AL.logical_shift_right, AL.bitwise_and)
            vcopy(st("CU", t, a, a + n), A("CJ", a, a + n))
        for h in (t % 2, 1 - t % 2):
            x = xs(t, 128 * h, 128 * h + 128)
            c0 = 256 * t + 128 * h
            if HMODE[t, h][0] == "f":
                for k in range(16):
                    asel(A("XR", 16 * c0 + k, 16 * c0 + 2048, 16), x, [[0, 128]], AL.is_equal, 0.0, 0, 0)
            elif t == 0 and h in OPT["xbv"]:
                for gq in range(8):
                    lin("e", A("XB", 8 * c0 + gq, 8 * c0 + 1024, 8), x, A("BOC", gq, gq + 1))
            else:
                for gq in range(8):
                    p0 = 32 * (gq // 2)
                    o = A("XB", 8 * c0 + gq, 8 * c0 + 1024, 8, p0, p0 + 32)
                    i = A(x[0], x[4], x[5], 1, p0, p0 + 32)
                    if gq % 2 == 0:
                        asel(o, i, [[0, 128]], AL.is_gt, 0.0, 16, -1)
                    else:
                        asel(o, i, [[0, 128]], AL.is_ge, 0.0, -16, 1)
        ts(st("OS", t, 0, 256), ST[t], LANE, None, AL.is_equal)

    def ints(t, h):
        u0 = 128 * h
        zb = "Z" + role(t, h)
        za, aa, dd, d2, w_, wo = (A(zb, 128 * (i % 4), 128 * (i % 4) + 128) for i in range(6))
        mode, qs = HMODE[t, h][0], HMODE[t, h][1:]
        n = 128 // len(qs)
        table = A("H%d" % t, 0, 2048)
        for i, q in enumerate(qs):
            a = u0 + n * i
            if mode == "f":
                vgather(st("HP", t, a, a + n, 16), table, st("CU", t, a, a + n), st("XR", t, a, a + n, 16))
            else:
                gather(q, st("HP", t, a, a + n, 16), table, st("CU", t, a, a + n), 1.0, -8.0)
        if mode == "f":
            c0 = 16 * (256 * t + u0)
            mms(group(za, [(A("Z", 15 - k, 143 - k), A("HP", c0 + k, c0 + 2048, 16)) for k in range(16)]), 8)
        else:
            db = OPT["dd1"] if (t, h) == (0, 1) else "DD"
            items = []
            for j in range(2):
                for b in range(16):
                    s0 = u0 + 64 * j + 4 * b
                    items.append((A(db, 32 * b, 32 * b + 32, 1, 64 * j, 64 * j + 64), st("HP", t, s0, s0 + 4, 16),
                                  st("XB", t, s0, s0 + 4, 8), True, True))
            mms(items, 32 // len(qs))
            tt(A("D16", 512 * h, 512 * h + 512), A(db), A("MASK"), AL.mult)
            items = [(za, A("BOX"), xs(t, u0, u0 + 128), True, False)]
            for j in range(2):
                for gq in range(8):
                    items.append((A(zb, 64 * j, 64 * j + 64), A("SEL", 240 * j + 112 - 16 * gq, 240 * j + 240 - 16 * gq),
                                  A("D16", 512 * h + gq, 512 * h + 512, 8), False, j == 1 and gq == 7))
            mm(items)
        hs = lambda nm: A(nm, u0, u0 + 128)
        oh = st("OH", t, u0, u0 + 128)
        ts(hs("ZH"), za, 1800.0, None, AL.subtract)
        if h == t % 2 and t < STEPS - 1:
            aa = A("UU", 0, 128)
            ts(hs("RR"), hs("ZH"), -1.0, -14084.5, AL.mult, AL.add)
            mm(group(d2, [(A("DM"), hs("ZH")), (A("DM"), hs("RR"))]))
            ts(hs("EQ"), d2, 0.0, 4096.0, AL.is_equal, AL.mult)
            ts(hs("YA"), hs("ZH"), 37.0, col(KBZ), AL.mult, AL.add)
            mm(group(aa, [(A("I37"), hs("ZH")), (A("NI"), hs("YA"))]))
            ts(st("AU", t, u0, u0 + 128), aa, col(KAD), None, AL.add)
        else:
            lin("e", hs("YA"), za, 37.0, col(KBI))
            mm(group(aa, [(A("I37"), hs("ZH")), (A("NI"), hs("YA"))]) + group(dd, [(A("DM"), hs("ZH"))]))
            ts(st("AU", t, u0, u0 + 128), aa, col(KAD), None, AL.add)
            ts(hs("RR"), dd, 12284.5, None, AL.add)
            mm(group(d2, [(A("DM"), hs("ZH")), (A("NI"), hs("RR"))]))
            act(hs("EQ"), d2, AF.Relu, scale=-4096.0, bias=-4096.0 * 12287)
            ts(hs("EQ"), d2, -12288.0, 4096.0, AL.is_equal, AL.mult)
            either("e")
        qs = PMODE[t, h]
        n = 128 // len(qs)
        for i, q in enumerate(qs):
            gather(q, pp(t, h, 16 * n * i, 16 * n * (i + 1)), A("SC"), st("AU", t, u0 + n * i, u0 + n * (i + 1)))
        mm(group(w_, [(A("WM"), hs("EQ"))]))
        act(oh, w_, AF.Relu)
        ts(oh, w_, 0.0, None, AL.max)
        either("e")
        mm(group(wo, [(A("Q16", p1=32), A("R%d" % t, u0, u0 + 128, p1=32)), (A("MOF"), oh)]))
        ts(st("WU", t, u0, u0 + 128), wo, LANE, None, AL.add)

    def hist_update(t, h):
        u0 = 128 * h
        k1, k2, p_, nw = (A("HD", 128 * i, 128 * i + 128) for i in range(4))
        o_ = A("UU", 128, 256)
        cf = A("CF", u0, u0 + 128)
        ts(cf, st("CU", t, u0, u0 + 128), 1.0, None, AL.add)
        mm(group(p_, [(ID, cf), (A("WM"), A("EQ", u0, u0 + 128))]))
        ts(A("PC"), p_, 4096.0, 0.0, AL.subtract, AL.max)
        mm(group(k2, [(ID, A("MD")), (A("BO"), A("PC"))]) + group(k1, [(A("BO"), A("PC"))]))
        mm([(o_, ID, A("MD"), True, False), (o_, A("BO"), A("PC"), False, False)])
        scan(A("KS"), A("D0"), k2, AL.mult, AL.max)
        ts(A("HV"), A("KS", 15, 128, 16), 1.0, None, AL.subtract)
        gather("e", A("OLD"), A("H%d" % t, 0, 2048), A("HV"))
        tt(A("EM", 0, 128), A("KS"), k1, AL.is_equal)
        items = [(o_, A("BO4"), A("EM", 0, 128), False, False)]
        at = 128
        for b in range(7):
            n = 112 - 16 * b
            key = A("KS", 16 * b + 15, 16 * b + 16)
            if b < OPT["ems"][t]:
                act(A("AB", at - 128, at - 128 + n), A("HD", 128 - n, 128), AF.Abs, scale=-1.0, bias=key)
                if b == OPT["ems"][t] - 1:
                    act(A("EM", 128, at + n), A("AB", 0, at - 128 + n), AF.Relu, scale=-1.0, bias=1.0)
            else:
                ts(A("EM", at, at + n), A("HD", 128 - n, 128), key, None, AL.is_equal)
            items.append((A("UU", 256 - n, 256), A("BO4"), A("EM", at, at + n), False, b == 6))
            at += n
        mm(items[:5])
        mm(items[5:])
        mm(group(nw, [(A("S0S", p1=8), A("R%d" % t, u0, u0 + 128, p1=8)), (A("SH"), A("OLD"))]))
        lin("e", A("NEW"), nw)
        tt(A("OM"), A("DUI"), o_, AL.min)
        scan(A("OT"), A("D0"), A("OM"), AL.mult, AL.max)
        ts(A("HU"), A("OT", 15, 128, 16), 4097.0, None, AL.subtract)
        vscatter(A("H%d" % (t + 1)), A("HU"), A("NEW"))
        if t == 0:
            dma("y", A("H2"), A("H1"), 544)

    def firsts(t, h):
        u0 = 128 * h
        items = []
        for q in range(4):
            items += group(A("UU", 128 * q, 128 * q + 128),
                           [(A("VQ", 128 * q, 128 * q + 128, p1=32), A("R%d" % t, u0, u0 + 128, p1=32)),
                            (A("BI") if h else ID, st("OH", t, u0, u0 + 128))])
        mm(items)
        scan(A("FS"), A("RM"), A("UU"), AL.mult, AL.max)
        for q in range(4):
            lin("e", A("SP", 64 * q, 64 * q + 64), A("DG"), A("FS", 128 * q + 127, 128 * q + 128))
        mm(group(A("UU", 0, 64), [(ID, A("JR"))] + [(A("BR", 128 * q, 128 * q + 128), A("SP", 64 * q, 64 * q + 64)) for q in range(4)]))
        ts(A("UE", 16 * t, 16 * t + 16), A("UU", 0, 16), 1.0 / 16, 128.0, AL.mult, AL.add)
        ts(A("UP", 64 * t, 64 * t + 64), A("UU", 0, 64), col(OFP), None, AL.add)

    first_sig = [0.0 if OPT["d0"] == "s" else 1.3]

    def carry(t, lg, a, n, learner):
        o = a % 128
        oh = st("OS", t, a, a + n)
        c = a + (8 if t == 0 and a >= 128 else 0)
        bn = A("BN%d" % t, c, c + n)
        tail = t == STEPS - 1 and not learner
        bh = A("ZN", 128 + o, 128 + o + n) if tail else A(lg, 384, 384 + n)
        if t == 0 or learner:
            y = A(lg, 256, 256 + n)
            act(y, A(lg, 0, n), AF.Sigmoid, extra=first_sig[0])
            if t == 0:
                tt(bn, oh, y, AL.subtract)
            else:
                tt(A("ES", o, o + n), oh, y, AL.subtract)
                if OPT["bhs"]:
                    lin("s", bh, A("BI%d" % t, a, a + n), 0.5)
                else:
                    mm(group(bh, [(A("HI"), A("BI%d" % t, a, a + n))]))
                tt(bn, A("ES", o, o + n), bh, AL.add)
        else:
            y = A("Y", a, a + n)
            if o == 0:
                mm(group(A(bh[0], bh[4], bh[4] + 128), [(ID, st("OS", t, a, a + 128)), (A("HI"), A("BI%d" % t, a, a + 128))]))
            act(y, A(lg, 0, n), AF.Sigmoid)
            tt(bn, bh, y, AL.subtract)
        first_sig[0] = 0.0
        to = (rank + MOVE) % NR if t < STEPS - 1 else (rank - MOVE * t) % NR
        remote(A("BI%d" % (t + 1), a, a + n), bn, to, n / 2)
        if t == STEPS - 1:
            dma("y", A("yb", a, a + n), A("BI3", a, a + n), n / 2)

    def mix(t, h, learner):
        u0 = 128 * h
        tail = t == STEPS - 1 and not learner
        a = u0
        for i, (n, q) in enumerate(TAIL if tail else [(64, "t"), (64, "t")]):
            lg = ("LGN", "DD", "UU", "ZL")[i] if tail else "LG" + role(t, h)
            lo = 0 if tail else a - u0
            c0 = 16 * (a - u0)
            m = min(n, OPT["pw"])
            for b in range(0, n, m):
                vgather(A("PW", 16 * (a + b), 16 * (a + b + m)), A("W%d" % t), st("WU", t, a + b, a + b + m),
                        pp(t, h, c0 + 16 * b, c0 + 16 * (b + m)))
            roll = [(PCY, A("BI%d" % t, a, a + n))] if tail else []
            whole = t > 0 and not tail
            if whole and i == 0:
                mm([(A(lg, 0, 128), ID, A("ZT", 0, 128), True, False)])
            if q == "v":
                scan(A("LS", 0, 16 * n), A("KM", 0, 16 * n), A("PW", 16 * a, 16 * (a + n)), AL.mult, AL.add)
                mms(group(A(lg, lo, lo + n), roll + [(IF, A("LS", 15, 16 * n, 16))], not whole, not whole), 1)
            else:
                items = group(A(lg, lo, lo + n), roll + [(IF, A("PW", 16 * a + k, 16 * (a + n), 16)) for k in range(16)],
                              not whole, not whole)
                mms(items[:len(roll)], 1)
                mms(items[len(roll):], OPT["gl"])
            if tail:
                carry(t, lg, a, n, False)
            a += n
        if not tail:
            if t > 0:
                mm([(A(lg, 0, 128), PCY, A("BI%d" % t, u0, u0 + 128), False, True)])
            carry(t, lg, u0, 128, learner)

    def learn(t, h):
        gather("e", A("E4"), A("BN0" if t == 0 else "ES", 0, 136), A("UE", 16 * t, 16 * t + 16), 1.0 / 32)
        for j in range(4):
            vgather(A("DW", j, 1024, 4), pp(t, h), A("UP", 64 * t + 16 * j, 64 * t + 16 * j + 16), A("E4"))
        how = OPT["wadd"][t]
        nxt = "W%d" % (t + 1) if t < STEPS - 1 else "yw"
        if how == "d":
            dma("g", A(nxt), A("DW"), 512, True)
        else:
            for j, bk in enumerate(OPT["wbk"][t]):
                c0, c1 = 512 * j, 512 * j + 512
                if bk:
                    lin("s", A(bk), A("W%d" % t, c0, c1))
                tt(A("W%d" % (t + 1), c0, c1), A("DW", c0, c1), A(bk) if bk else A("W%d" % t, c0, c1), AL.add)
                if t == STEPS - 1:
                    dma("s", A("yw", c0, c1), A("W3", c0, c1), 256)
        if t < STEPS - 1 and OPT["wadd"][t + 1] == "d":
            dma("y", A("W2" if t == 0 else "yw"), A(nxt), 512)

    for w in SEQ[0].split():
        t = int(w[1])
        hl = t % 2
        {"p": lambda: prep(t), "l": lambda: ints(t, hl), "n": lambda: ints(t, 1 - hl), "h": lambda: hist_update(t, hl),
         "f": lambda: firsts(t, hl), "L": lambda: mix(t, hl, True), "N": lambda: mix(t, 1 - hl, False), "w": lambda: learn(t, hl)}[w[0]]()
    return ops


HOP = 0.11
ROUNDS = [1500, 180000]
WIN = [4.0, 0.15, 0.5, 0.3, 0.2, 0.3]
SEED = [12345]
PLAN = {}


def order(ops):
    acc, bank = {}, {}
    for i, o in enumerate(ops):
        deps, soft = set(), set()
        me = "e%d" % i if "alt" in o else o["eng"]
        for lst, w in ((o["rd"], False), (o["wr"], True)):
            for a in lst:
                if a[0] in BANKS:
                    if a[0] in bank and bank[a[0]][1] != i:
                        e_, j = bank[a[0]]
                        both_read = all(x[0] != a[0] for x in ops[j]["wr"] + o["wr"])
                        (soft if e_ == me and (e_ == "t" or both_read) else deps).add(j)
                    continue
                pm, cm = _bits(a[1], a[2], a[3]), _bits(a[4], a[5], a[6])
                for j, w2, pm2, cm2 in acc.setdefault(a[0], []):
                    if j != i and (w or w2) and pm & pm2 and cm & cm2:
                        deps.add(j)
        for lst, w in ((o["rd"], False), (o["wr"], True)):
            for a in lst:
                if a[0] in BANKS:
                    bank[a[0]] = (me, i)
                else:
                    acc[a[0]].append((i, w, _bits(a[1], a[2], a[3]), _bits(a[4], a[5], a[6])))
        o["deps"], o["soft"] = deps, soft - deps
    n = len(ops)
    above = []
    for i, o in enumerate(ops):
        m = 0
        for j in o["deps"]:
            m |= above[j]
        o["deps"] = set(j for j in o["deps"] if not m >> j & 1)
        for j in o["deps"]:
            m |= 1 << j
        above.append(0 if o["kind"] == "rem" else m)
    if "t0" not in PLAN:
        PLAN.update(search(ops))
    for i, o in enumerate(ops):
        o["eng"], o["t0"], o["t1"], o["busy"] = PLAN["eng"][i], PLAN["t0"][i], PLAN["t1"][i], PLAN["busy"][i]
        if "alt" in o:
            o["fn"] = o["alt"][o["eng"]][0]
    return PLAN["lst"]


def search(ops):
    n = len(ops)
    cases = []
    for f, ga, sa, dl, wt in CASES:
        cost = lambda c: f * (c[0] + (c[1] * ga + c[2] * sa) * CYC)
        busy = [{e: cost(v[1]) for e, v in o["alt"].items()} if "alt" in o else {o["eng"]: cost(o["cost"])} for o in ops]
        lat = [o["lat"] * dl for o in ops]
        pre = [[(j, lat[j] + (HOP if j in o["deps"] else 0.0)) for j in o["deps"] | o["soft"]] + [(j, 0.0) for j in o.get("ord", [])]
               for o in ops]
        cases.append((busy, lat, pre, 1.0 / wt))
    busy, lat, pre, _ = cases[0]
    post = [[] for _ in range(n)]
    for i in range(n):
        for j, d in pre[i]:
            post[j].append((i, d))
    flex = [i for i in range(n) if "alt" in ops[i]]

    def place(lst, before, rel, eng):
        end = [0.0] * n
        st = {e: [] for e in "vstgy"}
        en = {e: [] for e in "vstgy"}
        for i in lst:
            t0 = rel[i]
            for j, d in before[i]:
                if end[j] + d > t0:
                    t0 = end[j] + d
            pick = None
            for q in eng[i] or "sv":
                s_, e_, b, t = st[q], en[q], busy[i][q], t0
                k = len(s_)
                while k > 0 and e_[k - 1] > t:
                    k -= 1
                while k < len(s_) and s_[k] < t + b:
                    if e_[k] > t:
                        t = e_[k]
                    k += 1
                if pick is None or t + b < pick[0]:
                    pick = (t + b, q, k, t)
            end[i], q, k, t = pick
            eng[i] = q
            st[q].insert(k, t)
            en[q].insert(k, end[i])
        return end

    def replay(lst, eng, case):
        b_, l_, p_, _w = case
        end, free, top = [0.0] * n, {e: 0.0 for e in "vstgy"}, 0.0
        for i in lst:
            q = eng[i]
            t = free[q]
            for j, d in p_[i]:
                if end[j] + d > t:
                    t = end[j] + d
            end[i] = free[q] = t = t + b_[i][q]
            if t + l_[i] > top:
                top = t + l_[i]
        return top

    zero, wsum = [0.0] * n, sum(c[3] for c in cases)

    def polish(lst, eng):
        end = place(lst, pre, zero, eng)
        back = place(sorted(range(n), key=lambda i: (-end[i], -i)), post, lat, eng)
        end = place(sorted(range(n), key=lambda i: (-back[i], i)), pre, zero, eng)
        t0 = [end[i] - busy[i][eng[i]] for i in range(n)]
        lst = sorted(range(n), key=lambda i: (t0[i], i))
        times = [max(end[i] + lat[i] for i in range(n))] + [replay(lst, eng, c) for c in cases[1:]]
        load = sum(busy[i]["v"] for i in flex if eng[i] == "v")
        return (sum(x * c[3] for x, c in zip(times, cases)) / wsum + WIN[3] * load, t0, times, eng)

    seed = [SEED[0]]

    def rnd():
        seed[0] = (seed[0] * 1103515245 + 12345) % 2147483648
        return (seed[0] >> 8) % 4096 / 4096.0

    best = cur = polish(list(range(n)), [o["eng"] for o in ops])
    for it in range(ROUNDS[0]):
        key, eng = list(cur[1]), list(cur[3])
        mid, amp, move = rnd() * cur[2][0], (0.5, 1.0, 2.0, 4.0)[it % 4], rnd()
        if move < WIN[2]:
            for _ in range(1 + it % 2):
                i = flex[int(rnd() * len(flex))]
                eng[i] = "s" if eng[i] == "v" else "v"
        if move > 0.5 * WIN[2]:
            for i in range(n):
                if abs(key[i] - mid) < WIN[0]:
                    key[i] += rnd() * amp
                for j, d in pre[i]:
                    if key[j] >= key[i]:
                        key[i] = key[j] + 1e-6
        cand = polish(sorted(range(n), key=lambda i: (key[i], i)), eng)
        if cand[0] <= cur[0] + WIN[1] * (1.0 - it / ROUNDS[0]):
            cur = cand
        if cand[0] <= best[0]:
            best = cand
    anc = []
    for i in range(n):
        m = 0
        for j, d in pre[i]:
            m |= anc[j] | 1 << j
        anc.append(m)

    def path(lst, eng, case):
        b_, l_, p_, _w = case
        end, why, free, prev, top, last = [0.0] * n, [None] * n, {e: 0.0 for e in "vstgy"}, {}, 0.0, 0
        for i in lst:
            q = eng[i]
            t, w = free[q], (prev.get(q), True)
            for j, d in p_[i]:
                if end[j] + d > t:
                    t, w = end[j] + d, (j, False)
            end[i] = free[q] = t = t + b_[i][q]
            prev[q], why[i] = i, w
            if t + l_[i] > top:
                top, last = t + l_[i], i
        out = []
        while last is not None:
            out.append((last, why[last][0], why[last][1]))
            last = why[last][0]
        return out, end

    sinks = [i for i in range(n) if not post[i]]

    def value(lst, eng, at=0, now=None):
        times, ends = [], []
        seen = {}
        for i in lst[at - 1::-1] if at else []:
            if eng[i] not in seen:
                seen[eng[i]] = i
                if len(seen) == 5:
                    break
        rest = lst[at:]
        for k, (b_, l_, p_, w_) in enumerate(cases):
            end = list(now[2][k]) if now else [0.0] * n
            free = {e: end[seen[e]] if e in seen else 0.0 for e in "vstgy"}
            for i in rest:
                q = eng[i]
                t = free[q]
                for j, d in p_[i]:
                    if end[j] + d > t:
                        t = end[j] + d
                end[i] = free[q] = t + b_[i][q]
            times.append(max(end[i] + l_[i] for i in sinks))
            if now and times[k] > now[1][k] + 1.0:
                return 1e9, times, ends
            ends.append(end)
        rel = [x / c[4] * CASES[0][4] for x, c in zip(times, CASES)]
        return (1 - WIN[5]) * sum(rel) / len(rel) + WIN[5] * max(rel), times, ends

    lst, eng = sorted(range(n), key=lambda i: (best[1][i], i)), list(best[3])
    now = value(lst, eng)
    top, crit = (now, lst, eng), None
    for it in range(ROUNDS[1]):
        if crit is None or it % 64 == 0:
            case = cases[int(rnd() * len(cases))]
            crit, end = path(lst, eng, case)
            lst = sorted(lst, key=lambda i: end[i] - case[0][i][eng[i]])
        v, u, queued = crit[int(rnd() * len(crit))]
        e2, r = eng, rnd()
        if r < 0.15:
            v = v if rnd() < 0.5 or u is None else u
            if "alt" not in ops[v]:
                continue
            e2 = list(eng)
            e2[v] = "s" if eng[v] == "v" else "v"
            l2, pu = lst, lst.index(v)
        elif not queued or u is None:
            continue
        elif r < 0.6:
            pv = lst.index(v)
            pu, hops = lst.index(u), int(rnd() * rnd() * 6)
            while hops and pu > 0:
                pu -= 1
                hops -= eng[lst[pu]] == eng[v]
            if anc[v] >> lst[pu] & 1 and eng[lst[pu]] == eng[v]:
                continue
            mid = lst[pu:pv]
            l2 = lst[:pu] + [i for i in mid if anc[v] >> i & 1] + [v] + [i for i in mid if not anc[v] >> i & 1] + lst[pv + 1:]
        else:
            pu = lst.index(u)
            pv, hops = lst.index(v), int(rnd() * rnd() * 6)
            while hops and pv < n - 1:
                pv += 1
                hops -= eng[lst[pv]] == eng[u]
            mid = lst[pu + 1:pv + 1]
            l2 = lst[:pu] + [i for i in mid if not anc[i] >> u & 1] + [u] + [i for i in mid if anc[i] >> u & 1] + lst[pv + 1:]
        cand = value(l2, e2, pu, now)
        if cand[0] <= now[0] + WIN[4] * (1.0 - it / ROUNDS[1]) * rnd():
            now, lst, eng, crit = cand, l2, e2, None
            if now[0] < top[0][0]:
                top = (now, lst, eng)
    now, lst, eng = top
    end = path(lst, eng, cases[0])[1]
    b = [busy[i][eng[i]] for i in range(n)]
    return {"t0": [end[i] - b[i] for i in range(n)], "t1": [end[i] + lat[i] for i in range(n)], "eng": eng, "busy": b, "times": now[1],
            "lst": lst}


def rank_program(g, core, T, topo):
    if T.rank_of(core) is None:
        return
    ops = build(T, topo, core)
    seq = order(ops)
    queue = {"v": g.vector, "s": g.scalar, "t": g.tensor, "g": g, "y": g.sync}
    count = {e: 0 for e in "vstg"}
    known = {e: {} for e in "vstgy"}
    final, ndma, pool = {}, 0, []
    for i in seq:
        o = ops[i]
        e = o["eng"]
        kn = known[e]
        for j in sorted(o["deps"], key=lambda j: -ops[j]["t1"]):
            s, v = ops[j]["sig"]
            if kn.get(s, 0) < v:
                queue[e].wait_ge(T.sem[s], v)
                kn[s] = v
                if ops[j]["kind"] != "rem":
                    for s2, v2 in ops[j]["known"].items():
                        if kn.get(s2, 0) < v2:
                            kn[s2] = v2
        if e == "g" and o["kind"] == "c":
            p0, p1 = o["wr"][0][1], o["wr"][0][2]
            need = max([c for c, q0, q1 in pool if q0 != p0 and q0 < p1 and p0 < q1] + [0])
            if kn.get("g", 0) < need:
                g.wait_ge(T.sem["g"], need)
                kn["g"] = need
            pool.append((count["g"] + 1, p0, p1))
        o["known"] = dict(kn)
        ins = o["fn"](queue[e])
        if o["kind"] == "c":
            count[e] += 1
            ins.then_inc(T.sem[e], 1)
            o["sig"] = (e, count[e])
        elif o["kind"] == "dma":
            o["sig"] = ("d%d" % ndma, 16)
            ndma += 1
            ins.then_inc(T.sem[o["sig"][0]], 16)
        else:
            o["sig"] = (o["sem"], 8)
            final["sent"] = final.get("sent", 0) + 8
        final[o["sig"][0]] = o["sig"][1]
    for s, v in final.items():
        if all(known[e].get(s, 0) < v for e in known):
            g.sync.wait_ge(T.sem[s], v)
